import numpy as np, ml_dtypes
CORES = [6,15,38,47]
N = 4
import mx_ref
BF = ml_dtypes.bfloat16
def pick(q, e):
    c = np.concatenate([q[0].reshape(128, -1, 4), np.zeros((128, 1, 4), np.uint8)], axis=1); s = np.concatenate([q[1], np.ones((16, 1), np.uint8)], axis=1)
    return (np.ascontiguousarray(c[:, e].reshape(128, -1)), np.ascontiguousarray(s[:, e]))
def join(*qs):
    return (np.concatenate([q[0] for q in qs], axis=1), np.concatenate([q[1] for q in qs], axis=1))
def put(q, e, v):
    c, s = q[0].reshape(128, -1, 4).copy(), q[1].copy(); c[:, e] = v[0].reshape(128, -1, 4); s[:, e] = v[1]
    return (c.reshape(128, -1), s)
def pk(c, s):
    return (np.ascontiguousarray(c), mx_ref.live(s))
def emit(q):
    return q[0], q[1]
def tile(rs):
    return np.stack(rs, axis=2).reshape(128, -1).astype(BF)
def cut(t, i, w=512):
    return t[:, w * i:w * i + w]
def f(rng, *shape):
    return mx_ref.flush((rng.standard_normal(shape, dtype=np.float32) * np.exp2(rng.integers(-2, 3, shape[:-1] + (1,)))).astype(BF))
def wide(rng, *shape, cols=0):
    v = rng.standard_normal(shape, dtype=np.float32) * np.exp2(rng.integers(-12, 13, shape)).astype(np.float32)
    if cols: v *= np.repeat(np.exp2(rng.integers(-cols, cols + 1, shape[:-2] + (1, shape[-1] // 4))) * (rng.random(shape[:-2] + (1, shape[-1] // 4)) > 0.0625), 4, axis=-1).astype(np.float32)
    return mx_ref.flush(v.astype(BF))
T, CAPP, CAPR = 224, 128, 48
def same(t):
    return np.stack([np.concatenate([t, np.zeros((128, 512 - t.shape[1]), BF)], axis=1)] * N)
def bf(t):
    return np.asarray(t, np.float32).astype(BF)
def sized(rng, *shape):
    return 1 + rng.random(shape)
def signs(rng, *shape):
    return 1 - 2 * rng.integers(0, 2, shape)
def setup_inputs(rng):
    return {"x": f(rng, N, 128, 4 * T), "rt": same(f(rng, 128, 4 * N)), "w": f(rng, N, 128, 2048), "u": same(f(rng, 128, 4)), "v": f(rng, N, 128, 512)}
def planted(rng, a, b, own=1.0, off=1.0, way=1):
    d = setup_inputs(rng)
    at = np.arange(128) // (128 // N)
    big, mid = at[None, :, None] == a[:, None, :], at[None, :, None] == b[:, None, :]
    k = np.where(big, 16.0, np.where(mid, 4.0, 1.0))[..., None]
    g = np.where((big | mid)[..., None], 1, signs(rng, N, 128, T, 4))
    d["x"] = bf(sized(rng, N, 128, T, 4) * k * g).reshape(N, 128, 4 * T)
    d["rt"] = same(bf(sized(rng, 128, N, 4) * (at[:, None] == np.arange(N))[..., None]).reshape(128, 4 * N))
    d["w"] = bf(sized(rng, N, 128, 2048) * signs(rng, N, 128, 2048) * np.where(at == np.arange(N)[:, None], own, off)[..., None])
    d["u"] = same(bf(way * sized(rng, 128, 4)))
    return d
def setup_inputs_crowd(rng):
    a, b = np.zeros((N, T), int), np.zeros((N, T), int)
    for s in range(N):
        h, k = (s + (0, 1, 1)[s % 3]) % N, (s + (1, 0, 2)[s % 3]) % N
        rest = rng.permutation(np.array([e for e in range(N) if e not in (h, k)]))
        m, n = rest[np.arange(T) % rest.size], rest[np.arange(1, T + 1) % rest.size]
        p = rng.permutation(T)
        p[:CAPP + 16] = np.sort(p[:CAPP + 16])
        m[:CAPP + 16] = h
        m[CAPP + 16:CAPP + 16 + CAPR] = k
        n[np.concatenate([np.arange(CAPP + 16 + CAPR, T), np.arange(CAPP)])[:CAPP - CAPR]] = k
        a[s, p], b[s, p] = m, n
    return planted(rng, a, b, own=2.0 ** -4, way=-2.0 ** 24)
def setup_inputs_second(rng):
    a, b = np.zeros((N, T), int), np.zeros((N, T), int)
    one, i = int(rng.integers(0, N)), np.arange(T)
    half, last = CAPP // 2, CAPP + CAPP // 2 + 16
    for s in range(N):
        g = rng.permutation(N)
        h, k, rest = g[0], g[1], g[2:]
        m, n = rest[i % rest.size], rest[(i + 1) % rest.size]
        if s == one:
            m[:] = h
            n = g[1 + i % (N - 1)]
        else:
            m[:last] = h
            n[half:last] = k
        turn = (i + rng.integers(0, 2)) % 2 == 1
        p = rng.permutation(T)
        p[:last] = np.sort(p[:last])
        a[s, p], b[s, p] = np.where(turn, m, n), np.where(turn, n, m)
    return planted(rng, a, b, own=2.0 ** 4, way=-1)
def setup_inputs_ties(rng):
    kind = np.stack([rng.permutation(T) % N for s in range(N)])
    e = rng.integers(2, N, (N, T))
    a = np.where(kind == 0, 0, e)
    b = np.where(kind == 0, e, np.where(kind == 1, 0, e ^ 1))
    d = planted(rng, a, b)
    d["rt"][:, :, 4:8] = d["rt"][:, :, :4]
    d["w"][1::2] = d["w"][::2]
    d["w"][:2, :, :4] = 0
    d["w"][1, 128 // N, 0] = BF(4)
    return d
def setup_inputs_zero(rng):
    a = rng.integers(0, N, (N, T))
    b = (a + rng.integers(1, N, (N, T))) % N
    d = planted(rng, a, b, way=-1)
    at, late = np.arange(128) // (128 // N), np.arange(128) % (128 // N) >= 128 // N // 2
    kind = np.stack([rng.permutation(T) % 4 for s in range(N)])
    low = (at[None, :, None] == a[:, None, :]) & (kind % 2 == 1)[:, None, :] | (at[None, :, None] == b[:, None, :]) & (kind >= 2)[:, None, :]
    t = d["x"].astype(np.float32).reshape(N, 128, T, 4)
    d["x"] = bf(np.where(late[None, :, None, None], np.abs(t) * np.where(low, -1, 1)[..., None], t)).reshape(N, 128, 4 * T)
    d["rt"] = bf(d["rt"].astype(np.float32) * ~late[None, :, None])
    d["w"] = bf(np.abs(d["w"].astype(np.float32)) * ((at == np.arange(N)[:, None]) & late)[..., None])
    return d
def setup_inputs_spread(rng):
    return {**setup_inputs(rng), "x": wide(rng, N, 128, 4 * T, cols=6)}
def check_inputs(d):
    b = []
    for k in ("x", "rt", "w", "u", "v"):
        t = np.abs(d[k].astype(np.float32))
        if not (np.isfinite(t).all() and ((t == 0) | (t >= 2.0 ** -30) & (t <= 2.0 ** 30)).all()): b.append("a value of " + k)
    for k, n in (("rt", N), ("u", 1)):
        t = d[k].astype(np.float32)
        if (t[:, :, 4 * n:] != 0).any(): b.append(k + " has numbers behind its first columns")
        if (t != t[:1]).any(): b.append(k + " isn't the same on all ranks")
    return b
def reference(x, rt, w, u, v):
    q, a, b = [], [], []
    for s in range(N):
        q.append(mx_ref.quantize(np.ascontiguousarray(x[s])))
        z = mx_ref.matmul(mx_ref.quantize(np.ascontiguousarray(rt[s])), q[s])[:N] + np.float32(0)
        o = np.argsort(-z, axis=0, kind="stable")
        a.append(o[0])
        b.append(o[1])
    took = [[np.flatnonzero((a[s] == e) | (b[s] == e))[:CAPP] for e in range(N)] for s in range(N)]
    good = np.full((N, N, T), -np.inf, np.float32)
    made = []
    for e in range(N):
        t = join(*[pick(q[s], np.concatenate([took[s][e], np.full(CAPP - took[s][e].size, -1)])) for s in range(N)])
        rs = [mx_ref.matmul(mx_ref.quantize(np.ascontiguousarray(cut(w[e], i))), t) for i in range(4)]
        made.append(mx_ref.quantize(tile([np.maximum(k, np.float32(0)) * np.float32(0.0625) for k in rs])))
        z = mx_ref.matmul(mx_ref.quantize(np.ascontiguousarray(u[e])), made[e])[0] + np.float32(0)
        for s in range(N): good[s, e, took[s][e]] = z[s * CAPP:s * CAPP + took[s][e].size]
    every = join(*made)
    oc, osc = np.zeros((N, 128, 4 * T), np.uint8), np.zeros((N, 16, T), np.uint8)
    wn, y = np.zeros((N, 1, T), np.float32), np.zeros((N, 128, T), np.float32)
    for s in range(N):
        ga, gb = good[s, a[s], np.arange(T)], good[s, b[s], np.arange(T)]
        win = np.where(ga >= gb, a[s], b[s])
        none = np.maximum(ga, gb) == -np.inf
        wn[s, 0] = np.where(none, -100, -1 - win)
        at = np.full(T, -1)
        for e in range(N):
            home = np.flatnonzero((win == e) & ~none)[:CAPR]
            wn[s, 0, home] = e
            at[home] = (e * N + s) * CAPP + np.searchsorted(took[s][e], home)
        z = pick(every, at)
        oc[s], osc[s] = emit(z)
        y[s] = mx_ref.matmul(mx_ref.quantize(np.ascontiguousarray(v[s])), z)
    return {"oc": oc, "osc": osc, "wn": wn, "y": y}

@@ -1,0 +1,362 @@
+from concourse.bass import IndirectOffsetOnAxis
+from concourse.mybir import dt, AluOpType as A, ActivationFunctionType as F
+
+CAP, HOME, TOK = 128, 48, 224
+S = "sbuf"
+SCRATCH = {
+    "xt": (S, [128, 1088], "bfloat16"), "rtt": (S, [128, 512], "bfloat16"), "wt": (S, [128, 2048], "bfloat16"),
+    "ut": (S, [128, 512], "bfloat16"), "vt": (S, [128, 512], "bfloat16"),
+    "xq": (S, [128, 272], "float8_e4m3fn_x4"), "xqs": (S, [128, 288], "uint8"),
+    "rq": (S, [128, 128], "float8_e4m3fn_x4"), "rqs": (S, [128, 128], "uint8"),
+    "rr": (S, [128, 288], "float8_e4m3fn_x4"), "rrs": (S, [128, 288], "uint8"),
+    "wq": (S, [128, 512], "float8_e4m3fn_x4"), "wqs": (S, [128, 512], "uint8"),
+    "uq": (S, [128, 128], "float8_e4m3fn_x4"), "uqs": (S, [128, 128], "uint8"),
+    "ur": (S, [128, 128], "float8_e4m3fn_x4"), "urs": (S, [128, 128], "uint8"),
+    "vq": (S, [128, 128], "float8_e4m3fn_x4"), "vqs": (S, [128, 128], "uint8"),
+    "xs": (S, [128, 512], "float8_e4m3fn_x4"), "xss": (S, [128, 512], "uint8"),
+    "xl": (S, [128, 384], "float8_e4m3fn_x4"), "xls": (S, [128, 384], "uint8"),
+    "hb": (S, [128, 2112], "bfloat16"),
+    "hq": (S, [128, 384], "float8_e4m3fn_x4"), "hqs": (S, [128, 384], "uint8"),
+    "hs": (S, [128, 144], "float8_e4m3fn_x4"), "hss": (S, [128, 144], "uint8"),
+    "zq": (S, [128, 288], "float8_e4m3fn_x4"), "zqs": (S, [128, 288], "uint8"),
+    "z": (S, [128, 224], "float8_e4m3fn_x4"), "zs": (S, [128, 224], "uint8"),
+    "ysb": (S, [128, 224], "float32"),
+    "si": (S, [128, 8], "int32"), "sf": (S, [128, 32], "float32"), "zero": (S, [128, 8], "float32"),
+    "sl": (S, [128, 18], "uint16"), "ul": (S, [128, 8], "uint16"),
+    "rst": (S, [128, 256], "bfloat16"), "one": (S, [128, 256], "bfloat16"),
+    "tokf": (S, [128, 512], "float32"), "tok": (S, [128, 512], "bfloat16"),
+    "k1": (S, [128, 64], "float32"), "k3": (S, [128, 64], "float32"), "ka": (S, [128, 64], "float32"),
+    "kb": (S, [128, 64], "float32"), "kz": (S, [128, 64], "float32"), "kr": (S, [128, 64], "float32"),
+    "kv": (S, [128, 64], "float32"), "kv2": (S, [128, 64], "float32"), "tr": (S, [128, 16], "float32"),
+    "a1": (S, [128, 256], "bfloat16"), "a2": (S, [128, 256], "bfloat16"), "cc": (S, [128, 256], "bfloat16"),
+    "mm": (S, [128, 256], "bfloat16"), "nn": (S, [128, 256], "bfloat16"), "pp": (S, [128, 256], "bfloat16"),
+    "tp": (S, [128, 256], "bfloat16"), "mab": (S, [128, 128], "float32"), "vv": (S, [128, 64], "float32"),
+    "pab": (S, [128, 128], "float32"), "t1": (S, [128, 64], "float32"), "dd": (S, [128, 32], "float32"),
+    "off1": (S, [128, 32], "uint16"), "el": (S, [128, 1088], "bfloat16"), "lt": (S, [128, 640], "bfloat16"),
+    "xn": (S, [128, 40], "float32"), "xp": (S, [128, 40], "float32"), "wl": (S, [128, 40], "float32"),
+    "off2": (S, [128, 40], "uint16"),
+    "tk": (S, [128, 64], "float32"), "abe": (S, [128, 128], "float32"), "v2": (S, [128, 64], "float32"),
+    "pab2": (S, [128, 128], "float32"), "t2": (S, [128, 64], "float32"), "d2": (S, [128, 32], "float32"),
+    "off3": (S, [128, 32], "uint16"), "ae": (S, [128, 64], "float32"), "be": (S, [128, 64], "float32"),
+    "de": (S, [128, 64], "float32"), "qs": (S, [128, 4], "float32"), "gt": (S, [128, 520], "float32"),
+    "gab": (S, [128, 512], "float32"), "wa": (S, [128, 256], "bfloat16"), "wat": (S, [128, 256], "bfloat16"),
+    "x4": (S, [128, 64], "float32"), "m2": (S, [128, 256], "bfloat16"), "n2": (S, [128, 256], "bfloat16"),
+    "rc": (S, [128, 256], "bfloat16"), "rtr": (S, [128, 256], "bfloat16"), "s1": (S, [128, 64], "float32"),
+    "s2": (S, [128, 64], "float32"), "s3": (S, [128, 32], "float32"), "s4": (S, [128, 16], "float32"),
+    "s5": (S, [128, 16], "float32"), "off4": (S, [128, 16], "uint16"), "l3": (S, [128, 912], "bfloat16"),
+    "l3t": (S, [128, 256], "bfloat16"), "l3n": (S, [128, 256], "bfloat16"), "l3p": (S, [128, 256], "bfloat16"),
+    "ll": (S, [128, 16], "float32"), "ls": (S, [128, 16], "uint16"), "la": (S, [128, 12], "uint16"),
+    "h1": (S, [128, 64], "float32"), "hm": (S, [128, 64], "float32"), "xz": (S, [128, 64], "float32"),
+    "z1": (S, [128, 64], "float32"), "z2": (S, [128, 64], "float32"), "z3": (S, [128, 32], "float32"),
+    "zi": (S, [128, 16], "float32"), "zn": (S, [128, 16], "float32"), "zp": (S, [128, 16], "float32"),
+    "zl": (S, [128, 14], "float32"), "off5": (S, [128, 14], "uint16"),
+    "w3": (S, [128, 96], "float32"), "wa1": (S, [128, 64], "float32"), "wnw": (S, [128, 256], "float32"), "wnf": (S, [128, 256], "float32"),
+    "dg": ("dram", [384, 1], "float32"),
+    "ps": ("psum", [128, 4096], "float32"),
+}
+SEMAPHORES = ["v", "s", "t", "p", "dx", "dr", "dw", "du", "dv", "dgt", "out", "sent", "qa", "ha"] \
+    + ["xa%d" % i for i in range(3)] + ["ar%d" % i for i in range(3)]
+
+
+def rank_program(g, core, T, topo):
+    me = T.rank_of(core)
+    if me is None:
+        return
+    others = [r for r in range(4) if r != me]
+    place = lambda src, dst: [r for r in range(4) if r != dst].index(src)
+
+    def far(r):
+        a, b = topo.chip(core), topo.chip(T.cores[r])
+        return 2 if topo.mates(a, b) else 1 if topo.same_plane(a, b) else 0
+    order = sorted(others, key=far)
+
+    V, SC, TE = g.vector, g.scalar, g.tensor
+    queue = {"v": V, "s": SC, "t": TE, "p": g, "y": g.sync}
+    count = {"v": 0, "s": 0, "t": 0, "p": 0}
+    seen = {q: {} for q in queue}
+    total = {}
+
+    def wait(q, *toks):
+        for s, n in toks:
+            if seen[q].get(s, 0) < n:
+                queue[q].wait_ge(T.sem[s], n)
+                seen[q][s] = n
+
+    def do(q, call, args, *toks):
+        best = {}
+        for s, n in toks:
+            best[s] = max(n, best.get(s, 0))
+        wait(q, *best.items())
+        call(*args).then_inc(T.sem[q], 1)
+        count[q] += 1
+        return (q, count[q])
+
+    def v(name, args, *toks):
+        return do("v", {"copy": V.tensor_copy, "tt": V.tensor_tensor, "ts": V.tensor_scalar, "set": V.memset, "tr": V.transpose,
+                        "scan": V.tensor_tensor_scan, "q": V.quantize_mx}[name], args, *toks)
+
+    def act(args, *toks):
+        return do("s", SC.activation, args, *toks)
+
+    def mx(args, *toks):
+        return do("t", TE.matmul_mx, args, *toks)
+
+    def iota(buf, pattern, base, mul, f=True):
+        return do("p", lambda *a: g.iota(*a, allow_small_or_imprecise_dtypes=f), (buf, pattern, base, mul))
+
+    def dma(q, out, in_, sem, *toks):
+        wait(q, *toks)
+        queue[q].dma_start(out, in_).then_inc(T.sem[sem], 16)
+        total[sem] = total.get(sem, 0) + 16
+        return (sem, total[sem])
+
+    def send(dst, out, in_, sem, *toks):
+        wait("p", *toks)
+        c = T.cores[dst]
+        rid, pid, _ = topo.addr(c)
+        g.remote_dma(out, in_, T.sem[sem], T.sem["sent"], pid, rid, topo.mask(core, c))
+        total["sent"] = total.get("sent", 0) + len(topo.engines(core, c))
+
+    u8, u32 = dt.uint8, dt.uint32
+    codes = lambda b, a, z: b[:, a:z].bitcast(u8)
+
+    def pick(dc, ds, a, z, wc, ws, c, d, off, tc, ts=()):
+        x = v("copy", (dc[:, a:z].bitcast(u32), wc[:, c:d].bitcast(u32).indirect(off)), *tc)
+        y = act((ds[:, a:z], ws[:, c:d].indirect(off), F.Copy), *(tuple(tc) + tuple(ts)))
+        return x, y
+
+    dr = dma("s", T.rtt[:, 0:16], T.rt[:, 0:16], "dr")
+    dx = dma("y", T.xt[:, 64:960], T.x[:, :], "dx")
+    wait("y", dx)
+    dw = dma("y", T.wt[:, :], T.w[:, :], "dw")
+    du = dma("y", T.ut[:, 0:8], T.u[:, 0:8], "du")
+    dv = dma("y", T.vt[:, :], T.v[:, :], "dv")
+
+    p0 = iota(T.si[:, 0:1], [[0, 1]], 0, 1, False)
+    p1 = iota(T.tokf[:, :], [[0, 2], [1, 256]], 0, 0)
+    p2 = iota(T.k1[:, :], [[0, 16], [256, 4]], 0, 0)
+    p3 = iota(T.kv[:, :], [[1, 16], [0, 4]], 0, 0)
+    p4 = iota(T.k3[:, :], [[-16, 16], [160, 4]], -657, 0)
+    p5 = iota(T.tr[:, :], [[16, 16]], 656, 0)
+    p6 = iota(T.ka[:, :], [[0, 16], [-1, 4]], 99, 0)
+    p7 = iota(T.kb[:, :], [[0, 16], [2, 4]], 1, 0)
+    zr = v("set", (T.rtt[:, 32:512], 0.0))
+    v("set", (T.zero[:, :], 0.0))
+    v("set", (T.sl[:, :], 8))
+    z0 = v("set", (T.xt[:, 0:64], 0.0))
+    zx = v("set", (T.xt[:, 960:1088], 0.0))
+    i1 = v("ts", (T.si[:, 1:2], T.si[:, 0:1], 15, None, A.bitwise_and), p0)
+    v("ts", (T.si[:, 2:3], T.si[:, 0:1], 15, 2, A.bitwise_and, A.logical_shift_right))
+    v("ts", (T.si[:, 3:4], T.si[:, 0:1], 3, None, A.bitwise_and))
+    i4 = v("ts", (T.si[:, 4:5], T.si[:, 0:1], 16, 4, A.bitwise_and, A.logical_shift_right))
+    f = lambda k: T.sf[:, k:k + 1]
+    c0 = v("copy", (T.sf[:, 0:4], T.si[:, 1:5]), i4)
+    v("ts", (f(4), f(2), f(1), None, A.is_lt), c0)
+    v("ts", (f(5), f(2), 3.0, None, A.is_lt))
+    v("ts", (f(6), f(1), -4.0, None, A.add))
+    c1 = v("ts", (f(7), f(2), -7.0, None, A.add))
+    v("ts", (f(13), f(3), -1.0, 1.0, A.mult, A.add))
+    v("ts", (f(15), f(1), 2.0, -16.0, A.is_lt, A.mult))
+    c2 = v("tt", (f(8), f(7), f(4), A.subtract), c1)
+    v("tt", (f(9), f(6), f(5), A.mult))
+    c3 = v("tt", (f(10), f(8), f(5), A.mult), c2)
+    c4 = v("ts", (T.sl[:, 0:9:2], T.zero[:, 0:5], f(10), 8.0, A.add, A.add), c3)
+    c4 = v("ts", (T.sl[:, 9:18:2], T.zero[:, 0:5], f(9), 8.0, A.add, A.add))
+    v("ts", (f(11), f(2), 0.0, 8.0, A.is_equal, A.mult))
+    c5 = v("ts", (f(12), f(2), 3.0, -8.0, A.is_equal, A.mult))
+    c6 = v("tt", (f(14), f(11), f(12), A.add), c5)
+    v("ts", (f(16), f(4), -1e-30, None, A.mult), c5)
+    v("tt", (f(17), f(15), f(13), A.mult))
+    c7 = v("ts", (f(18), f(3), 16.0, 31.0, A.mult, A.add))
+
+    n0 = v("ts", (T.rtt[:, 16:32], T.rtt[:, 0:16], -1.0, None, A.mult), dr)
+    n1 = v("q", (T.rq[:, :], T.rqs[:, :], T.rtt[:, :]), n0, zr)
+    r1, r2 = pick(T.rr, T.rrs, 0, 288, T.rq, T.rqs, 0, 128, T.sl[:, 0:18], (n1, c4))
+    v("set", (T.rst[:, :], 1.0))
+    v("set", (T.one[:, :], 1.0))
+    k0 = v("set", (T.el[:, :], 0.0))
+    kt = v("ts", (T.tok[:, 0:512], T.tokf[:, :], T.sf[:, 20:21], 240.0, A.add, A.min),
+           v("ts", (f(20), f(3), 16.0, None, A.mult), c7), p1)
+    k5 = v("set", (T.rst[:, 0:256:4], 0.0), k0)
+    q1 = v("q", (T.xq[:, 0:272], T.xqs[:, 0:272], T.xt[:, :]), dx, zx)
+    ps = lambda b, n: T.ps[:, 512 * b:512 * b + n]
+    for j, (lo, sh) in enumerate([(0, 0), (16, 16), (144, 0), (160, 16)]):
+        m0 = mx((ps(0, 256), T.rr[:, lo:lo + 128], T.rrs[:, lo:lo + 128], T.xq[:, sh:sh + 256], T.xqs[:, sh:sh + 256], j == 0, j == 3), q1, r1, r2)
+
+    a = v("ts", (T.a1[:, :], ps(0, 256), f(16), f(14), A.is_gt, A.add), m0, c7)
+    a = v("tr", (T.a2[:, :], T.a1[:, :]), a)
+    b = v("scan", (T.cc[:, :], T.rst[:, :], T.a2[:, :], 0.0, A.mult, A.add), a, k5)
+    a = v("ts", (T.mm[:, :], T.cc[:, :], 1.5, None, A.is_lt), b)
+    a = v("tr", (T.nn[:, :], T.mm[:, :]), a)
+    v("ts", (T.mab[:, 0:64], T.cc[:, 3:256:4], 0.0, None, A.is_equal))
+    b = v("ts", (T.mab[:, 64:128], T.cc[:, 3:256:4], 1.0, None, A.is_equal))
+    pt = v("scan", (T.pp[:, :], T.one[:, :], T.nn[:, :], f(17), A.mult, A.add), a)
+    a = tp = v("tr", (T.tp[:, :], T.pp[:, :]), pt)
+    a = v("tt", (T.vv[:, :], T.tp[:, 3:256:4], T.k1[:, :], A.add), a, p2)
+    v("tt", (T.pab[:, 0:64], T.mab[:, 0:64], T.vv[:, :], A.mult), a)
+    a = v("tt", (T.pab[:, 64:128], T.mab[:, 64:128], T.vv[:, :], A.mult))
+    a = v("tt", (T.t1[:, :], T.pab[:, 0:128:2], T.pab[:, 1:128:2], A.add), a)
+    a = v("tt", (T.dd[:, :], T.t1[:, 0:64:2], T.t1[:, 1:64:2], A.add), a)
+    a = v("ts", (T.off1[:, :], T.dd[:, :], f(18), None, A.add), a)
+    a = v("copy", (T.el[:, 0:1088].indirect(T.off1[:, 0:32]), T.tok[:, :]), a, kt, k0)
+    for e in range(4):
+        b = v("tr", (T.lt[:, 160 * e:160 * e + 160], T.el[:, 256 * e + 32:256 * e + 192]), a)
+    v("ts", (T.xn[:, :], T.lt[:, 0:640:16], f(13), None, A.mult), b)
+    a = v("ts", (T.xp[:, :], T.lt[:, 0:640:16], f(3), None, A.mult))
+    v("tt", (T.wl[:, 0:40:2], T.xn[:, 0:40:2], T.xp[:, 1:40:2], A.add), a)
+    a = v("tt", (T.wl[:, 1:39:2], T.xn[:, 3:40:2], T.xp[:, 0:38:2], A.add))
+    a = v("copy", (T.off2[:, 0:39], T.wl[:, 0:39]), a)
+    xtok = {}
+    for e in order + [me]:
+        xtok[e] = pick(T.xs, T.xss, 128 * e, 128 * e + 128, T.xq, T.xqs, 0, 272, T.off2[:, 10 * e:10 * e + 8], (a,))
+    for e in order:
+        i = place(me, e)
+        send(e, codes(T.xl, 128 * i, 128 * i + 128), codes(T.xs, 128 * e, 128 * e + 128), "xa%d" % i, xtok[e][0])
+        send(e, T.xls[:, 128 * i:128 * i + 128], T.xss[:, 128 * e:128 * e + 128], "xa%d" % i, xtok[e][1])
+
+    for i in range(4):
+        wq = v("q", (T.wq[:, 128 * i:128 * i + 128], T.wqs[:, 128 * i:128 * i + 128], T.wt[:, 512 * i:512 * i + 512]), dw)
+    v("set", (T.ul[:, :], 0))
+    zu = v("set", (T.ut[:, 8:512], 0.0))
+    zh = v("set", (T.hb[:, 512:576], 0.0))
+    uq = v("q", (T.uq[:, :], T.uqs[:, :], T.ut[:, :]), du, zu)
+    ur = pick(T.ur, T.urs, 0, 128, T.uq, T.uqs, 0, 128, T.ul[:, 0:8], (uq,))
+
+    sets = [0]
+
+    def chunk(xc, xsc, lo, toks, hlo, hn, hc, hsc, hto, free):
+        b = 4 * (sets[0] % 2)
+        sets[0] += 1
+        h = []
+        for i in range(4):
+            m = mx((ps(b + i, 128), T.wq[:, 128 * i:128 * i + 128], T.wqs[:, 128 * i:128 * i + 128], xc[:, lo:lo + 128], xsc[:, lo:lo + 128], True, True), wq, *(tuple(toks) + tuple(free)))
+            out = T.hb[:, hlo + i:hlo + 512:4]
+            h.append(act((out, ps(b + i, 128), F.Relu, 0.0, 0.0625), m) if i % 2 == 0 else v("ts", (out, ps(b + i, 128), 0.0, 0.0625, A.max, A.mult), m))
+        return b, v("q", (hc[:, hto:hto + hn], hsc[:, hto:hto + hn], T.hb[:, hlo:hlo + 4 * hn]), *h)
+
+    b0, h0 = chunk(T.xs, T.xss, 128 * me, xtok[me], 0, 144, T.zq, T.zqs, 0, ())
+    g0 = v("set", (T.gt[:, :], -9e29))
+    m = mx((ps(b0, 128), T.ur[:, :], T.urs[:, :], T.zq[:, 0:128], T.zqs[:, 0:128], True, True), h0, *ur)
+    own = v("copy", (T.gt[:, 0:128], ps(b0, 128)), m, g0)
+
+    rel = {me: 0}
+    for i, r in enumerate(others):
+        rel[r] = 128 + 128 * i
+    for e in range(4):
+        c = v("set", (T.kr[:, e:64:4], float(rel[e] - 1 - 512)))
+    for e in range(4):
+        v("set", (T.kz[:, e:64:4], float(-1 - 128 if e == me else 144 + 48 * others.index(e) - 1 - 128)))
+    v("ts", (T.tk[:, :], T.tp[:, 3:256:4], 128.5, None, A.is_lt))
+    v("tt", (T.v2[:, :], T.tp[:, 3:256:4], T.kr[:, :], A.add), c)
+    k7 = v("ts", (T.kv[:, :], T.kv[:, :], f(13), None, A.subtract), p3)
+    v("ts", (T.k3[:, :], T.k3[:, :], f(20), f(0), A.add, A.subtract), p4)
+    v("ts", (T.tr[:, :], T.tr[:, :], f(0), None, A.add), p5)
+    v("set", (T.m2[:, :], 0.0))
+    v("set", (T.l3[:, :], 1.0))
+    c = v("ts", (T.kv2[:, :], T.kv[:, :], 0.0, None, A.is_ge), k7)
+    v("tt", (T.abe[:, 0:64], T.mab[:, 0:64], T.tk[:, :], A.mult), c)
+    a = v("tt", (T.abe[:, 64:128], T.mab[:, 64:128], T.tk[:, :], A.mult))
+    c = v("ts", (T.kv[:, :], T.kv[:, :], 13.5, None, A.is_lt), c)
+    v("tt", (T.pab2[:, 0:64], T.abe[:, 0:64], T.v2[:, :], A.mult), a)
+    a = v("tt", (T.pab2[:, 64:128], T.abe[:, 64:128], T.v2[:, :], A.mult))
+    c = v("tt", (T.kv2[:, :], T.kv2[:, :], T.kv[:, :], A.mult), c)
+    a = v("tt", (T.t2[:, :], T.pab2[:, 0:128:2], T.pab2[:, 1:128:2], A.add), a)
+    v("tt", (T.ae[:, :], T.abe[:, 0:64], T.kv2[:, :], A.mult), c)
+    c = v("tt", (T.be[:, :], T.abe[:, 64:128], T.kv2[:, :], A.mult))
+    a = v("tt", (T.d2[:, :], T.t2[:, 0:64:2], T.t2[:, 1:64:2], A.add), a)
+    c = v("tt", (T.de[:, :], T.ae[:, :], T.be[:, :], A.subtract), c)
+    o3 = v("ts", (T.off3[:, :], T.d2[:, :], 512.0, None, A.add), a)
+    v("set", (T.ll[:, :], 1.0))
+    v("set", (T.wnw[:, :], 0.0))
+    vq = v("q", (T.vq[:, :], T.vqs[:, :], T.vt[:, :]), dv)
+
+    bank = {b0: (own,)}
+    hq = {}
+    for s in order:
+        i = others.index(s)
+        n = 2 * len(topo.engines(T.cores[s], core))
+        total["xa%d" % i] = n
+        b = 4 * (sets[0] % 2)
+        b, h = chunk(T.xl, T.xls, 128 * i, (("xa%d" % i, n),), 576 + 512 * i, 128, T.hq, T.hqs, 128 * i, bank.get(b, ()))
+        hq[s] = h
+        m = mx((ps(b, 128), T.hq[:, 128 * i:128 * i + 128], T.hqs[:, 128 * i:128 * i + 128], T.uq[:, :], T.uqs[:, :], True, True), h)
+        c = act((T.qs[:, i:i + 1], ps(b, 1), F.Copy), m)
+        bank[b] = (c, h)
+        k = place(me, s)
+        send(s, T.dg[128 * k:128 * k + 128, :], T.qs[:, i:i + 1], "qa", c)
+
+    qa = ("qa", sum(len(topo.engines(T.cores[s], core)) for s in others))
+    for k in range(8):
+        gd = dma("y" if k % 2 == 0 else "s", T.gt[16 * k:16 * k + 1, 128:512], T.dg[:, :], "dgt", qa, own)
+    a = v("copy", (T.gab[:, :], T.gt[:, 0:520].indirect(T.off3[:, 0:32])), gd, o3, own)
+    a = v("tt", (T.wa[:, :], T.gab[:, 0:256], T.gab[:, 256:512], A.is_ge), a)
+    a = v("tr", (T.wat[:, :], T.wa[:, :]), a)
+    for e in range(4):
+        b = v("tt", (T.x4[:, e:64:4], T.wat[:, 0:256:16], T.de[:, e:64:4], A.mult), a)
+    w4 = T.m2[:, 3:256:4]
+    a = v("tt", (w4, T.x4[:, :], T.be[:, :], A.add), b)
+    a = v("tr", (T.n2[:, :], T.m2[:, :]), a)
+    a = v("scan", (T.rc[:, :], T.one[:, :], T.n2[:, :], 0.0, A.mult, A.add), a)
+    rt = v("tr", (T.rtr[:, :], T.rc[:, :]), a)
+    r4 = T.rtr[:, 3:256:4]
+    a = v("tt", (T.s1[:, :], r4, T.k3[:, :], A.add), rt)
+    a = v("tt", (T.s2[:, :], T.s1[:, :], w4, A.mult), a)
+    a = v("tt", (T.s3[:, :], T.s2[:, 0:64:2], T.s2[:, 1:64:2], A.add), a)
+    a = v("tt", (T.s4[:, :], T.s3[:, 0:32:2], T.s3[:, 1:32:2], A.add), a)
+    a = v("tt", (T.s5[:, :], T.s4[:, :], T.tr[:, :], A.add), a)
+    a = v("copy", (T.off4[:, :], T.s5[:, :]), a)
+    a = v("copy", (T.l3[:, 0:912].indirect(T.off4[:, 0:16]), T.pp[:, :]), a)
+    for e in range(4):
+        b = v("tr", (T.l3t[:, 64 * e:64 * e + 64], T.l3[:, 160 * e:160 * e + 64]), a)
+    c = act((T.l3p[:, :], T.l3t[:, :], F.Copy, 0.0, f(3)), b)
+    b = v("ts", (T.l3n[:, :], T.l3t[:, :], f(13), None, A.mult), b)
+    at = lambda t, x: t[:, x:x + 205:68]
+    v("tt", (T.ll[:, 0:16:4], at(T.l3n, 3), at(T.l3p, 19), A.add), b, c)
+    v("tt", (T.ll[:, 1:16:4], at(T.l3n, 51), at(T.l3p, 3), A.add))
+    a = v("tt", (T.ll[:, 2:16:4], at(T.l3n, 35), at(T.l3p, 51), A.add))
+    a = v("ts", (T.ls[:, :], T.ll[:, :], -1.0, None, A.add), a)
+    for e in order:
+        i = place(me, e)
+        send(e, T.la[:, 4 * i:4 * i + 3], T.ls[:, 4 * e:4 * e + 3], "ar%d" % i, a)
+
+    v("ts", (T.h1[:, :], r4, 48.5, None, A.is_lt))
+    a = v("copy", (T.xz[:, :], r4))
+    c = v("tt", (T.wa1[:, :], w4, T.ka[:, :], A.mult), p6)
+    a = v("copy", (T.xz[:, me:64:4], T.tp[:, 4 * me + 3:256:16]), a)
+    b = v("tt", (T.hm[:, :], w4, T.h1[:, :], A.mult), c)
+    a = v("tt", (T.z1[:, :], T.xz[:, :], T.kz[:, :], A.add), a)
+    c = v("tt", (T.s1[:, :], T.hm[:, :], T.kb[:, :], A.mult), b, p7)
+    a = v("tt", (T.z2[:, :], T.z1[:, :], T.hm[:, :], A.mult), a, b)
+    c = v("tt", (T.s2[:, :], T.s1[:, :], T.wa1[:, :], A.add), c)
+    a = v("tt", (T.z3[:, :], T.z2[:, 0:64:2], T.z2[:, 1:64:2], A.add), a)
+    c = v("tt", (T.w3[:, 0:32], T.s2[:, 0:64:2], T.s2[:, 1:64:2], A.add), c)
+    a = v("tt", (T.zi[:, :], T.z3[:, 0:32:2], T.z3[:, 1:32:2], A.add), a)
+    c = v("tt", (T.w3[:, 32:48], T.w3[:, 0:32:2], T.w3[:, 1:32:2], A.add), c)
+    v("ts", (T.zn[:, :], T.zi[:, :], f(13), None, A.mult), a)
+    a = v("ts", (T.zp[:, :], T.zi[:, :], f(3), None, A.mult))
+    c = v("ts", (T.wnw[:, 0:256:16], T.w3[:, 32:48], -100.0, None, A.add), c)
+    a = v("tt", (T.zl[:, :], T.zn[:, 1:15], T.zp[:, 0:14], A.add), a)
+    c = v("tr", (T.wnf[:, :], T.wnw[:, :]), c)
+    zo = v("ts", (T.off5[:, :], T.zl[:, :], 128.0, None, A.add), a)
+    dma("y", T.wn[:, :], T.wnf[16:17, 0:224], "out", c)
+
+    for s in order:
+        i = others.index(s)
+        n = len(topo.engines(T.cores[s], core))
+        total["ar%d" % i] = n
+        x, y = pick(T.hs, T.hss, 48 * i, 48 * i + 48, T.hq, T.hqs, 128 * i, 128 * i + 128, T.la[:, 4 * i:4 * i + 3], (hq[s], ("ar%d" % i, n)))
+        k = 144 + 48 * place(me, s)
+        send(s, codes(T.zq, k, k + 48), codes(T.hs, 48 * i, 48 * i + 48), "ha", x)
+        send(s, T.zqs[:, k:k + 48], T.hss[:, 48 * i:48 * i + 48], "ha", y)
+
+    ha = ("ha", 2 * qa[1])
+    x, y = pick(T.z, T.zs, 0, 224, T.zq, T.zqs, 0, 288, T.off5[:, 0:14], (ha, zo, h0))
+    m = mx((ps(0, 224), T.vq[:, :], T.vqs[:, :], T.z[:, :], T.zs[:, :], True, True), x, y, vq)
+    yc = v("copy", (T.ysb[:, :], ps(0, 224)), m)
+    dma("y", T.oc[:, :], codes(T.z, 0, 224), "out", x)
+    for k in range(4):
+        dma("s" if k % 2 == 0 else "y", T.osc[4 * k:4 * k + 4, :], T.zs[32 * k:32 * k + 4, :], "out", y)
+    dma("y", T.y[:, :], T.ysb[:, :], "out", yc)
+    total["qa"], total["ha"] = qa[1], ha[1]
+    for s, n in list(total.items()) + list(count.items()):
+        wait("p", (s, n))

@@ -1,59 +1,30 @@
-from concourse.bass import IndirectOffsetOnAxis
 from concourse.mybir import dt, AluOpType as A, ActivationFunctionType as F
 
-CAP, HOME, TOK = 128, 48, 224
-S = "sbuf"
-SCRATCH = {
-    "xt": (S, [128, 1088], "bfloat16"), "rtt": (S, [128, 512], "bfloat16"), "wt": (S, [128, 2048], "bfloat16"),
-    "ut": (S, [128, 512], "bfloat16"), "vt": (S, [128, 512], "bfloat16"),
-    "xq": (S, [128, 272], "float8_e4m3fn_x4"), "xqs": (S, [128, 288], "uint8"),
-    "rq": (S, [128, 128], "float8_e4m3fn_x4"), "rqs": (S, [128, 128], "uint8"),
-    "rr": (S, [128, 288], "float8_e4m3fn_x4"), "rrs": (S, [128, 288], "uint8"),
-    "wq": (S, [128, 512], "float8_e4m3fn_x4"), "wqs": (S, [128, 512], "uint8"),
-    "uq": (S, [128, 128], "float8_e4m3fn_x4"), "uqs": (S, [128, 128], "uint8"),
-    "ur": (S, [128, 128], "float8_e4m3fn_x4"), "urs": (S, [128, 128], "uint8"),
-    "vq": (S, [128, 128], "float8_e4m3fn_x4"), "vqs": (S, [128, 128], "uint8"),
-    "xs": (S, [128, 512], "float8_e4m3fn_x4"), "xss": (S, [128, 512], "uint8"),
-    "xl": (S, [128, 384], "float8_e4m3fn_x4"), "xls": (S, [128, 384], "uint8"),
-    "hb": (S, [128, 2112], "bfloat16"),
-    "hq": (S, [128, 384], "float8_e4m3fn_x4"), "hqs": (S, [128, 384], "uint8"),
-    "hs": (S, [128, 144], "float8_e4m3fn_x4"), "hss": (S, [128, 144], "uint8"),
-    "zq": (S, [128, 288], "float8_e4m3fn_x4"), "zqs": (S, [128, 288], "uint8"),
-    "z": (S, [128, 224], "float8_e4m3fn_x4"), "zs": (S, [128, 224], "uint8"),
-    "ysb": (S, [128, 224], "float32"),
-    "si": (S, [128, 8], "int32"), "sf": (S, [128, 32], "float32"), "zero": (S, [128, 8], "float32"),
-    "sl": (S, [128, 18], "uint16"), "ul": (S, [128, 8], "uint16"),
-    "rst": (S, [128, 256], "bfloat16"), "one": (S, [128, 256], "bfloat16"),
-    "tokf": (S, [128, 512], "float32"), "tok": (S, [128, 512], "bfloat16"),
-    "k1": (S, [128, 64], "float32"), "k3": (S, [128, 64], "float32"), "ka": (S, [128, 64], "float32"),
-    "kb": (S, [128, 64], "float32"), "kz": (S, [128, 64], "float32"), "kr": (S, [128, 64], "float32"),
-    "kv": (S, [128, 64], "float32"), "kv2": (S, [128, 64], "float32"), "tr": (S, [128, 16], "float32"),
-    "a1": (S, [128, 256], "bfloat16"), "a2": (S, [128, 256], "bfloat16"), "cc": (S, [128, 256], "bfloat16"),
-    "mm": (S, [128, 256], "bfloat16"), "nn": (S, [128, 256], "bfloat16"), "pp": (S, [128, 256], "bfloat16"),
-    "tp": (S, [128, 256], "bfloat16"), "mab": (S, [128, 128], "float32"), "vv": (S, [128, 64], "float32"),
-    "pab": (S, [128, 128], "float32"), "t1": (S, [128, 64], "float32"), "dd": (S, [128, 32], "float32"),
-    "off1": (S, [128, 32], "uint16"), "el": (S, [128, 1088], "bfloat16"), "lt": (S, [128, 640], "bfloat16"),
-    "xn": (S, [128, 40], "float32"), "xp": (S, [128, 40], "float32"), "wl": (S, [128, 40], "float32"),
-    "off2": (S, [128, 40], "uint16"),
-    "tk": (S, [128, 64], "float32"), "abe": (S, [128, 128], "float32"), "v2": (S, [128, 64], "float32"),
-    "pab2": (S, [128, 128], "float32"), "t2": (S, [128, 64], "float32"), "d2": (S, [128, 32], "float32"),
-    "off3": (S, [128, 32], "uint16"), "ae": (S, [128, 64], "float32"), "be": (S, [128, 64], "float32"),
-    "de": (S, [128, 64], "float32"), "qs": (S, [128, 4], "float32"), "gt": (S, [128, 520], "float32"),
-    "gab": (S, [128, 512], "float32"), "wa": (S, [128, 256], "bfloat16"), "wat": (S, [128, 256], "bfloat16"),
-    "x4": (S, [128, 64], "float32"), "m2": (S, [128, 256], "bfloat16"), "n2": (S, [128, 256], "bfloat16"),
-    "rc": (S, [128, 256], "bfloat16"), "rtr": (S, [128, 256], "bfloat16"), "s1": (S, [128, 64], "float32"),
-    "s2": (S, [128, 64], "float32"), "s3": (S, [128, 32], "float32"), "s4": (S, [128, 16], "float32"),
-    "s5": (S, [128, 16], "float32"), "off4": (S, [128, 16], "uint16"), "l3": (S, [128, 912], "bfloat16"),
-    "l3t": (S, [128, 256], "bfloat16"), "l3n": (S, [128, 256], "bfloat16"), "l3p": (S, [128, 256], "bfloat16"),
-    "ll": (S, [128, 16], "float32"), "ls": (S, [128, 16], "uint16"), "la": (S, [128, 12], "uint16"),
-    "h1": (S, [128, 64], "float32"), "hm": (S, [128, 64], "float32"), "xz": (S, [128, 64], "float32"),
-    "z1": (S, [128, 64], "float32"), "z2": (S, [128, 64], "float32"), "z3": (S, [128, 32], "float32"),
-    "zi": (S, [128, 16], "float32"), "zn": (S, [128, 16], "float32"), "zp": (S, [128, 16], "float32"),
-    "zl": (S, [128, 14], "float32"), "off5": (S, [128, 14], "uint16"),
-    "w3": (S, [128, 96], "float32"), "wa1": (S, [128, 64], "float32"), "wnw": (S, [128, 256], "float32"), "wnf": (S, [128, 256], "float32"),
-    "dg": ("dram", [384, 1], "float32"),
-    "ps": ("psum", [128, 4096], "float32"),
-}
+
+def _buffers():
+    d = {"dg": ("dram", [384, 1], "float32"), "ps": ("psum", [128, 4096], "float32")}
+    kinds = {
+        "bfloat16": "xt 1088 rtt 512 wt 2048 ut 512 vt 512 hb 2112 rst 256 one 256 tok 512 a1 256 a2 256 cc 256 mm 256 nn 256 "
+                    "pp 256 tp 256 el 1088 lt 640 wa 256 wat 256 m2 256 n2 256 rc 256 rtr 256 l3 912 l3t 256 l3n 256 l3p 256",
+        "float32": "ysb 224 sf 32 zero 8 tokf 512 k1 64 k3 64 ka 64 kb 64 kz 64 kr 64 kv 64 kv2 64 tr 16 mab 128 vv 64 pab 128 "
+                   "t1 128 xn 40 xp 40 wl 40 xn1 10 xp1 10 wl1 10 tk 64 abe 128 v2 64 pab2 128 t2 128 ae 64 be 64 de 64 qs 4 "
+                   "gt 520 gab 256 x4 64 s1 64 s2 64 s3 64 s5 16 ll 16 h1 64 hm 64 xz 64 z1 64 z2 64 z3 64 zn 16 zp 16 zl 14 "
+                   "w1 64 w2 64 w3 64 w4 64 wnw 256 wnf 256",
+        "uint16": "sl 18 ul 8 off1 32 off2 40 off2a 10 off3 32 off4 16 off5 14 ls 16 la 12",
+        "int32": "si 8",
+    }
+    for t, text in kinds.items():
+        w = text.split()
+        for name, n in zip(w[::2], w[1::2]):
+            d[name] = ("sbuf", [128, int(n)], t)
+    w = "xq 272 rq 128 rr 288 wq 512 uq 128 ur 128 vq 128 xs 512 xl 384 hq 384 hs 144 zq 288 z 224".split()
+    for name, n in zip(w[::2], w[1::2]):
+        d[name] = ("sbuf", [128, int(n)], "float8_e4m3fn_x4")
+        d[name + "s"] = ("sbuf", [128, int(n)], "uint8")
+    return d
+
+
+SCRATCH = _buffers()
 SEMAPHORES = ["v", "s", "t", "p", "dx", "dr", "dw", "du", "dv", "dgt", "out", "sent", "qa", "ha"] \
     + ["xa%d" % i for i in range(3)] + ["ar%d" % i for i in range(3)]
 
@@ -77,29 +48,25 @@ def rank_program(g, core, T, topo):
     total = {}
 
     def wait(q, *toks):
+        best = {}
         for s, n in toks:
+            best[s] = max(n, best.get(s, 0))
+        for s, n in best.items():
             if seen[q].get(s, 0) < n:
                 queue[q].wait_ge(T.sem[s], n)
                 seen[q][s] = n
 
     def do(q, call, args, *toks):
-        best = {}
-        for s, n in toks:
-            best[s] = max(n, best.get(s, 0))
-        wait(q, *best.items())
+        wait(q, *toks)
         call(*args).then_inc(T.sem[q], 1)
         count[q] += 1
         return (q, count[q])
 
-    def v(name, args, *toks):
-        return do("v", {"copy": V.tensor_copy, "tt": V.tensor_tensor, "ts": V.tensor_scalar, "set": V.memset, "tr": V.transpose,
-                        "scan": V.tensor_tensor_scan, "q": V.quantize_mx}[name], args, *toks)
-
-    def act(args, *toks):
-        return do("s", SC.activation, args, *toks)
-
-    def mx(args, *toks):
-        return do("t", TE.matmul_mx, args, *toks)
+    calls = {"copy": V.tensor_copy, "tt": V.tensor_tensor, "ts": V.tensor_scalar, "set": V.memset, "tr": V.transpose,
+             "scan": V.tensor_tensor_scan, "q": V.quantize_mx}
+    v = lambda name, args, *toks: do("v", calls[name], args, *toks)
+    act = lambda args, *toks: do("s", SC.activation, args, *toks)
+    mx = lambda args, *toks: do("t", TE.matmul_mx, args, *toks)
 
     def iota(buf, pattern, base, mul, f=True):
         return do("p", lambda *a: g.iota(*a, allow_small_or_imprecise_dtypes=f), (buf, pattern, base, mul))
@@ -120,9 +87,9 @@ def rank_program(g, core, T, topo):
     u8, u32 = dt.uint8, dt.uint32
     codes = lambda b, a, z: b[:, a:z].bitcast(u8)
 
-    def pick(dc, ds, a, z, wc, ws, c, d, off, tc, ts=()):
-        x = v("copy", (dc[:, a:z].bitcast(u32), wc[:, c:d].bitcast(u32).indirect(off)), *tc)
-        y = act((ds[:, a:z], ws[:, c:d].indirect(off), F.Copy), *(tuple(tc) + tuple(ts)))
+    def pick(to, a, z, win, c, d, off, *toks):
+        x = v("copy", (T[to][:, a:z].bitcast(u32), T[win][:, c:d].bitcast(u32).indirect(off)), *toks)
+        y = act((T[to + "s"][:, a:z], T[win + "s"][:, c:d].indirect(off), F.Copy), *toks)
         return x, y
 
     dr = dma("s", T.rtt[:, 0:16], T.rt[:, 0:16], "dr")
@@ -133,142 +100,145 @@ def rank_program(g, core, T, topo):
     dv = dma("y", T.vt[:, :], T.v[:, :], "dv")
 
     p0 = iota(T.si[:, 0:1], [[0, 1]], 0, 1, False)
-    p1 = iota(T.tokf[:, :], [[0, 2], [1, 256]], 0, 0)
+    for k in range(2):
+        iota(T.tokf[:, 256 * k:256 * k + 240], [[1, 240]], 0, 0)
+        p1 = iota(T.tokf[:, 256 * k + 240:256 * k + 256], [[0, 16]], 240, 0)
     p2 = iota(T.k1[:, :], [[0, 16], [256, 4]], 0, 0)
     p3 = iota(T.kv[:, :], [[1, 16], [0, 4]], 0, 0)
     p4 = iota(T.k3[:, :], [[-16, 16], [160, 4]], -657, 0)
     p5 = iota(T.tr[:, :], [[16, 16]], 656, 0)
     p6 = iota(T.ka[:, :], [[0, 16], [-1, 4]], 99, 0)
     p7 = iota(T.kb[:, :], [[0, 16], [2, 4]], 1, 0)
+    f = lambda k: T.sf[:, k:k + 1]
     zr = v("set", (T.rtt[:, 32:512], 0.0))
     v("set", (T.zero[:, :], 0.0))
     v("set", (T.sl[:, :], 8))
-    z0 = v("set", (T.xt[:, 0:64], 0.0))
-    zx = v("set", (T.xt[:, 960:1088], 0.0))
-    i1 = v("ts", (T.si[:, 1:2], T.si[:, 0:1], 15, None, A.bitwise_and), p0)
+    v("ts", (T.si[:, 1:2], T.si[:, 0:1], 15, None, A.bitwise_and), p0)
     v("ts", (T.si[:, 2:3], T.si[:, 0:1], 15, 2, A.bitwise_and, A.logical_shift_right))
     v("ts", (T.si[:, 3:4], T.si[:, 0:1], 3, None, A.bitwise_and))
     i4 = v("ts", (T.si[:, 4:5], T.si[:, 0:1], 16, 4, A.bitwise_and, A.logical_shift_right))
-    f = lambda k: T.sf[:, k:k + 1]
+    v("set", (T.xt[:, 0:64], 0.0))
+    zx = v("set", (T.xt[:, 960:1088], 0.0))
     c0 = v("copy", (T.sf[:, 0:4], T.si[:, 1:5]), i4)
+    v("set", (T.rst[:, :], 1.0))
     v("ts", (f(4), f(2), f(1), None, A.is_lt), c0)
     v("ts", (f(5), f(2), 3.0, None, A.is_lt))
     v("ts", (f(6), f(1), -4.0, None, A.add))
     c1 = v("ts", (f(7), f(2), -7.0, None, A.add))
+    c8 = v("ts", (f(20), f(3), 16.0, None, A.mult))
+    v("tt", (f(8), f(7), f(4), A.subtract), c1)
+    c2 = v("tt", (f(9), f(6), f(5), A.mult))
     v("ts", (f(13), f(3), -1.0, 1.0, A.mult, A.add))
     v("ts", (f(15), f(1), 2.0, -16.0, A.is_lt, A.mult))
-    c2 = v("tt", (f(8), f(7), f(4), A.subtract), c1)
-    v("tt", (f(9), f(6), f(5), A.mult))
     c3 = v("tt", (f(10), f(8), f(5), A.mult), c2)
-    c4 = v("ts", (T.sl[:, 0:9:2], T.zero[:, 0:5], f(10), 8.0, A.add, A.add), c3)
+    v("set", (T.rst[:, 0:256:4], 0.0), c0)
+    v("ts", (T.sl[:, 0:9:2], T.zero[:, 0:5], f(10), 8.0, A.add, A.add), c3)
     c4 = v("ts", (T.sl[:, 9:18:2], T.zero[:, 0:5], f(9), 8.0, A.add, A.add))
-    v("ts", (f(11), f(2), 0.0, 8.0, A.is_equal, A.mult))
-    c5 = v("ts", (f(12), f(2), 3.0, -8.0, A.is_equal, A.mult))
-    c6 = v("tt", (f(14), f(11), f(12), A.add), c5)
-    v("ts", (f(16), f(4), -1e-30, None, A.mult), c5)
-    v("tt", (f(17), f(15), f(13), A.mult))
-    c7 = v("ts", (f(18), f(3), 16.0, 31.0, A.mult, A.add))
+    k0 = v("set", (T.el[:, :], 0.0))
+    kt = act((T.tok[:, :], T.tokf[:, :], F.Identity, f(20)), c8, p1)
 
     n0 = v("ts", (T.rtt[:, 16:32], T.rtt[:, 0:16], -1.0, None, A.mult), dr)
     n1 = v("q", (T.rq[:, :], T.rqs[:, :], T.rtt[:, :]), n0, zr)
-    r1, r2 = pick(T.rr, T.rrs, 0, 288, T.rq, T.rqs, 0, 128, T.sl[:, 0:18], (n1, c4))
-    v("set", (T.rst[:, :], 1.0))
-    v("set", (T.one[:, :], 1.0))
-    k0 = v("set", (T.el[:, :], 0.0))
-    kt = v("ts", (T.tok[:, 0:512], T.tokf[:, :], T.sf[:, 20:21], 240.0, A.add, A.min),
-           v("ts", (f(20), f(3), 16.0, None, A.mult), c7), p1)
-    k5 = v("set", (T.rst[:, 0:256:4], 0.0), k0)
+    r1, r2 = pick("rr", 0, 288, "rq", 0, 128, T.sl[:, 0:18], n1, c4)
     q1 = v("q", (T.xq[:, 0:272], T.xqs[:, 0:272], T.xt[:, :]), dx, zx)
     ps = lambda b, n: T.ps[:, 512 * b:512 * b + n]
     for j, (lo, sh) in enumerate([(0, 0), (16, 16), (144, 0), (160, 16)]):
         m0 = mx((ps(0, 256), T.rr[:, lo:lo + 128], T.rrs[:, lo:lo + 128], T.xq[:, sh:sh + 256], T.xqs[:, sh:sh + 256], j == 0, j == 3), q1, r1, r2)
+    v("ts", (f(11), f(2), 0.0, 8.0, A.is_equal, A.mult))
+    c5 = v("ts", (f(12), f(2), 3.0, -8.0, A.is_equal, A.mult))
+    v("ts", (f(16), f(4), -1e-30, None, A.mult))
+    v("tt", (f(17), f(15), f(13), A.mult))
+    v("ts", (f(18), f(3), 16.0, 31.0, A.mult, A.add))
+    v("tt", (f(14), f(11), f(12), A.add), c5)
+    c7 = v("set", (T.one[:, :], 1.0))
+    v("set", (T.m2[:, :], 0.0))
+    v("set", (T.wa[:, :], 0.0))
+    v("set", (T.ul[:, :], 0))
 
     a = v("ts", (T.a1[:, :], ps(0, 256), f(16), f(14), A.is_gt, A.add), m0, c7)
     a = v("tr", (T.a2[:, :], T.a1[:, :]), a)
-    b = v("scan", (T.cc[:, :], T.rst[:, :], T.a2[:, :], 0.0, A.mult, A.add), a, k5)
+    b = v("scan", (T.cc[:, :], T.rst[:, :], T.a2[:, :], 0.0, A.mult, A.add), a)
     a = v("ts", (T.mm[:, :], T.cc[:, :], 1.5, None, A.is_lt), b)
-    a = v("tr", (T.nn[:, :], T.mm[:, :]), a)
     v("ts", (T.mab[:, 0:64], T.cc[:, 3:256:4], 0.0, None, A.is_equal))
-    b = v("ts", (T.mab[:, 64:128], T.cc[:, 3:256:4], 1.0, None, A.is_equal))
-    pt = v("scan", (T.pp[:, :], T.one[:, :], T.nn[:, :], f(17), A.mult, A.add), a)
-    a = tp = v("tr", (T.tp[:, :], T.pp[:, :]), pt)
+    a = v("tr", (T.nn[:, :], T.mm[:, :]), a)
+    v("ts", (T.mab[:, 64:128], T.cc[:, 3:256:4], 1.0, None, A.is_equal))
+    a = v("scan", (T.pp[:, :], T.one[:, :], T.nn[:, :], f(17), A.mult, A.add), a)
+    a = v("tr", (T.tp[:, :], T.pp[:, :]), a)
     a = v("tt", (T.vv[:, :], T.tp[:, 3:256:4], T.k1[:, :], A.add), a, p2)
     v("tt", (T.pab[:, 0:64], T.mab[:, 0:64], T.vv[:, :], A.mult), a)
     a = v("tt", (T.pab[:, 64:128], T.mab[:, 64:128], T.vv[:, :], A.mult))
-    a = v("tt", (T.t1[:, :], T.pab[:, 0:128:2], T.pab[:, 1:128:2], A.add), a)
-    a = v("tt", (T.dd[:, :], T.t1[:, 0:64:2], T.t1[:, 1:64:2], A.add), a)
-    a = v("ts", (T.off1[:, :], T.dd[:, :], f(18), None, A.add), a)
-    a = v("copy", (T.el[:, 0:1088].indirect(T.off1[:, 0:32]), T.tok[:, :]), a, kt, k0)
-    for e in range(4):
-        b = v("tr", (T.lt[:, 160 * e:160 * e + 160], T.el[:, 256 * e + 32:256 * e + 192]), a)
-    v("ts", (T.xn[:, :], T.lt[:, 0:640:16], f(13), None, A.mult), b)
-    a = v("ts", (T.xp[:, :], T.lt[:, 0:640:16], f(3), None, A.mult))
-    v("tt", (T.wl[:, 0:40:2], T.xn[:, 0:40:2], T.xp[:, 1:40:2], A.add), a)
-    a = v("tt", (T.wl[:, 1:39:2], T.xn[:, 3:40:2], T.xp[:, 0:38:2], A.add))
-    a = v("copy", (T.off2[:, 0:39], T.wl[:, 0:39]), a)
-    xtok = {}
-    for e in order + [me]:
-        xtok[e] = pick(T.xs, T.xss, 128 * e, 128 * e + 128, T.xq, T.xqs, 0, 272, T.off2[:, 10 * e:10 * e + 8], (a,))
-    for e in order:
-        i = place(me, e)
-        send(e, codes(T.xl, 128 * i, 128 * i + 128), codes(T.xs, 128 * e, 128 * e + 128), "xa%d" % i, xtok[e][0])
-        send(e, T.xls[:, 128 * i:128 * i + 128], T.xss[:, 128 * e:128 * e + 128], "xa%d" % i, xtok[e][1])
+    a = v("scan", (T.t1[:, :], T.rst[:, 0:128], T.pab[:, :], 0.0, A.mult, A.add), a)
+    a = v("ts", (T.off1[:, :], T.t1[:, 3:128:4], f(18), None, A.add), a)
+    sc = v("copy", (T.el[:, 0:1088].indirect(T.off1[:, 0:32]), T.tok[:, :]), a, kt, k0)
 
+    def turn(e):
+        return v("tr", (T.lt[:, 160 * e:160 * e + 160], T.el[:, 256 * e + 32:256 * e + 192]), sc)
+
+    def wrap(xn, xp, wl, off, lo, n, tok):
+        v("ts", (xn[:, 0:n], T.lt[:, lo:lo + 16 * n:16], f(13), None, A.mult), tok)
+        a = v("ts", (xp[:, 0:n], T.lt[:, lo:lo + 16 * n:16], f(3), None, A.mult))
+        v("tt", (wl[:, 0:n:2], xn[:, 0:n:2], xp[:, 1:n:2], A.add), a)
+        a = v("tt", (wl[:, 1:n - 1:2], xn[:, 3:n:2], xp[:, 0:n - 2:2], A.add))
+        return v("copy", (off[:, 0:n - 1], wl[:, 0:n - 1]), a)
+
+    xtok = {}
+
+    def token(e, off, lo, tok):
+        xtok[e] = pick("xs", 128 * e, 128 * e + 128, "xq", 0, 272, off[:, lo:lo + 8], tok)
+        if e != me:
+            i = place(me, e)
+            send(e, codes(T.xl, 128 * i, 128 * i + 128), codes(T.xs, 128 * e, 128 * e + 128), "xa%d" % i, xtok[e][0])
+            send(e, T.xls[:, 128 * i:128 * i + 128], T.xss[:, 128 * e:128 * e + 128], "xa%d" % i, xtok[e][1])
+    e0 = order[0]
+    token(e0, T.off2a, 0, wrap(T.xn1, T.xp1, T.wl1, T.off2a, 160 * e0, 10, turn(e0)))
+    for e in order[1:] + [me]:
+        a = turn(e)
+    a = wrap(T.xn, T.xp, T.wl, T.off2, 0, 40, a)
+    for e in order[1:] + [me]:
+        token(e, T.off2, 10 * e, a)
+
+    zh = v("set", (T.hb[:, 512:576], 0.0))
+    zu = v("set", (T.ut[:, 8:512], 0.0))
     for i in range(4):
         wq = v("q", (T.wq[:, 128 * i:128 * i + 128], T.wqs[:, 128 * i:128 * i + 128], T.wt[:, 512 * i:512 * i + 512]), dw)
-    v("set", (T.ul[:, :], 0))
-    zu = v("set", (T.ut[:, 8:512], 0.0))
-    zh = v("set", (T.hb[:, 512:576], 0.0))
-    uq = v("q", (T.uq[:, :], T.uqs[:, :], T.ut[:, :]), du, zu)
-    ur = pick(T.ur, T.urs, 0, 128, T.uq, T.uqs, 0, 128, T.ul[:, 0:8], (uq,))
 
     sets = [0]
 
-    def chunk(xc, xsc, lo, toks, hlo, hn, hc, hsc, hto, free):
+    def chunk(xc, lo, toks, hlo, hn, hc, hto, free):
         b = 4 * (sets[0] % 2)
         sets[0] += 1
         h = []
         for i in range(4):
-            m = mx((ps(b + i, 128), T.wq[:, 128 * i:128 * i + 128], T.wqs[:, 128 * i:128 * i + 128], xc[:, lo:lo + 128], xsc[:, lo:lo + 128], True, True), wq, *(tuple(toks) + tuple(free)))
+            m = mx((ps(b + i, 128), T.wq[:, 128 * i:128 * i + 128], T.wqs[:, 128 * i:128 * i + 128], T[xc][:, lo:lo + 128], T[xc + "s"][:, lo:lo + 128], True, True), wq, *(tuple(toks) + tuple(free)))
             out = T.hb[:, hlo + i:hlo + 512:4]
             h.append(act((out, ps(b + i, 128), F.Relu, 0.0, 0.0625), m) if i % 2 == 0 else v("ts", (out, ps(b + i, 128), 0.0, 0.0625, A.max, A.mult), m))
-        return b, v("q", (hc[:, hto:hto + hn], hsc[:, hto:hto + hn], T.hb[:, hlo:hlo + 4 * hn]), *h)
+        return b, v("q", (T[hc][:, hto:hto + hn], T[hc + "s"][:, hto:hto + hn], T.hb[:, hlo:hlo + 4 * hn]), *h)
 
-    b0, h0 = chunk(T.xs, T.xss, 128 * me, xtok[me], 0, 144, T.zq, T.zqs, 0, ())
+    b0, h0 = chunk("xs", 128 * me, xtok[me], 0, 144, "zq", 0, ())
+    uq = v("q", (T.uq[:, :], T.uqs[:, :], T.ut[:, :]), du, zu)
+    ur = pick("ur", 0, 128, "uq", 0, 128, T.ul[:, 0:8], uq)
     g0 = v("set", (T.gt[:, :], -9e29))
     m = mx((ps(b0, 128), T.ur[:, :], T.urs[:, :], T.zq[:, 0:128], T.zqs[:, 0:128], True, True), h0, *ur)
     own = v("copy", (T.gt[:, 0:128], ps(b0, 128)), m, g0)
 
-    rel = {me: 0}
-    for i, r in enumerate(others):
-        rel[r] = 128 + 128 * i
+    rel = [0 if e == me else 128 + 128 * others.index(e) for e in range(4)]
     for e in range(4):
         c = v("set", (T.kr[:, e:64:4], float(rel[e] - 1 - 512)))
-    for e in range(4):
-        v("set", (T.kz[:, e:64:4], float(-1 - 128 if e == me else 144 + 48 * others.index(e) - 1 - 128)))
     v("ts", (T.tk[:, :], T.tp[:, 3:256:4], 128.5, None, A.is_lt))
-    v("tt", (T.v2[:, :], T.tp[:, 3:256:4], T.kr[:, :], A.add), c)
     k7 = v("ts", (T.kv[:, :], T.kv[:, :], f(13), None, A.subtract), p3)
-    v("ts", (T.k3[:, :], T.k3[:, :], f(20), f(0), A.add, A.subtract), p4)
-    v("ts", (T.tr[:, :], T.tr[:, :], f(0), None, A.add), p5)
-    v("set", (T.m2[:, :], 0.0))
-    v("set", (T.l3[:, :], 1.0))
-    c = v("ts", (T.kv2[:, :], T.kv[:, :], 0.0, None, A.is_ge), k7)
+    c = v("tt", (T.v2[:, :], T.tp[:, 3:256:4], T.kr[:, :], A.add), c)
     v("tt", (T.abe[:, 0:64], T.mab[:, 0:64], T.tk[:, :], A.mult), c)
     a = v("tt", (T.abe[:, 64:128], T.mab[:, 64:128], T.tk[:, :], A.mult))
-    c = v("ts", (T.kv[:, :], T.kv[:, :], 13.5, None, A.is_lt), c)
+    v("ts", (T.kv2[:, :], T.kv[:, :], 0.0, None, A.is_ge), k7)
+    c = v("ts", (T.kv[:, :], T.kv[:, :], 13.5, None, A.is_lt))
     v("tt", (T.pab2[:, 0:64], T.abe[:, 0:64], T.v2[:, :], A.mult), a)
     a = v("tt", (T.pab2[:, 64:128], T.abe[:, 64:128], T.v2[:, :], A.mult))
     c = v("tt", (T.kv2[:, :], T.kv2[:, :], T.kv[:, :], A.mult), c)
-    a = v("tt", (T.t2[:, :], T.pab2[:, 0:128:2], T.pab2[:, 1:128:2], A.add), a)
+    a = v("scan", (T.t2[:, :], T.rst[:, 0:128], T.pab2[:, :], 0.0, A.mult, A.add), a)
     v("tt", (T.ae[:, :], T.abe[:, 0:64], T.kv2[:, :], A.mult), c)
     c = v("tt", (T.be[:, :], T.abe[:, 64:128], T.kv2[:, :], A.mult))
-    a = v("tt", (T.d2[:, :], T.t2[:, 0:64:2], T.t2[:, 1:64:2], A.add), a)
-    c = v("tt", (T.de[:, :], T.ae[:, :], T.be[:, :], A.subtract), c)
-    o3 = v("ts", (T.off3[:, :], T.d2[:, :], 512.0, None, A.add), a)
-    v("set", (T.ll[:, :], 1.0))
-    v("set", (T.wnw[:, :], 0.0))
-    vq = v("q", (T.vq[:, :], T.vqs[:, :], T.vt[:, :]), dv)
+    o3 = v("ts", (T.off3[:, :], T.t2[:, 3:128:4], 512.0, None, A.add), a)
+    v("tt", (T.de[:, :], T.ae[:, :], T.be[:, :], A.subtract), c)
 
     bank = {b0: (own,)}
     hq = {}
@@ -277,7 +247,7 @@ def rank_program(g, core, T, topo):
         n = 2 * len(topo.engines(T.cores[s], core))
         total["xa%d" % i] = n
         b = 4 * (sets[0] % 2)
-        b, h = chunk(T.xl, T.xls, 128 * i, (("xa%d" % i, n),), 576 + 512 * i, 128, T.hq, T.hqs, 128 * i, bank.get(b, ()))
+        b, h = chunk("xl", 128 * i, (("xa%d" % i, n),), 576 + 512 * i, 128, "hq", 128 * i, bank.get(b, ()))
         hq[s] = h
         m = mx((ps(b, 128), T.hq[:, 128 * i:128 * i + 128], T.hqs[:, 128 * i:128 * i + 128], T.uq[:, :], T.uqs[:, :], True, True), h)
         c = act((T.qs[:, i:i + 1], ps(b, 1), F.Copy), m)
@@ -285,11 +255,20 @@ def rank_program(g, core, T, topo):
         k = place(me, s)
         send(s, T.dg[128 * k:128 * k + 128, :], T.qs[:, i:i + 1], "qa", c)
 
+    v("ts", (T.k3[:, :], T.k3[:, :], f(20), f(0), A.add, A.subtract), p4)
+    v("ts", (T.tr[:, :], T.tr[:, :], f(0), None, A.add), p5)
+    v("set", (T.l3[:, :], 1.0))
+    v("set", (T.ll[:, :], 1.0))
+    v("set", (T.wnw[:, :], 0.0))
+    for e in range(4):
+        v("set", (T.kz[:, e:64:4], float(-1 - 128 if e == me else 144 + 48 * others.index(e) - 1 - 128)))
+    vq = v("q", (T.vq[:, :], T.vqs[:, :], T.vt[:, :]), dv)
+
     qa = ("qa", sum(len(topo.engines(T.cores[s], core)) for s in others))
     for k in range(8):
         gd = dma("y" if k % 2 == 0 else "s", T.gt[16 * k:16 * k + 1, 128:512], T.dg[:, :], "dgt", qa, own)
-    a = v("copy", (T.gab[:, :], T.gt[:, 0:520].indirect(T.off3[:, 0:32])), gd, o3, own)
-    a = v("tt", (T.wa[:, :], T.gab[:, 0:256], T.gab[:, 256:512], A.is_ge), a)
+    a = v("copy", (T.gab[:, 0:240], T.gt[:, 0:520].indirect(T.off3[:, 16:31])), gd, vq)
+    a = v("tt", (T.wa[:, 0:240], T.gt[:, 0:520].indirect(T.off3[:, 0:15]), T.gab[:, 0:240], A.is_ge), a)
     a = v("tr", (T.wat[:, :], T.wa[:, :]), a)
     for e in range(4):
         b = v("tt", (T.x4[:, e:64:4], T.wat[:, 0:256:16], T.de[:, e:64:4], A.mult), a)
@@ -297,21 +276,20 @@ def rank_program(g, core, T, topo):
     a = v("tt", (w4, T.x4[:, :], T.be[:, :], A.add), b)
     a = v("tr", (T.n2[:, :], T.m2[:, :]), a)
     a = v("scan", (T.rc[:, :], T.one[:, :], T.n2[:, :], 0.0, A.mult, A.add), a)
-    rt = v("tr", (T.rtr[:, :], T.rc[:, :]), a)
+    a = v("tr", (T.rtr[:, :], T.rc[:, :]), a)
     r4 = T.rtr[:, 3:256:4]
-    a = v("tt", (T.s1[:, :], r4, T.k3[:, :], A.add), rt)
+    a = v("tt", (T.s1[:, :], r4, T.k3[:, :], A.add), a)
     a = v("tt", (T.s2[:, :], T.s1[:, :], w4, A.mult), a)
-    a = v("tt", (T.s3[:, :], T.s2[:, 0:64:2], T.s2[:, 1:64:2], A.add), a)
-    a = v("tt", (T.s4[:, :], T.s3[:, 0:32:2], T.s3[:, 1:32:2], A.add), a)
-    a = v("tt", (T.s5[:, :], T.s4[:, :], T.tr[:, :], A.add), a)
+    a = v("scan", (T.s3[:, :], T.rst[:, 0:64], T.s2[:, :], 0.0, A.mult, A.add), a)
+    a = v("tt", (T.s5[:, :], T.s3[:, 3:64:4], T.tr[:, :], A.add), a)
     a = v("copy", (T.off4[:, :], T.s5[:, :]), a)
-    a = v("copy", (T.l3[:, 0:912].indirect(T.off4[:, 0:16]), T.pp[:, :]), a)
+    a = v("copy", (T.l3[:, 0:912].indirect(T.off4[:, 0:15]), T.pp[:, 0:240]), a)
     for e in range(4):
         b = v("tr", (T.l3t[:, 64 * e:64 * e + 64], T.l3[:, 160 * e:160 * e + 64]), a)
-    c = act((T.l3p[:, :], T.l3t[:, :], F.Copy, 0.0, f(3)), b)
-    b = v("ts", (T.l3n[:, :], T.l3t[:, :], f(13), None, A.mult), b)
+    v("ts", (T.l3n[:, :], T.l3t[:, :], f(13), None, A.mult), b)
+    b = v("ts", (T.l3p[:, :], T.l3t[:, :], f(3), None, A.mult))
     at = lambda t, x: t[:, x:x + 205:68]
-    v("tt", (T.ll[:, 0:16:4], at(T.l3n, 3), at(T.l3p, 19), A.add), b, c)
+    v("tt", (T.ll[:, 0:16:4], at(T.l3n, 3), at(T.l3p, 19), A.add), b)
     v("tt", (T.ll[:, 1:16:4], at(T.l3n, 51), at(T.l3p, 3), A.add))
     a = v("tt", (T.ll[:, 2:16:4], at(T.l3n, 35), at(T.l3p, 51), A.add))
     a = v("ts", (T.ls[:, :], T.ll[:, :], -1.0, None, A.add), a)
@@ -321,20 +299,18 @@ def rank_program(g, core, T, topo):
 
     v("ts", (T.h1[:, :], r4, 48.5, None, A.is_lt))
     a = v("copy", (T.xz[:, :], r4))
-    c = v("tt", (T.wa1[:, :], w4, T.ka[:, :], A.mult), p6)
+    c = v("tt", (T.w1[:, :], w4, T.ka[:, :], A.mult), p6)
     a = v("copy", (T.xz[:, me:64:4], T.tp[:, 4 * me + 3:256:16]), a)
     b = v("tt", (T.hm[:, :], w4, T.h1[:, :], A.mult), c)
     a = v("tt", (T.z1[:, :], T.xz[:, :], T.kz[:, :], A.add), a)
-    c = v("tt", (T.s1[:, :], T.hm[:, :], T.kb[:, :], A.mult), b, p7)
+    c = v("tt", (T.w2[:, :], T.hm[:, :], T.kb[:, :], A.mult), b, p7)
     a = v("tt", (T.z2[:, :], T.z1[:, :], T.hm[:, :], A.mult), a, b)
-    c = v("tt", (T.s2[:, :], T.s1[:, :], T.wa1[:, :], A.add), c)
-    a = v("tt", (T.z3[:, :], T.z2[:, 0:64:2], T.z2[:, 1:64:2], A.add), a)
-    c = v("tt", (T.w3[:, 0:32], T.s2[:, 0:64:2], T.s2[:, 1:64:2], A.add), c)
-    a = v("tt", (T.zi[:, :], T.z3[:, 0:32:2], T.z3[:, 1:32:2], A.add), a)
-    c = v("tt", (T.w3[:, 32:48], T.w3[:, 0:32:2], T.w3[:, 1:32:2], A.add), c)
-    v("ts", (T.zn[:, :], T.zi[:, :], f(13), None, A.mult), a)
-    a = v("ts", (T.zp[:, :], T.zi[:, :], f(3), None, A.mult))
-    c = v("ts", (T.wnw[:, 0:256:16], T.w3[:, 32:48], -100.0, None, A.add), c)
+    c = v("tt", (T.w3[:, :], T.w2[:, :], T.w1[:, :], A.add), c)
+    a = v("scan", (T.z3[:, :], T.rst[:, 0:64], T.z2[:, :], 0.0, A.mult, A.add), a)
+    c = v("scan", (T.w4[:, :], T.rst[:, 0:64], T.w3[:, :], 0.0, A.mult, A.add), c)
+    v("ts", (T.zn[:, :], T.z3[:, 3:64:4], f(13), None, A.mult), a)
+    a = v("ts", (T.zp[:, :], T.z3[:, 3:64:4], f(3), None, A.mult))
+    c = v("ts", (T.wnw[:, 0:256:16], T.w4[:, 3:64:4], -100.0, None, A.add), c)
     a = v("tt", (T.zl[:, :], T.zn[:, 1:15], T.zp[:, 0:14], A.add), a)
     c = v("tr", (T.wnf[:, :], T.wnw[:, :]), c)
     zo = v("ts", (T.off5[:, :], T.zl[:, :], 128.0, None, A.add), a)
@@ -344,13 +320,13 @@ def rank_program(g, core, T, topo):
         i = others.index(s)
         n = len(topo.engines(T.cores[s], core))
         total["ar%d" % i] = n
-        x, y = pick(T.hs, T.hss, 48 * i, 48 * i + 48, T.hq, T.hqs, 128 * i, 128 * i + 128, T.la[:, 4 * i:4 * i + 3], (hq[s], ("ar%d" % i, n)))
+        x, y = pick("hs", 48 * i, 48 * i + 48, "hq", 128 * i, 128 * i + 128, T.la[:, 4 * i:4 * i + 3], hq[s], ("ar%d" % i, n))
         k = 144 + 48 * place(me, s)
         send(s, codes(T.zq, k, k + 48), codes(T.hs, 48 * i, 48 * i + 48), "ha", x)
         send(s, T.zqs[:, k:k + 48], T.hss[:, 48 * i:48 * i + 48], "ha", y)
 
     ha = ("ha", 2 * qa[1])
-    x, y = pick(T.z, T.zs, 0, 224, T.zq, T.zqs, 0, 288, T.off5[:, 0:14], (ha, zo, h0))
+    x, y = pick("z", 0, 224, "zq", 0, 288, T.off5[:, 0:14], ha, zo, h0)
     m = mx((ps(0, 224), T.vq[:, :], T.vqs[:, :], T.z[:, :], T.zs[:, :], True, True), x, y, vq)
     yc = v("copy", (T.ysb[:, :], ps(0, 224)), m)
     dma("y", T.oc[:, :], codes(T.z, 0, 224), "out", x)

@@ -6,7 +6,7 @@ def _buffers():
     kinds = {
         "bfloat16": "xt 1088 rtt 512 wt 2048 ut 512 vt 512 hb 2112 rst 256 one 256 tok 512 a1 256 a2 256 cc 256 mm 256 nn 256 "
                     "pp 256 tp 256 el 1088 lt 640 wa 256 wat 256 m2 256 n2 256 rc 256 rtr 256 l3 912 l3t 256 l3n 256 l3p 256",
-        "float32": "ysb 224 sf 32 zero 8 tokf 512 k1 64 k3 64 ka 64 kb 64 kz 64 kr 64 kv 64 kv2 64 tr 16 mab 128 vv 64 pab 128 "
+        "float32": "ysb 224 sf 32 zero 8 tokf 512 k1 64 k3 64 ka 64 kb 64 kz 64 kr 64 kv 64 kv2 64 kv3 64 tr 16 mab 128 vv 64 pab 128 "
                    "t1 128 xn 40 xp 40 wl 40 xn1 10 xp1 10 wl1 10 tk 64 abe 128 v2 64 pab2 128 t2 128 ae 64 be 64 de 64 qs 4 "
                    "gt 520 gab 256 x4 64 s1 64 s2 64 s3 64 s5 16 ll 16 h1 64 hm 64 xz 64 z1 64 z2 64 z3 64 zn 16 zp 16 zl 14 "
                    "w1 64 w2 64 w3 64 w4 64 wnw 256 wnf 256",
@@ -27,6 +27,109 @@ def _buffers():
 SCRATCH = _buffers()
 SEMAPHORES = ["v", "s", "t", "p", "dx", "dr", "dw", "du", "dv", "dgt", "out", "sent", "qa", "ha"] \
     + ["xa%d" % i for i in range(3)] + ["ar%d" % i for i in range(3)]
+WAKE, CYC = 0.12, 0.00083
+
+
+def _o(name, a=0, z=None, step=1):
+    return ("@", name, a, SCRATCH[name][1][1] if z is None else z, step, None, None)
+
+
+def _cast(o, how):
+    return o[:5] + (how, o[6])
+
+
+def _ind(o, off):
+    return o[:6] + (off,)
+
+
+def _keys(o):
+    if o[1] == "ps":
+        return [("ps", b) for b in range(o[2] // 512, (o[3] - 1) // 512 + 1)]
+    return [(o[1], c) for c in range(o[2], o[3], o[4])]
+
+
+def _isop(x):
+    return isinstance(x, tuple) and len(x) == 7 and x[0] == "@"
+
+
+def _width(o):
+    return 16 * (o[6][3] - o[6][2]) if o[6] else len(range(o[2], o[3], o[4]))
+
+
+def _cost(name, args):
+    out, n = args[0], _width(args[0])
+    if name == "mx":
+        return (n + 16) * CYC
+    if name == "q":
+        return .012 + .00088 * n
+    ops = [a for a in args if _isop(a)]
+    if name == "iota":
+        return .13 + 2 * n * CYC
+    if name == "act":
+        return .065 + n * CYC * (1.5 if args[1][6] else 1)
+    if out[6]:
+        return .05 + 3 * n * CYC
+    if any(a[6] for a in ops):
+        return .05 + 1.6 * n * CYC
+    two = all(SCRATCH[a[1]][2] in ("bfloat16", "uint16") for a in ops if _width(a) > 1)
+    return max(64, n * (2 if name == "tt" else .5 if two else 1)) * CYC
+
+
+def _order(ops):
+    n = len(ops)
+    prio = [0.0] * n
+    for i in range(n - 1, -1, -1):
+        prio[i] += ops[i]["cost"] + ops[i]["lat"]
+        for d in ops[i]["deps"]:
+            prio[d] = max(prio[d], prio[i] + WAKE)
+    need = [len(o["deps"]) for o in ops]
+    succ = [[] for o in ops]
+    for i, o in enumerate(ops):
+        for d in o["deps"]:
+            succ[d].append(i)
+    ready, fin, free = [0.0] * n, [0.0] * n, {}
+    can, lists = {}, {}
+
+    def release(i):
+        q = ops[i]["q"]
+        if q is None:
+            finish(i, ready[i])
+        else:
+            can.setdefault(q, []).append(i)
+
+    def finish(i, start):
+        fin[i] = start + ops[i]["cost"] + ops[i]["lat"]
+        for j in succ[i]:
+            ready[j] = max(ready[j], fin[i] + (WAKE if ops[j]["q"] else 0))
+            need[j] -= 1
+            if need[j] == 0:
+                release(j)
+    for i in range(n):
+        if not ops[i]["deps"]:
+            release(i)
+    while True:
+        best = None
+        for q, c in can.items():
+            if not c:
+                continue
+            t = free.get(q, 0.0)
+            m = min(max(t, ready[i]) for i in c)
+            pick = max((i for i in c if max(t, ready[i]) <= m + 1e-9), key=lambda i: prio[i])
+            for d in sorted(c, key=lambda i: -prio[i]):
+                e = max(t, ready[d])
+                if prio[d] > prio[pick] and e - m < m + ops[pick]["cost"] - e:
+                    pick, m = d, e
+                    break
+            if best is None or m < best[0]:
+                best = (m, q, pick)
+        if best is None:
+            break
+        m, q, i = best
+        can[q].remove(i)
+        lists.setdefault(q, []).append(i)
+        free[q] = m + ops[i]["cost"]
+        finish(i, m)
+    return lists
 
 
 def rank_program(g, core, T, topo):
@@ -41,298 +144,352 @@ def rank_program(g, core, T, topo):
         return 2 if topo.mates(a, b) else 1 if topo.same_plane(a, b) else 0
     order = sorted(others, key=far)
 
-    V, SC, TE = g.vector, g.scalar, g.tensor
-    queue = {"v": V, "s": SC, "t": TE, "p": g, "y": g.sync}
-    count = {"v": 0, "s": 0, "t": 0, "p": 0}
-    seen = {q: {} for q in queue}
+    ops, wrote, readers = [], {}, {}
     total = {}
+    kinds = {"u8": dt.uint8, "u32": dt.uint32}
 
-    def wait(q, *toks):
-        best = {}
-        for s, n in toks:
-            best[s] = max(n, best.get(s, 0))
-        for s, n in best.items():
-            if seen[q].get(s, 0) < n:
-                queue[q].wait_ge(T.sem[s], n)
-                seen[q][s] = n
+    def mat(o):
+        x = T[o[1]][:, o[2]:o[3]] if o[4] == 1 else T[o[1]][:, o[2]:o[3]:o[4]]
+        if o[5]:
+            x = x.bitcast(kinds[o[5]])
+        return x.indirect(mat(o[6])) if o[6] else x
 
-    def do(q, call, args, *toks):
-        wait(q, *toks)
-        call(*args).then_inc(T.sem[q], 1)
-        count[q] += 1
-        return (q, count[q])
+    def add(q, fn, outs, ins, cost, lat=0.0, sem=None, extra=()):
+        i, deps = len(ops), set(extra)
+        for o in list(ins) + list(outs):
+            if o[6]:
+                ins = list(ins) + [o[6]]
+        for o in ins:
+            if o[1] != "ps":
+                for k in _keys(o):
+                    if k in wrote:
+                        deps.add(wrote[k])
+                    readers.setdefault(k, []).append(i)
+        for o in list(outs) + [o for o in ins if o[1] == "ps"]:
+            for k in _keys(o):
+                if k in wrote:
+                    deps.add(wrote[k])
+                deps.update(readers.pop(k, ()))
+                wrote[k] = i
+        deps.discard(i)
+        ops.append({"q": q, "fn": fn, "deps": deps, "cost": cost, "lat": lat, "sem": sem})
+        return i
 
+    V = g.vector
     calls = {"copy": V.tensor_copy, "tt": V.tensor_tensor, "ts": V.tensor_scalar, "set": V.memset, "tr": V.transpose,
-             "scan": V.tensor_tensor_scan, "q": V.quantize_mx}
-    v = lambda name, args, *toks: do("v", calls[name], args, *toks)
-    act = lambda args, *toks: do("s", SC.activation, args, *toks)
-    mx = lambda args, *toks: do("t", TE.matmul_mx, args, *toks)
+             "scan": V.tensor_tensor_scan, "q": V.quantize_mx, "act": g.scalar.activation, "mx": g.tensor.matmul_mx,
+             "iota": lambda *a: g.iota(*a, allow_small_or_imprecise_dtypes=True), "iota32": g.iota}
 
-    def iota(buf, pattern, base, mul, f=True):
-        return do("p", lambda *a: g.iota(*a, allow_small_or_imprecise_dtypes=f), (buf, pattern, base, mul))
+    def do(q, name, args):
+        k = 2 if name == "q" else 1
+        fn = lambda: calls[name](*[mat(a) if _isop(a) else a for a in args])
+        return add(q, fn, args[:k], [a for a in args[k:] if _isop(a)], _cost(name.replace("32", ""), args), 0.0, "own")
 
-    def dma(q, out, in_, sem, *toks):
-        wait(q, *toks)
-        queue[q].dma_start(out, in_).then_inc(T.sem[sem], 16)
+    v = lambda name, *args: do("v", name, args)
+    act = lambda *args: do("s", "act", args)
+    mx = lambda *args: do("t", "mx", args)
+    iota = lambda *args: do("p", "iota", args)
+
+    def dma(q, sem, out, in_, outs, ins, extra=(), lat=2.1):
+        e = {"y": g.sync, "s": g.scalar}[q]
         total[sem] = total.get(sem, 0) + 16
-        return (sem, total[sem])
+        return add(q, lambda: e.dma_start(out(), in_()), outs, ins, 0.06, lat, sem, extra)
 
-    def send(dst, out, in_, sem, *toks):
-        wait("p", *toks)
+    def send(dst, out, in_, sem):
         c = T.cores[dst]
         rid, pid, _ = topo.addr(c)
-        g.remote_dma(out, in_, T.sem[sem], T.sem["sent"], pid, rid, topo.mask(core, c))
         total["sent"] = total.get("sent", 0) + len(topo.engines(core, c))
+        return add("p", lambda: g.remote_dma(mat(out), mat(in_), T.sem[sem], T.sem["sent"], pid, rid, topo.mask(core, c)), [], [in_], 0.25)
 
-    u8, u32 = dt.uint8, dt.uint32
-    codes = lambda b, a, z: b[:, a:z].bitcast(u8)
+    def arrive(sem, src, writes, outs, lat, extra):
+        total[sem] = total.get(sem, 0) + writes * sum(len(topo.engines(T.cores[s], core)) for s in src)
+        return add(None, None, outs, [], 0.0, lat, sem, extra)
 
-    def pick(to, a, z, win, c, d, off, *toks):
-        x = v("copy", (T[to][:, a:z].bitcast(u32), T[win][:, c:d].bitcast(u32).indirect(off)), *toks)
-        y = act((T[to + "s"][:, a:z], T[win + "s"][:, c:d].indirect(off), F.Copy), *toks)
-        return x, y
+    def pick(to, a, z, win, c, d, off):
+        v("copy", _cast(_o(to, a, z), "u32"), _ind(_cast(_o(win, c, d), "u32"), off))
+        act(_o(to + "s", a, z), _ind(_o(win + "s", c, d), off), F.Copy)
 
-    dr = dma("s", T.rtt[:, 0:16], T.rt[:, 0:16], "dr")
-    dx = dma("y", T.xt[:, 64:960], T.x[:, :], "dx")
-    wait("y", dx)
-    dw = dma("y", T.wt[:, :], T.w[:, :], "dw")
-    du = dma("y", T.ut[:, 0:8], T.u[:, 0:8], "du")
-    dv = dma("y", T.vt[:, :], T.v[:, :], "dv")
+    o, H, W = _o, [(0, 128), (128, 256)], [(0, 32), (32, 64)]
+    f = lambda k: _o("sf", k, k + 1)
+    role = lambda b: _o(b, 3, 256, 4)
+    ps = lambda b, n: _o("ps", 512 * b, 512 * b + n)
 
-    p0 = iota(T.si[:, 0:1], [[0, 1]], 0, 1, False)
-    for k in range(2):
-        iota(T.tokf[:, 256 * k:256 * k + 240], [[1, 240]], 0, 0)
-        p1 = iota(T.tokf[:, 256 * k + 240:256 * k + 256], [[0, 16]], 240, 0)
-    p2 = iota(T.k1[:, :], [[0, 16], [256, 4]], 0, 0)
-    p3 = iota(T.kv[:, :], [[1, 16], [0, 4]], 0, 0)
-    p4 = iota(T.k3[:, :], [[-16, 16], [160, 4]], -657, 0)
-    p5 = iota(T.tr[:, :], [[16, 16]], 656, 0)
-    p6 = iota(T.ka[:, :], [[0, 16], [-1, 4]], 99, 0)
-    p7 = iota(T.kb[:, :], [[0, 16], [2, 4]], 1, 0)
-    f = lambda k: T.sf[:, k:k + 1]
-    zr = v("set", (T.rtt[:, 32:512], 0.0))
-    v("set", (T.zero[:, :], 0.0))
-    v("set", (T.sl[:, :], 8))
-    v("ts", (T.si[:, 1:2], T.si[:, 0:1], 15, None, A.bitwise_and), p0)
-    v("ts", (T.si[:, 2:3], T.si[:, 0:1], 15, 2, A.bitwise_and, A.logical_shift_right))
-    v("ts", (T.si[:, 3:4], T.si[:, 0:1], 3, None, A.bitwise_and))
-    i4 = v("ts", (T.si[:, 4:5], T.si[:, 0:1], 16, 4, A.bitwise_and, A.logical_shift_right))
-    v("set", (T.xt[:, 0:64], 0.0))
-    zx = v("set", (T.xt[:, 960:1088], 0.0))
-    c0 = v("copy", (T.sf[:, 0:4], T.si[:, 1:5]), i4)
-    v("set", (T.rst[:, :], 1.0))
-    v("ts", (f(4), f(2), f(1), None, A.is_lt), c0)
-    v("ts", (f(5), f(2), 3.0, None, A.is_lt))
-    v("ts", (f(6), f(1), -4.0, None, A.add))
-    c1 = v("ts", (f(7), f(2), -7.0, None, A.add))
-    c8 = v("ts", (f(20), f(3), 16.0, None, A.mult))
-    v("tt", (f(8), f(7), f(4), A.subtract), c1)
-    c2 = v("tt", (f(9), f(6), f(5), A.mult))
-    v("ts", (f(13), f(3), -1.0, 1.0, A.mult, A.add))
-    v("ts", (f(15), f(1), 2.0, -16.0, A.is_lt, A.mult))
-    c3 = v("tt", (f(10), f(8), f(5), A.mult), c2)
-    v("set", (T.rst[:, 0:256:4], 0.0), c0)
-    v("ts", (T.sl[:, 0:9:2], T.zero[:, 0:5], f(10), 8.0, A.add, A.add), c3)
-    c4 = v("ts", (T.sl[:, 9:18:2], T.zero[:, 0:5], f(9), 8.0, A.add, A.add))
-    k0 = v("set", (T.el[:, :], 0.0))
-    kt = act((T.tok[:, :], T.tokf[:, :], F.Identity, f(20)), c8, p1)
+    dma("s", "dr", lambda: T.rtt[:, 0:16], lambda: T.rt[:, 0:16], [o("rtt", 0, 16)], [])
+    dx = dma("y", "dx", lambda: T.xt[:, 64:960], lambda: T.x[:, :], [o("xt", 64, 960)], [], (), 3.0)
+    dma("y", "dw", lambda: T.wt[:, :], lambda: T.w[:, :], [o("wt")], [], (dx,), 4.5)
+    dma("y", "du", lambda: T.ut[:, 0:8], lambda: T.u[:, 0:8], [o("ut", 0, 8)], [], (dx,), 4.8)
+    dma("y", "dv", lambda: T.vt[:, :], lambda: T.v[:, :], [o("vt")], [], (dx,), 5.0)
 
-    n0 = v("ts", (T.rtt[:, 16:32], T.rtt[:, 0:16], -1.0, None, A.mult), dr)
-    n1 = v("q", (T.rq[:, :], T.rqs[:, :], T.rtt[:, :]), n0, zr)
-    r1, r2 = pick("rr", 0, 288, "rq", 0, 128, T.sl[:, 0:18], n1, c4)
-    q1 = v("q", (T.xq[:, 0:272], T.xqs[:, 0:272], T.xt[:, :]), dx, zx)
-    ps = lambda b, n: T.ps[:, 512 * b:512 * b + n]
-    for j, (lo, sh) in enumerate([(0, 0), (16, 16), (144, 0), (160, 16)]):
-        m0 = mx((ps(0, 256), T.rr[:, lo:lo + 128], T.rrs[:, lo:lo + 128], T.xq[:, sh:sh + 256], T.xqs[:, sh:sh + 256], j == 0, j == 3), q1, r1, r2)
-    v("ts", (f(11), f(2), 0.0, 8.0, A.is_equal, A.mult))
-    c5 = v("ts", (f(12), f(2), 3.0, -8.0, A.is_equal, A.mult))
-    v("ts", (f(16), f(4), -1e-30, None, A.mult))
-    v("tt", (f(17), f(15), f(13), A.mult))
-    v("ts", (f(18), f(3), 16.0, 31.0, A.mult, A.add))
-    v("tt", (f(14), f(11), f(12), A.add), c5)
-    c7 = v("set", (T.one[:, :], 1.0))
-    v("set", (T.m2[:, :], 0.0))
-    v("set", (T.wa[:, :], 0.0))
-    v("set", (T.ul[:, :], 0))
+    do("p", "iota32", (o("si", 0, 1), [[0, 1]], 0, 1))
+    for k in (0, 256):
+        iota(o("tokf", k, k + 240), [[1, 240]], 0, 0)
+        iota(o("tokf", k + 240, k + 256), [[0, 16]], 240, 0)
+    iota(o("k1"), [[0, 16], [256, 4]], 0, 0)
+    iota(o("kv"), [[1, 16], [0, 4]], 0, 0)
+    iota(o("k3"), [[-16, 16], [160, 4]], -657, 0)
+    iota(o("tr"), [[16, 16]], 656, 0)
+    iota(o("ka"), [[0, 16], [-1, 4]], 99, 0)
+    iota(o("kb"), [[0, 16], [2, 4]], 1, 0)
+    v("set", o("rtt", 32, 512), 0.0)
+    v("set", o("zero"), 0.0)
+    v("set", o("sl"), 8)
+    v("set", o("ul"), 0)
+    v("set", o("xt", 0, 64), 0.0)
+    v("set", o("xt", 960, 1088), 0.0)
+    v("set", o("rst"), 1.0)
+    v("set", o("rst", 0, 256, 4), 0.0)
+    v("set", o("one"), 1.0)
+    v("set", o("el"), 0.0)
+    v("ts", o("si", 1, 2), o("si", 0, 1), 15, None, A.bitwise_and)
+    v("ts", o("si", 2, 3), o("si", 0, 1), 15, 2, A.bitwise_and, A.logical_shift_right)
+    v("ts", o("si", 3, 4), o("si", 0, 1), 3, None, A.bitwise_and)
+    v("ts", o("si", 4, 5), o("si", 0, 1), 16, 4, A.bitwise_and, A.logical_shift_right)
+    v("copy", o("sf", 0, 4), o("si", 1, 5))
+    v("ts", f(4), f(2), f(1), None, A.is_lt)
+    v("ts", f(5), f(2), 3.0, None, A.is_lt)
+    v("ts", f(6), f(1), -4.0, None, A.add)
+    v("ts", f(7), f(2), -7.0, None, A.add)
+    v("tt", f(8), f(7), f(4), A.subtract)
+    v("tt", f(9), f(6), f(5), A.mult)
+    v("tt", f(10), f(8), f(5), A.mult)
+    v("ts", o("sl", 0, 9, 2), o("zero", 0, 5), f(10), 8.0, A.add, A.add)
+    v("ts", o("sl", 9, 18, 2), o("zero", 0, 5), f(9), 8.0, A.add, A.add)
+    v("ts", f(13), f(3), -1.0, 1.0, A.mult, A.add)
+    v("ts", f(20), f(3), 16.0, None, A.mult)
+    v("ts", f(15), f(1), 2.0, -16.0, A.is_lt, A.mult)
+    v("tt", f(17), f(15), f(13), A.mult)
+    v("ts", f(11), f(2), 0.0, 8.0, A.is_equal, A.mult)
+    v("ts", f(12), f(2), 3.0, -8.0, A.is_equal, A.mult)
+    v("tt", f(14), f(11), f(12), A.add)
+    v("ts", f(16), f(4), -1e-30, None, A.mult)
+    v("ts", f(18), f(3), 16.0, 31.0, A.mult, A.add)
+    act(o("tok"), o("tokf"), F.Identity, f(20))
 
-    a = v("ts", (T.a1[:, :], ps(0, 256), f(16), f(14), A.is_gt, A.add), m0, c7)
-    a = v("tr", (T.a2[:, :], T.a1[:, :]), a)
-    b = v("scan", (T.cc[:, :], T.rst[:, :], T.a2[:, :], 0.0, A.mult, A.add), a)
-    a = v("ts", (T.mm[:, :], T.cc[:, :], 1.5, None, A.is_lt), b)
-    v("ts", (T.mab[:, 0:64], T.cc[:, 3:256:4], 0.0, None, A.is_equal))
-    a = v("tr", (T.nn[:, :], T.mm[:, :]), a)
-    v("ts", (T.mab[:, 64:128], T.cc[:, 3:256:4], 1.0, None, A.is_equal))
-    a = v("scan", (T.pp[:, :], T.one[:, :], T.nn[:, :], f(17), A.mult, A.add), a)
-    a = v("tr", (T.tp[:, :], T.pp[:, :]), a)
-    a = v("tt", (T.vv[:, :], T.tp[:, 3:256:4], T.k1[:, :], A.add), a, p2)
-    v("tt", (T.pab[:, 0:64], T.mab[:, 0:64], T.vv[:, :], A.mult), a)
-    a = v("tt", (T.pab[:, 64:128], T.mab[:, 64:128], T.vv[:, :], A.mult))
-    a = v("scan", (T.t1[:, :], T.rst[:, 0:128], T.pab[:, :], 0.0, A.mult, A.add), a)
-    a = v("ts", (T.off1[:, :], T.t1[:, 3:128:4], f(18), None, A.add), a)
-    sc = v("copy", (T.el[:, 0:1088].indirect(T.off1[:, 0:32]), T.tok[:, :]), a, kt, k0)
+    v("ts", o("rtt", 16, 32), o("rtt", 0, 16), -1.0, None, A.mult)
+    v("q", o("rq"), o("rqs"), o("rtt"))
+    pick("rr", 0, 288, "rq", 0, 128, o("sl"))
+    for h, (x0, x1) in enumerate([(0, 144), (144, 272)]):
+        v("q", o("xq", x0, x1), o("xqs", x0, x1), o("xt", 4 * x0, 4 * x1))
+        for j, (lo, sh) in enumerate([(0, 0), (16, 16), (144, 0), (160, 16)]):
+            sh += 128 * h
+            mx(ps(h, 128), o("rr", lo, lo + 128), o("rrs", lo, lo + 128), o("xq", sh, sh + 128), o("xqs", sh, sh + 128), j == 0, j == 3)
 
-    def turn(e):
-        return v("tr", (T.lt[:, 160 * e:160 * e + 160], T.el[:, 256 * e + 32:256 * e + 192]), sc)
+    for h, s in enumerate(H):
+        v("ts", o("a1", *s), ps(h, 128), f(16), f(14), A.is_gt, A.add)
+        v("tr", o("a2", *s), o("a1", *s))
+        v("scan", o("cc", *s), o("rst", *s), o("a2", *s), 0.0, A.mult, A.add)
+        v("ts", o("mm", *s), o("cc", *s), 1.5, None, A.is_lt)
+        v("tr", o("nn", *s), o("mm", *s))
+        v("scan", o("pp", *s), o("one", *s), o("nn", *s), o("pp", 127, 128) if h else f(17), A.mult, A.add)
+        v("tr", o("tp", *s), o("pp", *s))
+    v("ts", o("mab", 0, 64), role("cc"), 0.0, None, A.is_equal)
+    v("ts", o("mab", 64, 128), role("cc"), 1.0, None, A.is_equal)
+    v("tt", o("vv"), role("tp"), o("k1"), A.add)
+    v("tt", o("pab", 0, 64), o("mab", 0, 64), o("vv"), A.mult)
+    v("tt", o("pab", 64, 128), o("mab", 64, 128), o("vv"), A.mult)
+    v("scan", o("t1"), o("rst", 0, 128), o("pab"), 0.0, A.mult, A.add)
+    v("ts", o("off1"), o("t1", 3, 128, 4), f(18), None, A.add)
+    v("copy", _ind(o("el"), o("off1")), o("tok"))
 
-    def wrap(xn, xp, wl, off, lo, n, tok):
-        v("ts", (xn[:, 0:n], T.lt[:, lo:lo + 16 * n:16], f(13), None, A.mult), tok)
-        a = v("ts", (xp[:, 0:n], T.lt[:, lo:lo + 16 * n:16], f(3), None, A.mult))
-        v("tt", (wl[:, 0:n:2], xn[:, 0:n:2], xp[:, 1:n:2], A.add), a)
-        a = v("tt", (wl[:, 1:n - 1:2], xn[:, 3:n:2], xp[:, 0:n - 2:2], A.add))
-        return v("copy", (off[:, 0:n - 1], wl[:, 0:n - 1]), a)
+    def wrap(x, lo, n):
+        xn, xp, wl, off = "xn" + x, "xp" + x, "wl" + x, "off2" + ("a" if x else "")
+        v("ts", o(xn), o("lt", lo, lo + 16 * n, 16), f(13), None, A.mult)
+        v("ts", o(xp), o("lt", lo, lo + 16 * n, 16), f(3), None, A.mult)
+        v("tt", o(wl, 0, n, 2), o(xn, 0, n, 2), o(xp, 1, n, 2), A.add)
+        v("tt", o(wl, 1, n - 1, 2), o(xn, 3, n, 2), o(xp, 0, n - 2, 2), A.add)
+        v("copy", o(off, 0, n - 1), o(wl, 0, n - 1))
 
-    xtok = {}
+    sent = []
 
-    def token(e, off, lo, tok):
-        xtok[e] = pick("xs", 128 * e, 128 * e + 128, "xq", 0, 272, off[:, lo:lo + 8], tok)
+    def token(e, off):
+        pick("xs", 128 * e, 128 * e + 128, "xq", 0, 272, off)
         if e != me:
             i = place(me, e)
-            send(e, codes(T.xl, 128 * i, 128 * i + 128), codes(T.xs, 128 * e, 128 * e + 128), "xa%d" % i, xtok[e][0])
-            send(e, T.xls[:, 128 * i:128 * i + 128], T.xss[:, 128 * e:128 * e + 128], "xa%d" % i, xtok[e][1])
-    e0 = order[0]
-    token(e0, T.off2a, 0, wrap(T.xn1, T.xp1, T.wl1, T.off2a, 160 * e0, 10, turn(e0)))
+            sent.append(send(e, _cast(o("xl", 128 * i, 128 * i + 128), "u8"), _cast(o("xs", 128 * e, 128 * e + 128), "u8"), "xa%d" % i))
+            sent.append(send(e, o("xls", 128 * i, 128 * i + 128), o("xss", 128 * e, 128 * e + 128), "xa%d" % i))
+    for n, e in enumerate(order + [me]):
+        v("tr", o("lt", 160 * e, 160 * e + 160), o("el", 256 * e + 32, 256 * e + 192))
+        if n == 0:
+            wrap("1", 160 * e, 10)
+            token(e, o("off2a", 0, 8))
+    wrap("", 0, 40)
     for e in order[1:] + [me]:
-        a = turn(e)
-    a = wrap(T.xn, T.xp, T.wl, T.off2, 0, 40, a)
-    for e in order[1:] + [me]:
-        token(e, T.off2, 10 * e, a)
+        token(e, o("off2", 10 * e, 10 * e + 8))
 
-    zh = v("set", (T.hb[:, 512:576], 0.0))
-    zu = v("set", (T.ut[:, 8:512], 0.0))
+    v("set", o("hb", 512, 576), 0.0)
+    v("set", o("ut", 8, 512), 0.0)
     for i in range(4):
-        wq = v("q", (T.wq[:, 128 * i:128 * i + 128], T.wqs[:, 128 * i:128 * i + 128], T.wt[:, 512 * i:512 * i + 512]), dw)
-
+        v("q", o("wq", 128 * i, 128 * i + 128), o("wqs", 128 * i, 128 * i + 128), o("wt", 512 * i, 512 * i + 512))
+    v("q", o("uq"), o("uqs"), o("ut"))
+    pick("ur", 0, 128, "uq", 0, 128, o("ul"))
     sets = [0]
 
-    def chunk(xc, lo, toks, hlo, hn, hc, hto, free):
+    def chunk(xc, lo, hlo, hn, hc, hto):
         b = 4 * (sets[0] % 2)
         sets[0] += 1
-        h = []
         for i in range(4):
-            m = mx((ps(b + i, 128), T.wq[:, 128 * i:128 * i + 128], T.wqs[:, 128 * i:128 * i + 128], T[xc][:, lo:lo + 128], T[xc + "s"][:, lo:lo + 128], True, True), wq, *(tuple(toks) + tuple(free)))
-            out = T.hb[:, hlo + i:hlo + 512:4]
-            h.append(act((out, ps(b + i, 128), F.Relu, 0.0, 0.0625), m) if i % 2 == 0 else v("ts", (out, ps(b + i, 128), 0.0, 0.0625, A.max, A.mult), m))
-        return b, v("q", (T[hc][:, hto:hto + hn], T[hc + "s"][:, hto:hto + hn], T.hb[:, hlo:hlo + 4 * hn]), *h)
+            mx(ps(b + i, 128), o("wq", 128 * i, 128 * i + 128), o("wqs", 128 * i, 128 * i + 128), o(xc, lo, lo + 128), o(xc + "s", lo, lo + 128), True, True)
+            out = o("hb", hlo + i, hlo + 512, 4)
+            if i % 2 == 0:
+                act(out, ps(b + i, 128), F.Relu, 0.0, 0.0625)
+            else:
+                v("ts", out, ps(b + i, 128), 0.0, 0.0625, A.max, A.mult)
+        v("q", o(hc, hto, hto + hn), o(hc + "s", hto, hto + hn), o("hb", hlo, hlo + 4 * hn))
+        return b
 
-    b0, h0 = chunk("xs", 128 * me, xtok[me], 0, 144, "zq", 0, ())
-    uq = v("q", (T.uq[:, :], T.uqs[:, :], T.ut[:, :]), du, zu)
-    ur = pick("ur", 0, 128, "uq", 0, 128, T.ul[:, 0:8], uq)
-    g0 = v("set", (T.gt[:, :], -9e29))
-    m = mx((ps(b0, 128), T.ur[:, :], T.urs[:, :], T.zq[:, 0:128], T.zqs[:, 0:128], True, True), h0, *ur)
-    own = v("copy", (T.gt[:, 0:128], ps(b0, 128)), m, g0)
+    b = chunk("xs", 128 * me, 0, 144, "zq", 0)
+    g0 = v("set", o("gt"), -9e29)
+    mx(ps(b, 128), o("ur"), o("urs"), o("zq", 0, 128), o("zqs", 0, 128), True, True)
+    act(o("gt", 0, 128), ps(b, 128), F.Copy)
 
     rel = [0 if e == me else 128 + 128 * others.index(e) for e in range(4)]
     for e in range(4):
-        c = v("set", (T.kr[:, e:64:4], float(rel[e] - 1 - 512)))
-    v("ts", (T.tk[:, :], T.tp[:, 3:256:4], 128.5, None, A.is_lt))
-    k7 = v("ts", (T.kv[:, :], T.kv[:, :], f(13), None, A.subtract), p3)
-    c = v("tt", (T.v2[:, :], T.tp[:, 3:256:4], T.kr[:, :], A.add), c)
-    v("tt", (T.abe[:, 0:64], T.mab[:, 0:64], T.tk[:, :], A.mult), c)
-    a = v("tt", (T.abe[:, 64:128], T.mab[:, 64:128], T.tk[:, :], A.mult))
-    v("ts", (T.kv2[:, :], T.kv[:, :], 0.0, None, A.is_ge), k7)
-    c = v("ts", (T.kv[:, :], T.kv[:, :], 13.5, None, A.is_lt))
-    v("tt", (T.pab2[:, 0:64], T.abe[:, 0:64], T.v2[:, :], A.mult), a)
-    a = v("tt", (T.pab2[:, 64:128], T.abe[:, 64:128], T.v2[:, :], A.mult))
-    c = v("tt", (T.kv2[:, :], T.kv2[:, :], T.kv[:, :], A.mult), c)
-    a = v("scan", (T.t2[:, :], T.rst[:, 0:128], T.pab2[:, :], 0.0, A.mult, A.add), a)
-    v("tt", (T.ae[:, :], T.abe[:, 0:64], T.kv2[:, :], A.mult), c)
-    c = v("tt", (T.be[:, :], T.abe[:, 64:128], T.kv2[:, :], A.mult))
-    o3 = v("ts", (T.off3[:, :], T.t2[:, 3:128:4], 512.0, None, A.add), a)
-    v("tt", (T.de[:, :], T.ae[:, :], T.be[:, :], A.subtract), c)
+        v("set", o("kr", e, 64, 4), float(rel[e] - 1 - 512))
+    v("ts", o("tk"), role("tp"), 128.5, None, A.is_lt)
+    v("tt", o("v2"), role("tp"), o("kr"), A.add)
+    v("tt", o("abe", 0, 64), o("mab", 0, 64), o("tk"), A.mult)
+    v("tt", o("abe", 64, 128), o("mab", 64, 128), o("tk"), A.mult)
+    v("tt", o("pab2", 0, 64), o("abe", 0, 64), o("v2"), A.mult)
+    v("tt", o("pab2", 64, 128), o("abe", 64, 128), o("v2"), A.mult)
+    v("scan", o("t2"), o("rst", 0, 128), o("pab2"), 0.0, A.mult, A.add)
+    v("ts", o("off3"), o("t2", 3, 128, 4), 512.0, None, A.add)
+    v("ts", o("kv2"), o("kv"), f(13), None, A.subtract)
+    v("ts", o("kv"), o("kv2"), 0.0, None, A.is_ge)
+    v("ts", o("kv3"), o("kv2"), 13.5, None, A.is_lt)
+    v("tt", o("kv2"), o("kv"), o("kv3"), A.mult)
+    v("tt", o("ae"), o("abe", 0, 64), o("kv2"), A.mult)
+    v("tt", o("be"), o("abe", 64, 128), o("kv2"), A.mult)
+    v("tt", o("de"), o("ae"), o("be"), A.subtract)
+    v("set", o("m2"), 0.0)
+    v("set", o("wa", 240, 256), 0.0)
+    v("ts", o("k3"), o("k3"), f(20), f(0), A.add, A.subtract)
+    v("ts", o("tr"), o("tr"), f(0), None, A.add)
+    v("set", o("l3"), 1.0)
 
-    bank = {b0: (own,)}
-    hq = {}
-    for s in order:
+    asked = []
+    for n, s in enumerate(order):
         i = others.index(s)
-        n = 2 * len(topo.engines(T.cores[s], core))
-        total["xa%d" % i] = n
-        b = 4 * (sets[0] % 2)
-        b, h = chunk("xl", 128 * i, (("xa%d" % i, n),), 576 + 512 * i, 128, "hq", 128 * i, bank.get(b, ()))
-        hq[s] = h
-        m = mx((ps(b, 128), T.hq[:, 128 * i:128 * i + 128], T.hqs[:, 128 * i:128 * i + 128], T.uq[:, :], T.uqs[:, :], True, True), h)
-        c = act((T.qs[:, i:i + 1], ps(b, 1), F.Copy), m)
-        bank[b] = (c, h)
-        k = place(me, s)
-        send(s, T.dg[128 * k:128 * k + 128, :], T.qs[:, i:i + 1], "qa", c)
+        arrive("xa%d" % i, [s], 2, [o("xl", 128 * i, 128 * i + 128), o("xls", 128 * i, 128 * i + 128)], 2.4, sent[2 * n:2 * n + 2])
+        b = chunk("xl", 128 * i, 576 + 512 * i, 128, "hq", 128 * i)
+        mx(ps(b, 128), o("hq", 128 * i, 128 * i + 128), o("hqs", 128 * i, 128 * i + 128), o("uq"), o("uqs"), True, True)
+        act(o("qs", i, i + 1), ps(b, 1), F.Copy)
+        k, c = place(me, s), T.cores[s]
+        rid, pid, _ = topo.addr(c)
+        total["sent"] += len(topo.engines(core, c))
+        asked.append(add("p", lambda i=i, k=k, c=c, rid=rid, pid=pid: g.remote_dma(T.dg[128 * k:128 * k + 128, :], T.qs[:, i:i + 1], T.sem.qa, T.sem.sent, pid, rid, topo.mask(core, c)),
+                         [], [o("qs", i, i + 1)], 0.25))
 
-    v("ts", (T.k3[:, :], T.k3[:, :], f(20), f(0), A.add, A.subtract), p4)
-    v("ts", (T.tr[:, :], T.tr[:, :], f(0), None, A.add), p5)
-    v("set", (T.l3[:, :], 1.0))
-    v("set", (T.ll[:, :], 1.0))
-    v("set", (T.wnw[:, :], 0.0))
-    for e in range(4):
-        v("set", (T.kz[:, e:64:4], float(-1 - 128 if e == me else 144 + 48 * others.index(e) - 1 - 128)))
-    vq = v("q", (T.vq[:, :], T.vqs[:, :], T.vt[:, :]), dv)
-
-    qa = ("qa", sum(len(topo.engines(T.cores[s], core)) for s in others))
+    arrive("qa", others, 1, [o("dg")], 1.7, asked)
     for k in range(8):
-        gd = dma("y" if k % 2 == 0 else "s", T.gt[16 * k:16 * k + 1, 128:512], T.dg[:, :], "dgt", qa, own)
-    a = v("copy", (T.gab[:, 0:240], T.gt[:, 0:520].indirect(T.off3[:, 16:31])), gd, vq)
-    a = v("tt", (T.wa[:, 0:240], T.gt[:, 0:520].indirect(T.off3[:, 0:15]), T.gab[:, 0:240], A.is_ge), a)
-    a = v("tr", (T.wat[:, :], T.wa[:, :]), a)
+        dma("y" if k % 2 == 0 else "s", "dgt", lambda k=k: T.gt[16 * k:16 * k + 1, 128:512], lambda: T.dg[:, :],
+            [o("gt", 128 + 48 * k, 176 + 48 * k)], [o("dg")], (g0,))
+    act(o("gab", 0, 128), _ind(o("gt"), o("off3", 16, 24)), F.Copy)
+    v("copy", o("gab", 128, 240), _ind(o("gt"), o("off3", 24, 31)))
+    v("tt", o("wa", 0, 128), _ind(o("gt"), o("off3", 0, 8)), o("gab", 0, 128), A.is_ge)
+    v("tt", o("wa", 128, 240), _ind(o("gt"), o("off3", 8, 15)), o("gab", 128, 240), A.is_ge)
+    quarter = lambda t, h: o(t, 3 + 128 * h, 128 + 128 * h, 4)
+    for s in H:
+        v("tr", o("wat", *s), o("wa", *s))
     for e in range(4):
-        b = v("tt", (T.x4[:, e:64:4], T.wat[:, 0:256:16], T.de[:, e:64:4], A.mult), a)
-    w4 = T.m2[:, 3:256:4]
-    a = v("tt", (w4, T.x4[:, :], T.be[:, :], A.add), b)
-    a = v("tr", (T.n2[:, :], T.m2[:, :]), a)
-    a = v("scan", (T.rc[:, :], T.one[:, :], T.n2[:, :], 0.0, A.mult, A.add), a)
-    a = v("tr", (T.rtr[:, :], T.rc[:, :]), a)
-    r4 = T.rtr[:, 3:256:4]
-    a = v("tt", (T.s1[:, :], r4, T.k3[:, :], A.add), a)
-    a = v("tt", (T.s2[:, :], T.s1[:, :], w4, A.mult), a)
-    a = v("scan", (T.s3[:, :], T.rst[:, 0:64], T.s2[:, :], 0.0, A.mult, A.add), a)
-    a = v("tt", (T.s5[:, :], T.s3[:, 3:64:4], T.tr[:, :], A.add), a)
-    a = v("copy", (T.off4[:, :], T.s5[:, :]), a)
-    a = v("copy", (T.l3[:, 0:912].indirect(T.off4[:, 0:15]), T.pp[:, 0:240]), a)
+        v("tt", o("x4", e, 64, 4), o("wat", 0, 256, 16), o("de", e, 64, 4), A.mult)
+    for h, s in enumerate(H):
+        v("tt", quarter("m2", h), o("x4", *W[h]), o("be", *W[h]), A.add)
+        v("tr", o("n2", *s), o("m2", *s))
+        v("scan", o("rc", *s), o("one", *s), o("n2", *s), o("rc", 127, 128) if h else 0.0, A.mult, A.add)
+        v("tr", o("rtr", *s), o("rc", *s))
+        v("tt", o("s1", *W[h]), quarter("rtr", h), o("k3", *W[h]), A.add)
+        v("tt", o("s2", *W[h]), o("s1", *W[h]), quarter("m2", h), A.mult)
+    v("scan", o("s3"), o("rst", 0, 64), o("s2"), 0.0, A.mult, A.add)
+    v("tt", o("s5"), o("s3", 3, 64, 4), o("tr"), A.add)
+    v("copy", o("off4"), o("s5"))
+    v("copy", _ind(o("l3"), o("off4", 0, 15)), o("pp", 0, 240))
     for e in range(4):
-        b = v("tr", (T.l3t[:, 64 * e:64 * e + 64], T.l3[:, 160 * e:160 * e + 64]), a)
-    v("ts", (T.l3n[:, :], T.l3t[:, :], f(13), None, A.mult), b)
-    b = v("ts", (T.l3p[:, :], T.l3t[:, :], f(3), None, A.mult))
-    at = lambda t, x: t[:, x:x + 205:68]
-    v("tt", (T.ll[:, 0:16:4], at(T.l3n, 3), at(T.l3p, 19), A.add), b)
-    v("tt", (T.ll[:, 1:16:4], at(T.l3n, 51), at(T.l3p, 3), A.add))
-    a = v("tt", (T.ll[:, 2:16:4], at(T.l3n, 35), at(T.l3p, 51), A.add))
-    a = v("ts", (T.ls[:, :], T.ll[:, :], -1.0, None, A.add), a)
+        v("tr", o("l3t", 64 * e, 64 * e + 64), o("l3", 160 * e, 160 * e + 64))
+    for s in H:
+        v("ts", o("l3n", *s), o("l3t", *s), f(13), None, A.mult)
+        v("ts", o("l3p", *s), o("l3t", *s), f(3), None, A.mult)
+    at = lambda t, x: o(t, x, x + 205, 68)
+    v("tt", o("ll", 0, 4), at("l3n", 3), at("l3p", 19), A.add)
+    v("tt", o("ll", 4, 8), at("l3n", 51), at("l3p", 3), A.add)
+    v("tt", o("ll", 8, 12), at("l3n", 35), at("l3p", 51), A.add)
+    told = []
     for e in order:
+        v("ts", o("ls", 4 * e, 4 * e + 3), o("ll", e, 12, 4), -1.0, None, A.add)
         i = place(me, e)
-        send(e, T.la[:, 4 * i:4 * i + 3], T.ls[:, 4 * e:4 * e + 3], "ar%d" % i, a)
+        told.append(send(e, o("la", 4 * i, 4 * i + 3), o("ls", 4 * e, 4 * e + 3), "ar%d" % i))
 
-    v("ts", (T.h1[:, :], r4, 48.5, None, A.is_lt))
-    a = v("copy", (T.xz[:, :], r4))
-    c = v("tt", (T.w1[:, :], w4, T.ka[:, :], A.mult), p6)
-    a = v("copy", (T.xz[:, me:64:4], T.tp[:, 4 * me + 3:256:16]), a)
-    b = v("tt", (T.hm[:, :], w4, T.h1[:, :], A.mult), c)
-    a = v("tt", (T.z1[:, :], T.xz[:, :], T.kz[:, :], A.add), a)
-    c = v("tt", (T.w2[:, :], T.hm[:, :], T.kb[:, :], A.mult), b, p7)
-    a = v("tt", (T.z2[:, :], T.z1[:, :], T.hm[:, :], A.mult), a, b)
-    c = v("tt", (T.w3[:, :], T.w2[:, :], T.w1[:, :], A.add), c)
-    a = v("scan", (T.z3[:, :], T.rst[:, 0:64], T.z2[:, :], 0.0, A.mult, A.add), a)
-    c = v("scan", (T.w4[:, :], T.rst[:, 0:64], T.w3[:, :], 0.0, A.mult, A.add), c)
-    v("ts", (T.zn[:, :], T.z3[:, 3:64:4], f(13), None, A.mult), a)
-    a = v("ts", (T.zp[:, :], T.z3[:, 3:64:4], f(3), None, A.mult))
-    c = v("ts", (T.wnw[:, 0:256:16], T.w4[:, 3:64:4], -100.0, None, A.add), c)
-    a = v("tt", (T.zl[:, :], T.zn[:, 1:15], T.zp[:, 0:14], A.add), a)
-    c = v("tr", (T.wnf[:, :], T.wnw[:, :]), c)
-    zo = v("ts", (T.off5[:, :], T.zl[:, :], 128.0, None, A.add), a)
-    dma("y", T.wn[:, :], T.wnf[16:17, 0:224], "out", c)
+    for e in range(4):
+        v("set", o("kz", e, 64, 4), float(-1 - 128 if e == me else 144 + 48 * others.index(e) - 1 - 128))
+    v("set", o("wnw"), 0.0)
+    v("q", o("vq"), o("vqs"), o("vt"))
+    v("ts", o("h1"), role("rtr"), 48.5, None, A.is_lt)
+    v("copy", o("xz"), role("rtr"))
+    v("copy", o("xz", me, 64, 4), o("tp", 4 * me + 3, 256, 16))
+    v("tt", o("hm"), role("m2"), o("h1"), A.mult)
+    v("tt", o("z1"), o("xz"), o("kz"), A.add)
+    v("tt", o("z2"), o("z1"), o("hm"), A.mult)
+    v("scan", o("z3"), o("rst", 0, 64), o("z2"), 0.0, A.mult, A.add)
+    v("ts", o("zn"), o("z3", 3, 64, 4), f(13), None, A.mult)
+    v("ts", o("zp"), o("z3", 3, 64, 4), f(3), None, A.mult)
+    v("tt", o("zl"), o("zn", 1, 15), o("zp", 0, 14), A.add)
+    v("ts", o("off5"), o("zl"), 128.0, None, A.add)
+    v("tt", o("w1"), role("m2"), o("ka"), A.mult)
+    v("tt", o("w2"), o("hm"), o("kb"), A.mult)
+    v("tt", o("w3"), o("w2"), o("w1"), A.add)
+    v("scan", o("w4"), o("rst", 0, 64), o("w3"), 0.0, A.mult, A.add)
+    v("ts", o("wnw", 0, 256, 16), o("w4", 3, 64, 4), -100.0, None, A.add)
+    v("tr", o("wnf"), o("wnw"))
+    dma("y", "out", lambda: T.wn[:, :], lambda: T.wnf[16:17, 0:224], [], [o("wnf")])
 
-    for s in order:
+    came = []
+    for n, s in enumerate(order):
         i = others.index(s)
-        n = len(topo.engines(T.cores[s], core))
-        total["ar%d" % i] = n
-        x, y = pick("hs", 48 * i, 48 * i + 48, "hq", 128 * i, 128 * i + 128, T.la[:, 4 * i:4 * i + 3], hq[s], ("ar%d" % i, n))
+        arrive("ar%d" % i, [s], 1, [o("la", 4 * i, 4 * i + 3)], 1.7, told[n:n + 1])
+        pick("hs", 48 * i, 48 * i + 48, "hq", 128 * i, 128 * i + 128, o("la", 4 * i, 4 * i + 3))
         k = 144 + 48 * place(me, s)
-        send(s, codes(T.zq, k, k + 48), codes(T.hs, 48 * i, 48 * i + 48), "ha", x)
-        send(s, T.zqs[:, k:k + 48], T.hss[:, 48 * i:48 * i + 48], "ha", y)
+        came.append(send(s, _cast(o("zq", k, k + 48), "u8"), _cast(o("hs", 48 * i, 48 * i + 48), "u8"), "ha"))
+        came.append(send(s, o("zqs", k, k + 48), o("hss", 48 * i, 48 * i + 48), "ha"))
 
-    ha = ("ha", 2 * qa[1])
-    x, y = pick("z", 0, 224, "zq", 0, 288, T.off5[:, 0:14], ha, zo, h0)
-    m = mx((ps(0, 224), T.vq[:, :], T.vqs[:, :], T.z[:, :], T.zs[:, :], True, True), x, y, vq)
-    yc = v("copy", (T.ysb[:, :], ps(0, 224)), m)
-    dma("y", T.oc[:, :], codes(T.z, 0, 224), "out", x)
+    arrive("ha", others, 2, [o("zq", 144, 288), o("zqs", 144, 288)], 2.0, came)
+    pick("z", 0, 128, "zq", 0, 288, o("off5", 0, 8))
+    pick("z", 128, 224, "zq", 0, 288, o("off5", 8, 14))
+    mx(ps(0, 128), o("vq"), o("vqs"), o("z", 0, 128), o("zs", 0, 128), True, True)
+    mx(ps(1, 128), o("vq"), o("vqs"), o("z", 96, 224), o("zs", 96, 224), True, True)
+    v("copy", o("ysb", 0, 128), ps(0, 128))
+    v("copy", o("ysb", 128, 224), o("ps", 544, 640))
+    dma("y", "out", lambda: T.oc[:, :], lambda: T.z[:, 0:224].bitcast(dt.uint8), [], [o("z")])
     for k in range(4):
-        dma("s" if k % 2 == 0 else "y", T.osc[4 * k:4 * k + 4, :], T.zs[32 * k:32 * k + 4, :], "out", y)
-    dma("y", T.y[:, :], T.ysb[:, :], "out", yc)
-    total["qa"], total["ha"] = qa[1], ha[1]
-    for s, n in list(total.items()) + list(count.items()):
-        wait("p", (s, n))
+        dma("s" if k % 2 == 0 else "y", "out", lambda k=k: T.osc[4 * k:4 * k + 4, :], lambda k=k: T.zs[32 * k:32 * k + 4, :], [], [o("zs")])
+    dma("y", "out", lambda: T.y[:, :], lambda: T.ysb[:, :], [], [o("ysb")])
+
+    queue = {"v": V, "s": g.scalar, "t": g.tensor, "p": g, "y": g.sync}
+    lists = _order(ops)
+    mark = {}
+    for q, items in lists.items():
+        n = 0
+        for i in items:
+            if ops[i]["sem"] == "own":
+                n += 1
+                mark[i] = (q, n)
+        total[q] = n
+    for i, x in enumerate(ops):
+        if x["sem"] and x["sem"] != "own":
+            mark[i] = (x["sem"], total[x["sem"]])
+    seen = {}
+    for q, items in lists.items():
+        for i in items:
+            best = {}
+            for d in ops[i]["deps"]:
+                if d in mark and not (q == "t" and ops[d]["q"] == "t"):
+                    s, n = mark[d]
+                    best[s] = max(n, best.get(s, 0))
+            for s, n in sorted(best.items()):
+                if seen.get((q, s), 0) < n:
+                    queue[q].wait_ge(T.sem[s], n)
+                    seen[(q, s)] = n
+            call = ops[i]["fn"]()
+            if ops[i]["sem"]:
+                call.then_inc(T.sem[mark[i][0]], 1 if ops[i]["sem"] == "own" else 16)
+    for s, n in sorted(total.items()):
+        if n and seen.get(("p", s), 0) < n:
+            g.wait_ge(T.sem[s], n)

@@ -4,20 +4,22 @@ from concourse.mybir import dt, AluOpType as A, ActivationFunctionType as F
 def _buffers():
     d = {"dg": ("dram", [384, 1], "float32"), "ps": ("psum", [128, 4096], "float32")}
     kinds = {
-        "bfloat16": "xt 1088 rtt 512 wt 2048 ut 512 vt 512 hb 2112 rst 256 one 256 tok 512 a1 256 a2 256 cc 256 mm 256 nn 256 "
-                    "pp 256 tp 256 el 1088 lt 640 wa 256 wat 256 m2 256 n2 256 rc 256 rtr 256 l3 912 l3t 256 l3n 256 l3p 256",
-        "float32": "ysb 224 sf 32 zero 8 tokf 512 k1 64 k3 64 ka 64 kb 64 kz 64 kr 64 kv 64 kv2 64 kv3 64 tr 16 mab 128 vv 64 pab 128 "
-                   "t1 128 xn 40 xp 40 wl 40 xn1 10 xp1 10 wl1 10 tk 64 abe 128 v2 64 pab2 128 t2 128 ae 64 be 64 de 64 qs 4 "
-                   "gt 520 gab 256 x4 64 s1 64 s2 64 s3 64 s5 16 ll 16 h1 64 hm 64 xz 64 z1 64 z2 64 z3 64 zn 16 zp 16 zl 14 "
-                   "w1 64 w2 64 w3 64 w4 64 wnw 256 wnf 256",
-        "uint16": "sl 18 ul 8 off1 32 off2 40 off2a 10 off3 32 off4 16 off5 14 ls 16 la 12",
+        "bfloat16": "xt 1088 rtt 528 wt 2048 ut 512 vt 512 hb 2112 rst 256 one 256 tok 480 a1 256 a2 256 cc 256 mm 256 nn 256 "
+                    "pp 256 tp 256 el 1088 lt 640 wa 256 wat 256 m2 256 n2 256 rc 256 rtr 256 "
+                    "tabw 512 tab 576 bt 1152 sc 1152 rsl 384",
+        "float32": "ysb 224 sf 32 zero 8 tokf 480 k1 60 ka 64 kb 64 kz 64 kr 64 kv 64 kv2 64 kv3 64 mab 128 vv 60 pab 120 "
+                   "t1 120 xn 40 xp 40 wl 40 xn1 10 xp1 10 wl1 10 tk 64 abe 128 v2 64 pab2 128 t2 128 ae 64 be 64 de 64 qs 4 "
+                   "gt 528 gab 256 x4 64 qo 128 own 128 gab2 256 isa 256 lab 256 lab2 320 lt1 256 lt0 256 h1 64 hm 64 xz 64 "
+                   "z1 64 z2 64 z3 64 zn 16 zp 16 zl 14 w1 64 w2 64 w3 64 w4 64 wnw 256 wnf 256",
+        "uint16": "sl 20 ul 8 off1 30 off2 40 off2a 10 off3 32 offl 24 off5 14 ls 16 la 12",
         "int32": "si 8",
     }
     for t, text in kinds.items():
         w = text.split()
         for name, n in zip(w[::2], w[1::2]):
             d[name] = ("sbuf", [128, int(n)], t)
-    w = "xq 272 rq 128 rr 288 wq 512 uq 128 ur 128 vq 128 xs 512 xl 384 hq 384 hs 144 zq 288 z 224".split()
+    d["cb"] = d.pop("one")[:1] + ([128, 640], "bfloat16")
+    w = "xq 272 rq 128 rqn 128 rr 288 wq 512 uq 128 ur 128 vq 128 xs 512 xl 384 hq 384 hs 144 zq 288 z 224".split()
     for name, n in zip(w[::2], w[1::2]):
         d[name] = ("sbuf", [128, int(n)], "float8_e4m3fn_x4")
         d[name + "s"] = ("sbuf", [128, int(n)], "uint8")
@@ -25,31 +27,36 @@ def _buffers():
 
 
 SCRATCH = _buffers()
-SEMAPHORES = ["v", "s", "t", "p", "dx", "dr", "dw", "du", "dv", "dgt", "out", "sent", "qa", "ha"] \
+SEMAPHORES = ["v", "s", "t", "p", "dx", "dx2", "dr", "dw", "du", "dv", "dgt", "out", "sent", "qa", "ha"] \
     + ["xa%d" % i for i in range(3)] + ["ar%d" % i for i in range(3)]
 WAKE, CYC = 0.12, 0.00083
 
 
 def _o(name, a=0, z=None, step=1):
-    return ("@", name, a, SCRATCH[name][1][1] if z is None else z, step, None, None)
+    return ("@", name, a, SCRATCH[name][1][1] if z is None else z, step, None, None, None)
 
 
 def _cast(o, how):
-    return o[:5] + (how, o[6])
+    return o[:5] + (how,) + o[6:]
 
 
 def _ind(o, off):
-    return o[:6] + (off,)
+    return o[:6] + (off, o[7])
+
+
+def _part(o, p, n=32):
+    return o[:7] + ((p, p + n),)
 
 
 def _keys(o):
     if o[1] == "ps":
         return [("ps", b) for b in range(o[2] // 512, (o[3] - 1) // 512 + 1)]
-    return [(o[1], c) for c in range(o[2], o[3], o[4])]
+    blocks = range(o[7][0] // 32, (o[7][1] - 1) // 32 + 1) if o[7] else range(4)
+    return [(o[1], c, b) for c in range(o[2], o[3], o[4]) for b in blocks]
 
 
 def _isop(x):
-    return isinstance(x, tuple) and len(x) == 7 and x[0] == "@"
+    return isinstance(x, tuple) and len(x) == 8 and x[0] == "@"
 
 
 def _width(o):
@@ -63,6 +70,8 @@ def _cost(name, args):
     if name == "q":
         return .012 + .00088 * n
     ops = [a for a in args if _isop(a)]
+    if name == "pb":
+        return .14 + 4 * n * CYC
     if name == "iota":
         return .13 + 2 * n * CYC
     if name == "act":
@@ -149,7 +158,8 @@ def rank_program(g, core, T, topo):
     kinds = {"u8": dt.uint8, "u32": dt.uint32}
 
     def mat(o):
-        x = T[o[1]][:, o[2]:o[3]] if o[4] == 1 else T[o[1]][:, o[2]:o[3]:o[4]]
+        p, z = o[7] or (0, SCRATCH[o[1]][1][0])
+        x = T[o[1]][p:z, o[2]:o[3]] if o[4] == 1 else T[o[1]][p:z, o[2]:o[3]:o[4]]
         if o[5]:
             x = x.bitcast(kinds[o[5]])
         return x.indirect(mat(o[6])) if o[6] else x
@@ -178,14 +188,14 @@ def rank_program(g, core, T, topo):
     V = g.vector
     calls = {"copy": V.tensor_copy, "tt": V.tensor_tensor, "ts": V.tensor_scalar, "set": V.memset, "tr": V.transpose,
              "scan": V.tensor_tensor_scan, "q": V.quantize_mx, "act": g.scalar.activation, "mx": g.tensor.matmul_mx,
-             "iota": lambda *a: g.iota(*a, allow_small_or_imprecise_dtypes=True), "iota32": g.iota}
+             "iota": lambda *a: g.iota(*a, allow_small_or_imprecise_dtypes=True), "iota32": g.iota, "pb": g.partition_broadcast}
 
-    def do(q, name, args):
+    def do(q, name, args, extra=()):
         k = 2 if name == "q" else 1
         fn = lambda: calls[name](*[mat(a) if _isop(a) else a for a in args])
-        return add(q, fn, args[:k], [a for a in args[k:] if _isop(a)], _cost(name.replace("32", ""), args), 0.0, "own")
+        return add(q, fn, args[:k], [a for a in args[k:] if _isop(a)], _cost(name.replace("32", ""), args), 0.0, "own", extra)
 
-    v = lambda name, *args: do("v", name, args)
+    v = lambda name, *args, extra=(): do("v", name, args, extra)
     act = lambda *args: do("s", "act", args)
     mx = lambda *args: do("t", "mx", args)
     iota = lambda *args: do("p", "iota", args)
@@ -213,24 +223,23 @@ def rank_program(g, core, T, topo):
     f = lambda k: _o("sf", k, k + 1)
     role = lambda b: _o(b, 3, 256, 4)
     ps = lambda b, n: _o("ps", 512 * b, 512 * b + n)
+    ones = lambda a, z: _o("cb", 384 + a, 384 + z)
 
     dma("s", "dr", lambda: T.rtt[:, 0:16], lambda: T.rt[:, 0:16], [o("rtt", 0, 16)], [])
-    dx = dma("y", "dx", lambda: T.xt[:, 64:960], lambda: T.x[:, :], [o("xt", 64, 960)], [], (), 3.0)
+    dma("y", "dx", lambda: T.xt[:, 64:576], lambda: T.x[:, 0:512], [o("xt", 64, 576)], [], (), 2.6)
+    dx = dma("y", "dx2", lambda: T.xt[:, 576:960], lambda: T.x[:, 512:896], [o("xt", 576, 960)], [], (), 3.0)
     dma("y", "dw", lambda: T.wt[:, :], lambda: T.w[:, :], [o("wt")], [], (dx,), 4.5)
     dma("y", "du", lambda: T.ut[:, 0:8], lambda: T.u[:, 0:8], [o("ut", 0, 8)], [], (dx,), 4.8)
     dma("y", "dv", lambda: T.vt[:, :], lambda: T.v[:, :], [o("vt")], [], (dx,), 5.0)
 
     do("p", "iota32", (o("si", 0, 1), [[0, 1]], 0, 1))
-    for k in (0, 256):
+    for k in (0, 240):
         iota(o("tokf", k, k + 240), [[1, 240]], 0, 0)
-        iota(o("tokf", k + 240, k + 256), [[0, 16]], 240, 0)
-    iota(o("k1"), [[0, 16], [256, 4]], 0, 0)
+    iota(o("k1"), [[0, 15], [256, 4]], 0, 0)
     iota(o("kv"), [[1, 16], [0, 4]], 0, 0)
-    iota(o("k3"), [[-16, 16], [160, 4]], -657, 0)
-    iota(o("tr"), [[16, 16]], 656, 0)
     iota(o("ka"), [[0, 16], [-1, 4]], 99, 0)
     iota(o("kb"), [[0, 16], [2, 4]], 1, 0)
-    v("set", o("rtt", 32, 512), 0.0)
+    v("set", o("rtt", 16, 512), 0.0)
     v("set", o("zero"), 0.0)
     v("set", o("sl"), 8)
     v("set", o("ul"), 0)
@@ -238,7 +247,7 @@ def rank_program(g, core, T, topo):
     v("set", o("xt", 960, 1088), 0.0)
     v("set", o("rst"), 1.0)
     v("set", o("rst", 0, 256, 4), 0.0)
-    v("set", o("one"), 1.0)
+    v("set", ones(0, 256), 1.0)
     v("set", o("el"), 0.0)
     v("ts", o("si", 1, 2), o("si", 0, 1), 15, None, A.bitwise_and)
     v("ts", o("si", 2, 3), o("si", 0, 1), 15, 2, A.bitwise_and, A.logical_shift_right)
@@ -247,13 +256,13 @@ def rank_program(g, core, T, topo):
     v("copy", o("sf", 0, 4), o("si", 1, 5))
     v("ts", f(4), f(2), f(1), None, A.is_lt)
     v("ts", f(5), f(2), 3.0, None, A.is_lt)
-    v("ts", f(6), f(1), -4.0, None, A.add)
+    v("ts", f(6), f(1), 116.0, None, A.add)
     v("ts", f(7), f(2), -7.0, None, A.add)
     v("tt", f(8), f(7), f(4), A.subtract)
     v("tt", f(9), f(6), f(5), A.mult)
     v("tt", f(10), f(8), f(5), A.mult)
     v("ts", o("sl", 0, 9, 2), o("zero", 0, 5), f(10), 8.0, A.add, A.add)
-    v("ts", o("sl", 9, 18, 2), o("zero", 0, 5), f(9), 8.0, A.add, A.add)
+    v("ts", o("sl", 10, 19, 2), o("zero", 0, 5), f(9), 8.0, A.add, A.add)
     v("ts", f(13), f(3), -1.0, 1.0, A.mult, A.add)
     v("ts", f(20), f(3), 16.0, None, A.mult)
     v("ts", f(15), f(1), 2.0, -16.0, A.is_lt, A.mult)
@@ -265,9 +274,11 @@ def rank_program(g, core, T, topo):
     v("ts", f(18), f(3), 16.0, 31.0, A.mult, A.add)
     act(o("tok"), o("tokf"), F.Identity, f(20))
 
-    v("ts", o("rtt", 16, 32), o("rtt", 0, 16), -1.0, None, A.mult)
-    v("q", o("rq"), o("rqs"), o("rtt"))
-    pick("rr", 0, 288, "rq", 0, 128, o("sl"))
+    v("ts", o("rtt", 512, 528), o("rtt", 0, 16), -1.0, None, A.mult)
+    v("q", o("rq"), o("rqs"), o("rtt", 0, 512))
+    v("q", o("rqn"), o("rqns"), o("rtt", 16, 528))
+    pick("rr", 0, 144, "rq", 0, 128, o("sl", 0, 9))
+    pick("rr", 144, 288, "rqn", 0, 128, o("sl", 10, 19))
     for h, (x0, x1) in enumerate([(0, 144), (144, 272)]):
         v("q", o("xq", x0, x1), o("xqs", x0, x1), o("xt", 4 * x0, 4 * x1))
         for j, (lo, sh) in enumerate([(0, 0), (16, 16), (144, 0), (160, 16)]):
@@ -280,15 +291,15 @@ def rank_program(g, core, T, topo):
         v("scan", o("cc", *s), o("rst", *s), o("a2", *s), 0.0, A.mult, A.add)
         v("ts", o("mm", *s), o("cc", *s), 1.5, None, A.is_lt)
         v("tr", o("nn", *s), o("mm", *s))
-        v("scan", o("pp", *s), o("one", *s), o("nn", *s), o("pp", 127, 128) if h else f(17), A.mult, A.add)
+        v("scan", o("pp", *s), ones(*s), o("nn", *s), o("pp", 127, 128) if h else f(17), A.mult, A.add)
         v("tr", o("tp", *s), o("pp", *s))
     v("ts", o("mab", 0, 64), role("cc"), 0.0, None, A.is_equal)
     v("ts", o("mab", 64, 128), role("cc"), 1.0, None, A.is_equal)
-    v("tt", o("vv"), role("tp"), o("k1"), A.add)
-    v("tt", o("pab", 0, 64), o("mab", 0, 64), o("vv"), A.mult)
-    v("tt", o("pab", 64, 128), o("mab", 64, 128), o("vv"), A.mult)
-    v("scan", o("t1"), o("rst", 0, 128), o("pab"), 0.0, A.mult, A.add)
-    v("ts", o("off1"), o("t1", 3, 128, 4), f(18), None, A.add)
+    v("tt", o("vv"), o("tp", 3, 240, 4), o("k1"), A.add)
+    v("tt", o("pab", 0, 60), o("mab", 0, 60), o("vv"), A.mult)
+    v("tt", o("pab", 60, 120), o("mab", 64, 124), o("vv"), A.mult)
+    v("scan", o("t1"), o("rst", 0, 120), o("pab"), 0.0, A.mult, A.add)
+    v("ts", o("off1"), o("t1", 3, 120, 4), f(18), None, A.add)
     v("copy", _ind(o("el"), o("off1")), o("tok"))
 
     def wrap(x, lo, n):
@@ -338,7 +349,8 @@ def rank_program(g, core, T, topo):
         return b
 
     b = chunk("xs", 128 * me, 0, 144, "zq", 0)
-    g0 = v("set", o("gt"), -9e29)
+    g0 = v("set", o("gt", 0, 520), -9e29)
+    v("set", o("gt", 520, 528), 9e29)
     mx(ps(b, 128), o("ur"), o("urs"), o("zq", 0, 128), o("zqs", 0, 128), True, True)
     act(o("gt", 0, 128), ps(b, 128), F.Copy)
 
@@ -362,30 +374,72 @@ def rank_program(g, core, T, topo):
     v("tt", o("de"), o("ae"), o("be"), A.subtract)
     v("set", o("m2"), 0.0)
     v("set", o("wa", 240, 256), 0.0)
-    v("ts", o("k3"), o("k3"), f(20), f(0), A.add, A.subtract)
-    v("ts", o("tr"), o("tr"), f(0), None, A.add)
-    v("set", o("l3"), 1.0)
+    for k in range(3):
+        v("ts", f(21 + k), f(0), float(16 * k), None, A.add)
+    v("set", o("rsl"), 1.0)
+    v("set", o("rsl", 0, 384, 128), 0.0)
 
     asked = []
     for n, s in enumerate(order):
         i = others.index(s)
         arrive("xa%d" % i, [s], 2, [o("xl", 128 * i, 128 * i + 128), o("xls", 128 * i, 128 * i + 128)], 2.4, sent[2 * n:2 * n + 2])
         b = chunk("xl", 128 * i, 576 + 512 * i, 128, "hq", 128 * i)
-        mx(ps(b, 128), o("hq", 128 * i, 128 * i + 128), o("hqs", 128 * i, 128 * i + 128), o("uq"), o("uqs"), True, True)
-        act(o("qs", i, i + 1), ps(b, 1), F.Copy)
+        mx(ps(b + 3, 128), o("hq", 128 * i, 128 * i + 128), o("hqs", 128 * i, 128 * i + 128), o("uq"), o("uqs"), True, True)
+        act(o("qs", i, i + 1), ps(b + 3, 1), F.Copy)
         k, c = place(me, s), T.cores[s]
         rid, pid, _ = topo.addr(c)
         total["sent"] += len(topo.engines(core, c))
         asked.append(add("p", lambda i=i, k=k, c=c, rid=rid, pid=pid: g.remote_dma(T.dg[128 * k:128 * k + 128, :], T.qs[:, i:i + 1], T.sem.qa, T.sem.sent, pid, rid, topo.mask(core, c)),
                          [], [o("qs", i, i + 1)], 0.25))
 
+    v("set", o("tabw"), 0.0)
+    v("set", o("tab", 256, 288), 0.0)
+    v("set", o("tab", 544, 576), 0.0)
+    v("set", o("lab2"), 0.0)
+    v("set", o("qo"), 0.0)
+    for e in range(4):
+        v("set", _part(f(24), 32 * e), float(rel[e] - 520))
+        v("copy", _part(o("offl", 16, 24), 32 * e), _part(o("off2", 10 * e, 10 * e + 8), 32 * e))
+    act(o("own"), o("tokf", 0, 128), F.Identity, f(24))
+    for k in range(2):
+        v("ts", o("tabw", 256 * k, 256 * k + 256, 16), o("t2", 64 * k + 3, 64 * k + 64, 4), 256.0, None, A.add)
+        v("tr", o("tab", 288 * k, 288 * k + 256), o("tabw", 256 * k, 256 * k + 256))
+        act(o("gab2", 128 * k, 128 * k + 128), _ind(o("tab", 288 * k, 288 * k + 272), o("offl", 16, 24)), F.Identity, -264.0)
+    for k, how in enumerate((A.is_equal, A.not_equal)):
+        s = H[k]
+        v("tt", o("isa", *s), o("gab2", 0, 128), o("own"), how, extra=asked)
+        v("tt", o("lab", *s), o("isa", *s), o("gab2", *H[1 - k]), A.mult)
+        act(o("lab2", 160 * k + 16, 160 * k + 144), o("lab", *s), F.Copy)
+        v("tr", o("lt1", *s), o("lab", *s))
+        v("tr", o("lt0", *s), o("lab2", 160 * k + 32, 160 * k + 160))
+        v("ts", o("offl", 8 * k, 8 * k + 8, 2), o("lt1", s[0], s[1], 32), 520.0, None, A.add)
+        v("ts", o("offl", 8 * k + 1, 8 * k + 8, 2), o("lt0", s[0], s[1], 32), 520.0, None, A.add)
+
     arrive("qa", others, 1, [o("dg")], 1.7, asked)
     for k in range(8):
         dma("y" if k % 2 == 0 else "s", "dgt", lambda k=k: T.gt[16 * k:16 * k + 1, 128:512], lambda: T.dg[:, :],
             [o("gt", 128 + 48 * k, 176 + 48 * k)], [o("dg")], (g0,))
+    for e in others:
+        i = others.index(e)
+        dma("y" if i % 2 == 0 else "s", "dgt", lambda e=e: T.qo[32 * e:32 * e + 1, :], lambda i=i: T.dg[128 * i:128 * i + 128, :],
+            [_part(o("qo"), 32 * e)], [o("dg")])
+    v("tt", o("a1", 0, 128), _ind(o("gt"), o("offl", 0, 8)), o("qo"), A.is_le)
+    v("tt", o("a1", 128, 256), _ind(o("gt"), o("offl", 8, 16)), o("qo"), A.is_lt)
+    counted = v("scan", o("a2", 0, 128), o("a1", 0, 128), o("a1", 128, 256), 0.0, A.add, A.add)
+    told = []
+    for n, e in enumerate(order):
+        s = (128 * n, 128 * n + 128)
+        do("p", "pb", (o("cb", *s), _part(o("a2", 0, 128), 32 * e, 1), 128))
+        for k in range(3):
+            v("ts", o("bt", 384 * n + 128 * k, 384 * n + 128 * k + 128), o("cb", *s), f(21 + k), None, A.is_le)
+        v("scan", o("sc", 384 * n, 384 * n + 384), o("rsl"), o("bt", 384 * n, 384 * n + 384), 0.0, A.mult, A.add)
+        v("ts", o("ls", 4 * e, 4 * e + 3), o("sc", 384 * n + 127, 384 * n + 384, 128), 127.0, None, A.min)
+        i = place(me, e)
+        told.append(send(e, o("la", 4 * i, 4 * i + 3), o("ls", 4 * e, 4 * e + 3), "ar%d" % i))
+
     act(o("gab", 0, 128), _ind(o("gt"), o("off3", 16, 24)), F.Copy)
-    v("copy", o("gab", 128, 240), _ind(o("gt"), o("off3", 24, 31)))
-    v("tt", o("wa", 0, 128), _ind(o("gt"), o("off3", 0, 8)), o("gab", 0, 128), A.is_ge)
+    v("copy", o("gab", 128, 240), _ind(o("gt"), o("off3", 24, 31)), extra=(counted,))
+    v("tt", o("wa", 0, 128), _ind(o("gt"), o("off3", 0, 8)), o("gab", 0, 128), A.is_ge, extra=(counted,))
     v("tt", o("wa", 128, 240), _ind(o("gt"), o("off3", 8, 15)), o("gab", 128, 240), A.is_ge)
     quarter = lambda t, h: o(t, 3 + 128 * h, 128 + 128 * h, 4)
     for s in H:
@@ -395,28 +449,8 @@ def rank_program(g, core, T, topo):
     for h, s in enumerate(H):
         v("tt", quarter("m2", h), o("x4", *W[h]), o("be", *W[h]), A.add)
         v("tr", o("n2", *s), o("m2", *s))
-        v("scan", o("rc", *s), o("one", *s), o("n2", *s), o("rc", 127, 128) if h else 0.0, A.mult, A.add)
+        v("scan", o("rc", *s), ones(*s), o("n2", *s), o("rc", 127, 128) if h else 0.0, A.mult, A.add)
         v("tr", o("rtr", *s), o("rc", *s))
-        v("tt", o("s1", *W[h]), quarter("rtr", h), o("k3", *W[h]), A.add)
-        v("tt", o("s2", *W[h]), o("s1", *W[h]), quarter("m2", h), A.mult)
-    v("scan", o("s3"), o("rst", 0, 64), o("s2"), 0.0, A.mult, A.add)
-    v("tt", o("s5"), o("s3", 3, 64, 4), o("tr"), A.add)
-    v("copy", o("off4"), o("s5"))
-    v("copy", _ind(o("l3"), o("off4", 0, 15)), o("pp", 0, 240))
-    for e in range(4):
-        v("tr", o("l3t", 64 * e, 64 * e + 64), o("l3", 160 * e, 160 * e + 64))
-    for s in H:
-        v("ts", o("l3n", *s), o("l3t", *s), f(13), None, A.mult)
-        v("ts", o("l3p", *s), o("l3t", *s), f(3), None, A.mult)
-    at = lambda t, x: o(t, x, x + 205, 68)
-    v("tt", o("ll", 0, 4), at("l3n", 3), at("l3p", 19), A.add)
-    v("tt", o("ll", 4, 8), at("l3n", 51), at("l3p", 3), A.add)
-    v("tt", o("ll", 8, 12), at("l3n", 35), at("l3p", 51), A.add)
-    told = []
-    for e in order:
-        v("ts", o("ls", 4 * e, 4 * e + 3), o("ll", e, 12, 4), -1.0, None, A.add)
-        i = place(me, e)
-        told.append(send(e, o("la", 4 * i, 4 * i + 3), o("ls", 4 * e, 4 * e + 3), "ar%d" % i))
 
     for e in range(4):
         v("set", o("kz", e, 64, 4), float(-1 - 128 if e == me else 144 + 48 * others.index(e) - 1 - 128))

@@ -4,12 +4,12 @@ from concourse.mybir import dt, AluOpType as A, ActivationFunctionType as F
 def _buffers():
     d = {"dg": ("dram", [384, 1], "float32"), "ps": ("psum", [128, 4096], "float32")}
     kinds = {
-        "bfloat16": "xt 1088 rtt 528 wt 2048 ut 512 vt 512 hb 2112 rst 256 one 256 tok 480 a1 256 a2 256 cc 256 mm 256 nn 256 "
+        "bfloat16": "xt 1088 rtt 512 wt 2048 ut 512 vt 512 hb 2112 rst 256 one 256 tok 480 a1 256 a2 256 cc 256 mm 256 nn 256 "
                     "pp 256 tp 256 el 1088 lt 640 wa 256 wat 256 m2 256 n2 256 rc 256 rtr 256 "
-                    "tabw 512 tab 576 bt 1152 sc 1152 rsl 384",
-        "float32": "ysb 224 sf 32 zero 8 tokf 480 k1 60 ka 64 kb 64 kz 64 kr 64 kv 64 kv2 64 kv3 64 mab 128 vv 60 pab 120 "
+                    "tabw 512 tab 576 vp 64 bt 588 sc 588 rsl 196",
+        "float32": "ysb 224 sf 40 zero 16 tokf 480 kp 60 pe 128 pp2 128 ka 64 kb 64 kz 64 kr 64 kv 64 kv2 64 kv3 64 mab 128 pab 120 "
                    "t1 120 xn 40 xp 40 wl 40 xn1 10 xp1 10 wl1 10 tk 64 abe 128 v2 64 pab2 128 t2 128 ae 64 be 64 de 64 qs 4 "
-                   "gt 528 gab 256 x4 64 qo 128 own 128 gab2 256 isa 256 lab 256 lab2 320 lt1 256 lt0 256 h1 64 hm 64 xz 64 "
+                   "gt 528 gtt 528 gab 256 x4 64 qo 128 own 128 gab2 256 isa 256 lab 256 lab2 320 lt1 256 lt0 256 h1 64 hm 64 xz 64 "
                    "z1 64 z2 64 z3 64 zn 16 zp 16 zl 14 w1 64 w2 64 w3 64 w4 64 wnw 256 wnf 256",
         "uint16": "sl 20 ul 8 off1 30 off2 40 off2a 10 off3 32 offl 24 off5 14 ls 16 la 12",
         "int32": "si 8",
@@ -19,7 +19,7 @@ def _buffers():
         for name, n in zip(w[::2], w[1::2]):
             d[name] = ("sbuf", [128, int(n)], t)
     d["cb"] = d.pop("one")[:1] + ([128, 640], "bfloat16")
-    w = "xq 272 rq 128 rqn 128 rr 288 wq 512 uq 128 ur 128 vq 128 xs 512 xl 384 hq 384 hs 144 zq 288 z 224".split()
+    w = "xq 272 rq 128 rr 288 wq 512 uq 128 ur 128 vq 128 xs 512 xl 384 hq 384 hs 144 zq 288 z 224".split()
     for name, n in zip(w[::2], w[1::2]):
         d[name] = ("sbuf", [128, int(n)], "float8_e4m3fn_x4")
         d[name + "s"] = ("sbuf", [128, int(n)], "uint8")
@@ -27,8 +27,9 @@ def _buffers():
 
 
 SCRATCH = _buffers()
-SEMAPHORES = ["v", "s", "t", "p", "dx", "dx2", "dr", "dw", "du", "dv", "dgt", "out", "sent", "qa", "ha"] \
+SEMAPHORES = ["v", "s", "t", "p", "dx", "dx2", "dr", "dw", "du", "dv", "dgt", "dgo", "out", "sent", "qa", "ha"] \
     + ["xa%d" % i for i in range(3)] + ["ar%d" % i for i in range(3)]
+FAR = 4096
 WAKE, CYC = 0.12, 0.00083
 
 
@@ -205,11 +206,11 @@ def rank_program(g, core, T, topo):
         total[sem] = total.get(sem, 0) + 16
         return add(q, lambda: e.dma_start(out(), in_()), outs, ins, 0.06, lat, sem, extra)
 
-    def send(dst, out, in_, sem):
+    def send(dst, out, in_, sem, *more):
         c = T.cores[dst]
         rid, pid, _ = topo.addr(c)
         total["sent"] = total.get("sent", 0) + len(topo.engines(core, c))
-        return add("p", lambda: g.remote_dma(mat(out), mat(in_), T.sem[sem], T.sem["sent"], pid, rid, topo.mask(core, c)), [], [in_], 0.25)
+        return add("p", lambda: g.remote_dma(mat(out), mat(in_), T.sem[sem], T.sem["sent"], pid, rid, topo.mask(core, c)), [], [in_] + list(more), 0.25)
 
     def arrive(sem, src, writes, outs, lat, extra):
         total[sem] = total.get(sem, 0) + writes * sum(len(topo.engines(T.cores[s], core)) for s in src)
@@ -219,7 +220,7 @@ def rank_program(g, core, T, topo):
         v("copy", _cast(_o(to, a, z), "u32"), _ind(_cast(_o(win, c, d), "u32"), off))
         act(_o(to + "s", a, z), _ind(_o(win + "s", c, d), off), F.Copy)
 
-    o, H, W = _o, [(0, 128), (128, 256)], [(0, 32), (32, 64)]
+    o, H, W = _o, [(0, 128), (128, 256)], [(0, 64), (64, 128)]
     f = lambda k: _o("sf", k, k + 1)
     role = lambda b: _o(b, 3, 256, 4)
     ps = lambda b, n: _o("ps", 512 * b, 512 * b + n)
@@ -235,11 +236,16 @@ def rank_program(g, core, T, topo):
     do("p", "iota32", (o("si", 0, 1), [[0, 1]], 0, 1))
     for k in (0, 240):
         iota(o("tokf", k, k + 240), [[1, 240]], 0, 0)
-    iota(o("k1"), [[0, 15], [256, 4]], 0, 0)
+    iota(o("kp"), [[0, 15], [256, 4]], 64 - FAR, 0)
+    fill = lambda out: iota(out, [[0, _width(out)]], 0, 0)
+    fill(o("el", 0, 544))
+    fill(o("el", 544, 1088))
     iota(o("kv"), [[1, 16], [0, 4]], 0, 0)
     iota(o("ka"), [[0, 16], [-1, 4]], 99, 0)
     iota(o("kb"), [[0, 16], [2, 4]], 1, 0)
-    v("set", o("rtt", 16, 512), 0.0)
+    for name in ("tabw", "lab2", "qo", "wnw", "m2"):
+        fill(o(name))
+    v("set", o("rtt", 16, 496), 0.0)
     v("set", o("zero"), 0.0)
     v("set", o("sl"), 8)
     v("set", o("ul"), 0)
@@ -248,7 +254,6 @@ def rank_program(g, core, T, topo):
     v("set", o("rst"), 1.0)
     v("set", o("rst", 0, 256, 4), 0.0)
     v("set", ones(0, 256), 1.0)
-    v("set", o("el"), 0.0)
     v("ts", o("si", 1, 2), o("si", 0, 1), 15, None, A.bitwise_and)
     v("ts", o("si", 2, 3), o("si", 0, 1), 15, 2, A.bitwise_and, A.logical_shift_right)
     v("ts", o("si", 3, 4), o("si", 0, 1), 3, None, A.bitwise_and)
@@ -271,14 +276,13 @@ def rank_program(g, core, T, topo):
     v("ts", f(12), f(2), 3.0, -8.0, A.is_equal, A.mult)
     v("tt", f(14), f(11), f(12), A.add)
     v("ts", f(16), f(4), -1e-30, None, A.mult)
-    v("ts", f(18), f(3), 16.0, 31.0, A.mult, A.add)
+    v("ts", f(18), f(3), 16.0, 31.0 - 64.0, A.mult, A.add)
     act(o("tok"), o("tokf"), F.Identity, f(20))
 
-    v("ts", o("rtt", 512, 528), o("rtt", 0, 16), -1.0, None, A.mult)
+    v("ts", o("rtt", 496, 512), o("rtt", 0, 16), -1.0, None, A.mult)
     v("q", o("rq"), o("rqs"), o("rtt", 0, 512))
-    v("q", o("rqn"), o("rqns"), o("rtt", 16, 528))
     pick("rr", 0, 144, "rq", 0, 128, o("sl", 0, 9))
-    pick("rr", 144, 288, "rqn", 0, 128, o("sl", 10, 19))
+    pick("rr", 144, 288, "rq", 0, 128, o("sl", 10, 19))
     for h, (x0, x1) in enumerate([(0, 144), (144, 272)]):
         v("q", o("xq", x0, x1), o("xqs", x0, x1), o("xt", 4 * x0, 4 * x1))
         for j, (lo, sh) in enumerate([(0, 0), (16, 16), (144, 0), (160, 16)]):
@@ -293,14 +297,15 @@ def rank_program(g, core, T, topo):
         v("tr", o("nn", *s), o("mm", *s))
         v("scan", o("pp", *s), ones(*s), o("nn", *s), o("pp", 127, 128) if h else f(17), A.mult, A.add)
         v("tr", o("tp", *s), o("pp", *s))
-    v("ts", o("mab", 0, 64), role("cc"), 0.0, None, A.is_equal)
-    v("ts", o("mab", 64, 128), role("cc"), 1.0, None, A.is_equal)
-    v("tt", o("vv"), o("tp", 3, 240, 4), o("k1"), A.add)
-    v("tt", o("pab", 0, 60), o("mab", 0, 60), o("vv"), A.mult)
-    v("tt", o("pab", 60, 120), o("mab", 64, 124), o("vv"), A.mult)
-    v("scan", o("t1"), o("rst", 0, 120), o("pab"), 0.0, A.mult, A.add)
+    for k in range(2):
+        v("ts", o("pe", *W[k]), role("cc"), float(k), float(FAR), A.is_equal, A.mult)
+        v("tt", o("pp2", 60 * k, 60 * k + 60), o("pe", 64 * k, 64 * k + 60), o("kp"), A.add)
+    for x0, x1 in ((0, 32), (32, 60)):
+        for k in (0, 60):
+            v("tt", o("pab", k + x0, k + x1), o("tp", 4 * x0 + 3, 4 * x1, 4), o("pp2", k + x0, k + x1), A.add)
+    v("scan", o("t1"), o("rst", 0, 120), o("pab"), 0.0, A.mult, A.max)
     v("ts", o("off1"), o("t1", 3, 120, 4), f(18), None, A.add)
-    v("copy", _ind(o("el"), o("off1")), o("tok"))
+    after = [v("copy", _ind(o("el"), o("off1")), o("tok"))]
 
     def wrap(x, lo, n):
         xn, xp, wl, off = "xn" + x, "xp" + x, "wl" + x, "off2" + ("a" if x else "")
@@ -308,7 +313,7 @@ def rank_program(g, core, T, topo):
         v("ts", o(xp), o("lt", lo, lo + 16 * n, 16), f(3), None, A.mult)
         v("tt", o(wl, 0, n, 2), o(xn, 0, n, 2), o(xp, 1, n, 2), A.add)
         v("tt", o(wl, 1, n - 1, 2), o(xn, 3, n, 2), o(xp, 0, n - 2, 2), A.add)
-        v("copy", o(off, 0, n - 1), o(wl, 0, n - 1))
+        return v("copy", o(off, 0, n - 1), o(wl, 0, n - 1))
 
     sent = []
 
@@ -317,88 +322,90 @@ def rank_program(g, core, T, topo):
         if e != me:
             i = place(me, e)
             sent.append(send(e, _cast(o("xl", 128 * i, 128 * i + 128), "u8"), _cast(o("xs", 128 * e, 128 * e + 128), "u8"), "xa%d" % i))
-            sent.append(send(e, o("xls", 128 * i, 128 * i + 128), o("xss", 128 * e, 128 * e + 128), "xa%d" % i))
+            sent.append(send(e, o("xls", 128 * i, 128 * i + 128), o("xss", 128 * e, 128 * e + 128), "xa%d" % i, o("xs", 128 * e, 128 * e + 128)))
     for n, e in enumerate(order + [me]):
         v("tr", o("lt", 160 * e, 160 * e + 160), o("el", 256 * e + 32, 256 * e + 192))
         if n == 0:
-            wrap("1", 160 * e, 10)
+            after = [wrap("1", 160 * e, 10)]
             token(e, o("off2a", 0, 8))
     wrap("", 0, 40)
     for e in order[1:] + [me]:
         token(e, o("off2", 10 * e, 10 * e + 8))
 
-    v("set", o("hb", 512, 576), 0.0)
-    v("set", o("ut", 8, 512), 0.0)
+    v("set", o("hb", 512, 576), 0.0, extra=after)
+    v("set", o("ut", 8, 512), 0.0, extra=after)
     for i in range(4):
-        v("q", o("wq", 128 * i, 128 * i + 128), o("wqs", 128 * i, 128 * i + 128), o("wt", 512 * i, 512 * i + 512))
-    v("q", o("uq"), o("uqs"), o("ut"))
+        v("q", o("wq", 128 * i, 128 * i + 128), o("wqs", 128 * i, 128 * i + 128), o("wt", 512 * i, 512 * i + 512), extra=after)
+    v("q", o("uq"), o("uqs"), o("ut"), extra=after)
     pick("ur", 0, 128, "uq", 0, 128, o("ul"))
-    sets = [0]
 
-    def chunk(xc, lo, hlo, hn, hc, hto):
-        b = 4 * (sets[0] % 2)
-        sets[0] += 1
-        for i in range(4):
-            mx(ps(b + i, 128), o("wq", 128 * i, 128 * i + 128), o("wqs", 128 * i, 128 * i + 128), o(xc, lo, lo + 128), o(xc + "s", lo, lo + 128), True, True)
+    def chunk(xc, lo, hlo, hn, hc, hto, banks):
+        for i, b in enumerate(banks):
+            mx(ps(b, 128), o("wq", 128 * i, 128 * i + 128), o("wqs", 128 * i, 128 * i + 128), o(xc, lo, lo + 128), o(xc + "s", lo, lo + 128), True, True)
             out = o("hb", hlo + i, hlo + 512, 4)
             if i % 2 == 0:
-                act(out, ps(b + i, 128), F.Relu, 0.0, 0.0625)
+                act(out, ps(b, 128), F.Relu, 0.0, 0.0625)
             else:
-                v("ts", out, ps(b + i, 128), 0.0, 0.0625, A.max, A.mult)
+                v("ts", out, ps(b, 128), 0.0, 0.0625, A.max, A.mult)
         v("q", o(hc, hto, hto + hn), o(hc + "s", hto, hto + hn), o("hb", hlo, hlo + 4 * hn))
-        return b
 
-    b = chunk("xs", 128 * me, 0, 144, "zq", 0)
-    g0 = v("set", o("gt", 0, 520), -9e29)
-    v("set", o("gt", 520, 528), 9e29)
-    mx(ps(b, 128), o("ur"), o("urs"), o("zq", 0, 128), o("zqs", 0, 128), True, True)
-    act(o("gt", 0, 128), ps(b, 128), F.Copy)
+    chunk("xs", 128 * me, 0, 144, "zq", 0, (0, 1, 2, 3))
+    fills = []
+    for t in ("gt", "gtt"):
+        fills.append(act(o(t, 0, 480), o("tokf"), F.Identity, -9e29, 0.0))
+        fills.append(act(o(t, 480, 520), o("tokf", 0, 40), F.Identity, -9e29, 0.0))
+        act(o(t, 520, 528), o("tokf", 0, 8), F.Identity, 9e29, 0.0)
+    mx(ps(0, 128), o("ur"), o("urs"), o("zq", 0, 128), o("zqs", 0, 128), True, True)
+    act(o("gt", 0, 128), ps(0, 128), F.Copy)
+    act(o("gtt", 0, 128), ps(0, 128), F.Copy)
 
     rel = [0 if e == me else 128 + 128 * others.index(e) for e in range(4)]
     for e in range(4):
-        v("set", o("kr", e, 64, 4), float(rel[e] - 1 - 512))
-    v("ts", o("tk"), role("tp"), 128.5, None, A.is_lt)
-    v("tt", o("v2"), role("tp"), o("kr"), A.add)
-    v("tt", o("abe", 0, 64), o("mab", 0, 64), o("tk"), A.mult)
-    v("tt", o("abe", 64, 128), o("mab", 64, 128), o("tk"), A.mult)
+        act(o("kr", e, 64, 4), o("zero"), F.Identity, float(rel[e] - 1 - 512))
+    v("ts", o("mab", 0, 64), role("cc"), 0.0, None, A.is_equal, extra=after)
+    v("ts", o("mab", 64, 128), role("cc"), 1.0, None, A.is_equal, extra=after)
+    v("ts", o("tk"), role("tp"), 128.5, None, A.is_lt, extra=after)
+    v("tt", o("v2"), role("tp"), o("kr"), A.add, extra=after)
+    v("tt", o("abe", 0, 64), o("mab", 0, 64), o("tk"), A.mult, extra=after)
+    v("tt", o("abe", 64, 128), o("mab", 64, 128), o("tk"), A.mult, extra=after)
     v("tt", o("pab2", 0, 64), o("abe", 0, 64), o("v2"), A.mult)
     v("tt", o("pab2", 64, 128), o("abe", 64, 128), o("v2"), A.mult)
     v("scan", o("t2"), o("rst", 0, 128), o("pab2"), 0.0, A.mult, A.add)
     v("ts", o("off3"), o("t2", 3, 128, 4), 512.0, None, A.add)
-    v("ts", o("kv2"), o("kv"), f(13), None, A.subtract)
-    v("ts", o("kv"), o("kv2"), 0.0, None, A.is_ge)
-    v("ts", o("kv3"), o("kv2"), 13.5, None, A.is_lt)
+    v("ts", o("kv2"), o("kv"), f(13), None, A.subtract, extra=after)
+    v("ts", o("kv"), o("kv2"), 0.0, None, A.is_ge, extra=after)
+    v("ts", o("kv3"), o("kv2"), 13.5, None, A.is_lt, extra=after)
     v("tt", o("kv2"), o("kv"), o("kv3"), A.mult)
     v("tt", o("ae"), o("abe", 0, 64), o("kv2"), A.mult)
     v("tt", o("be"), o("abe", 64, 128), o("kv2"), A.mult)
     v("tt", o("de"), o("ae"), o("be"), A.subtract)
-    v("set", o("m2"), 0.0)
-    v("set", o("wa", 240, 256), 0.0)
+    v("set", o("wa", 240, 256), 0.0, extra=after)
     for k in range(3):
-        v("ts", f(21 + k), f(0), float(16 * k), None, A.add)
-    v("set", o("rsl"), 1.0)
-    v("set", o("rsl", 0, 384, 128), 0.0)
+        v("ts", f(25 + k), f(0), float(16 * k), 2.0, A.add, A.mult, extra=after)
+        v("ts", f(28 + k), f(25 + k), 2.0, None, A.add, extra=after)
+        v("ts", o("bt", 65 * k, 588, 196), o("zero", 0, 3), f(28 + k), -64.0, A.add, A.mult, extra=after)
+    v("set", o("rsl"), 1.0, extra=after)
+    v("set", o("rsl", 0, 196, 65), 0.0, extra=after)
 
     asked = []
+    BANKS = [(4, 5, 6, 7), (0, 1, 2, 3), (4, 5, 6, 3)]
     for n, s in enumerate(order):
         i = others.index(s)
         arrive("xa%d" % i, [s], 2, [o("xl", 128 * i, 128 * i + 128), o("xls", 128 * i, 128 * i + 128)], 2.4, sent[2 * n:2 * n + 2])
-        b = chunk("xl", 128 * i, 576 + 512 * i, 128, "hq", 128 * i)
-        mx(ps(b + 3, 128), o("hq", 128 * i, 128 * i + 128), o("hqs", 128 * i, 128 * i + 128), o("uq"), o("uqs"), True, True)
-        act(o("qs", i, i + 1), ps(b + 3, 1), F.Copy)
+        chunk("xl", 128 * i, 576 + 512 * i, 128, "hq", 128 * i, BANKS[n])
+        b = BANKS[n][0 if n else 3]
+        mx(ps(b, 128), o("hq", 128 * i, 128 * i + 128), o("hqs", 128 * i, 128 * i + 128), o("uq"), o("uqs"), True, True)
+        act(o("qs", i, i + 1), ps(b, 1), F.Copy)
         k, c = place(me, s), T.cores[s]
         rid, pid, _ = topo.addr(c)
         total["sent"] += len(topo.engines(core, c))
         asked.append(add("p", lambda i=i, k=k, c=c, rid=rid, pid=pid: g.remote_dma(T.dg[128 * k:128 * k + 128, :], T.qs[:, i:i + 1], T.sem.qa, T.sem.sent, pid, rid, topo.mask(core, c)),
                          [], [o("qs", i, i + 1)], 0.25))
 
-    v("set", o("tabw"), 0.0)
-    v("set", o("tab", 256, 288), 0.0)
-    v("set", o("tab", 544, 576), 0.0)
-    v("set", o("lab2"), 0.0)
-    v("set", o("qo"), 0.0)
+    v("set", o("tab", 256, 288), 0.0, extra=after)
+    v("set", o("tab", 544, 576), 0.0, extra=after)
     for e in range(4):
-        v("set", _part(f(24), 32 * e), float(rel[e] - 520))
+        v("set", _part(f(24), 32 * e), float(rel[e] - 520), extra=after)
         v("copy", _part(o("offl", 16, 24), 32 * e), _part(o("off2", 10 * e, 10 * e + 8), 32 * e))
     act(o("own"), o("tokf", 0, 128), F.Identity, f(24))
     for k in range(2):
@@ -416,45 +423,47 @@ def rank_program(g, core, T, topo):
         v("ts", o("offl", 8 * k + 1, 8 * k + 8, 2), o("lt0", s[0], s[1], 32), 520.0, None, A.add)
 
     arrive("qa", others, 1, [o("dg")], 1.7, asked)
+    late = []
+    for n, e in enumerate(order):
+        i, q = others.index(e), "ys"
+        late.append(dma(q[n % 2], "dgt", lambda e=e: T.gt[32 * e:32 * e + 1, 128:512], lambda: T.dg[:, :], [_part(o("gt", 128, 512), 32 * e)], [o("dg")]))
+        late.append(dma(q[1 - n % 2], "dgt", lambda e=e: T.qo[32 * e:32 * e + 1, :], lambda i=i: T.dg[128 * i:128 * i + 128, :],
+                        [_part(o("qo"), 32 * e)], [o("dg")]))
     for k in range(8):
-        dma("y" if k % 2 == 0 else "s", "dgt", lambda k=k: T.gt[16 * k:16 * k + 1, 128:512], lambda: T.dg[:, :],
-            [o("gt", 128 + 48 * k, 176 + 48 * k)], [o("dg")], (g0,))
-    for e in others:
-        i = others.index(e)
-        dma("y" if i % 2 == 0 else "s", "dgt", lambda e=e: T.qo[32 * e:32 * e + 1, :], lambda i=i: T.dg[128 * i:128 * i + 128, :],
-            [_part(o("qo"), 32 * e)], [o("dg")])
+        dma("ys"[k % 2], "dgo", lambda k=k: T.gtt[16 * k:16 * k + 1, 128:512], lambda: T.dg[:, :],
+            [o("gtt", 128 + 48 * k, 176 + 48 * k)], [o("dg")], fills)
     v("tt", o("a1", 0, 128), _ind(o("gt"), o("offl", 0, 8)), o("qo"), A.is_le)
     v("tt", o("a1", 128, 256), _ind(o("gt"), o("offl", 8, 16)), o("qo"), A.is_lt)
     counted = v("scan", o("a2", 0, 128), o("a1", 0, 128), o("a1", 128, 256), 0.0, A.add, A.add)
     told = []
+    v("tt", o("vp"), o("a2", 0, 128, 2), o("a2", 1, 128, 2), A.add)
     for n, e in enumerate(order):
-        s = (128 * n, 128 * n + 128)
-        do("p", "pb", (o("cb", *s), _part(o("a2", 0, 128), 32 * e, 1), 128))
+        s, t = (64 * n, 64 * n + 64), 196 * n
+        do("p", "pb", (o("cb", *s), _part(o("vp"), 32 * e, 1), 128))
         for k in range(3):
-            v("ts", o("bt", 384 * n + 128 * k, 384 * n + 128 * k + 128), o("cb", *s), f(21 + k), None, A.is_le)
-        v("scan", o("sc", 384 * n, 384 * n + 384), o("rsl"), o("bt", 384 * n, 384 * n + 384), 0.0, A.mult, A.add)
-        v("ts", o("ls", 4 * e, 4 * e + 3), o("sc", 384 * n + 127, 384 * n + 384, 128), 127.0, None, A.min)
+            v("ts", o("bt", t + 65 * k + 1, t + 65 * k + 65), o("cb", *s), f(25 + k), f(28 + k), A.max, A.min)
+        v("scan", o("sc", t, t + 195), o("rsl", 0, 195), o("bt", t, t + 195), 0.0, A.mult, A.subtract)
+        v("ts", o("ls", 4 * e, 4 * e + 3), o("sc", t + 64, t + 195, 65), 127.0, None, A.min)
         i = place(me, e)
         told.append(send(e, o("la", 4 * i, 4 * i + 3), o("ls", 4 * e, 4 * e + 3), "ar%d" % i))
 
-    act(o("gab", 0, 128), _ind(o("gt"), o("off3", 16, 24)), F.Copy)
-    v("copy", o("gab", 128, 240), _ind(o("gt"), o("off3", 24, 31)), extra=(counted,))
-    v("tt", o("wa", 0, 128), _ind(o("gt"), o("off3", 0, 8)), o("gab", 0, 128), A.is_ge, extra=(counted,))
-    v("tt", o("wa", 128, 240), _ind(o("gt"), o("off3", 8, 15)), o("gab", 128, 240), A.is_ge)
+    act(o("gab", 0, 128), _ind(o("gtt"), o("off3", 16, 24)), F.Copy)
+    v("copy", o("gab", 128, 240), _ind(o("gtt"), o("off3", 24, 31)), extra=(counted,))
+    v("tt", o("wa", 0, 128), _ind(o("gtt"), o("off3", 0, 8)), o("gab", 0, 128), A.is_ge, extra=(counted,))
+    v("tt", o("wa", 128, 240), _ind(o("gtt"), o("off3", 8, 15)), o("gab", 128, 240), A.is_ge)
     quarter = lambda t, h: o(t, 3 + 128 * h, 128 + 128 * h, 4)
     for s in H:
         v("tr", o("wat", *s), o("wa", *s))
     for e in range(4):
         v("tt", o("x4", e, 64, 4), o("wat", 0, 256, 16), o("de", e, 64, 4), A.mult)
     for h, s in enumerate(H):
-        v("tt", quarter("m2", h), o("x4", *W[h]), o("be", *W[h]), A.add)
+        v("tt", quarter("m2", h), o("x4", 32 * h, 32 * h + 32), o("be", 32 * h, 32 * h + 32), A.add)
         v("tr", o("n2", *s), o("m2", *s))
         v("scan", o("rc", *s), ones(*s), o("n2", *s), o("rc", 127, 128) if h else 0.0, A.mult, A.add)
         v("tr", o("rtr", *s), o("rc", *s))
 
     for e in range(4):
-        v("set", o("kz", e, 64, 4), float(-1 - 128 if e == me else 144 + 48 * others.index(e) - 1 - 128))
-    v("set", o("wnw"), 0.0)
+        act(o("kz", e, 64, 4), o("zero"), F.Identity, float(-1 - 128 if e == me else 144 + 48 * others.index(e) - 1 - 128))
     v("q", o("vq"), o("vqs"), o("vt"))
     v("ts", o("h1"), role("rtr"), 48.5, None, A.is_lt)
     v("copy", o("xz"), role("rtr"))
@@ -482,7 +491,7 @@ def rank_program(g, core, T, topo):
         pick("hs", 48 * i, 48 * i + 48, "hq", 128 * i, 128 * i + 128, o("la", 4 * i, 4 * i + 3))
         k = 144 + 48 * place(me, s)
         came.append(send(s, _cast(o("zq", k, k + 48), "u8"), _cast(o("hs", 48 * i, 48 * i + 48), "u8"), "ha"))
-        came.append(send(s, o("zqs", k, k + 48), o("hss", 48 * i, 48 * i + 48), "ha"))
+        came.append(send(s, o("zqs", k, k + 48), o("hss", 48 * i, 48 * i + 48), "ha", o("hs", 48 * i, 48 * i + 48)))
 
     arrive("ha", others, 2, [o("zq", 144, 288), o("zqs", 144, 288)], 2.0, came)
     pick("z", 0, 128, "zq", 0, 288, o("off5", 0, 8))
@@ -494,7 +503,8 @@ def rank_program(g, core, T, topo):
     dma("y", "out", lambda: T.oc[:, :], lambda: T.z[:, 0:224].bitcast(dt.uint8), [], [o("z")])
     for k in range(4):
         dma("s" if k % 2 == 0 else "y", "out", lambda k=k: T.osc[4 * k:4 * k + 4, :], lambda k=k: T.zs[32 * k:32 * k + 4, :], [], [o("zs")])
-    dma("y", "out", lambda: T.y[:, :], lambda: T.ysb[:, :], [], [o("ysb")])
+    for a, z in ((0, 128), (128, 224)):
+        dma("y", "out", lambda a=a, z=z: T.y[:, a:z], lambda a=a, z=z: T.ysb[:, a:z], [], [o("ysb", a, z)])
 
     queue = {"v": V, "s": g.scalar, "t": g.tensor, "p": g, "y": g.sync}
     lists = _order(ops)

from concourse.mybir import dt, AluOpType as A, ActivationFunctionType as F


def _buffers():
    d = {"dg": ("dram", [384, 1], "float32"), "ps": ("psum", [128, 4096], "float32")}
    kinds = {
        "bfloat16": "xt 1088 rtt 512 wt 2048 ut 512 vt 512 hb 2112 rst 256 one 256 tok 480 a1 256 a2 256 cc 256 mm 256 nn 256 "
                    "pp 256 tp 256 el 1088 lt 640 wa 256 wat 256 m2 256 n2 256 rc 256 rtr 256 "
                    "tabw 512 tab 576 vp 64 bt 588 sc 588 rsl 196",
        "float32": "ysb 224 sf 40 zero 16 tokf 480 kp 60 pe 128 pp2 128 ka 64 kb 64 kz 64 kr 64 kv 64 kv2 64 kv3 64 mab 128 pab 120 "
                   "t1 120 xn 40 xp 40 wl 40 xn1 10 xp1 10 wl1 10 tk 64 abe 128 v2 64 pab2 128 t2 128 ae 64 be 64 de 64 qs 4 "
                   "gt 528 gtt 528 gab 256 x4 64 qo 128 own 128 gab2 256 isa 256 lab 256 lab2 320 lt1 256 lt0 256 h1 64 hm 64 xz 64 "
                   "z1 64 z2 64 z3 64 zn 16 zp 16 zl 14 w1 64 w2 64 w3 64 w4 64 wnw 256 wnf 256",
        "uint16": "sl 20 ul 8 off1 30 off2 40 off2a 10 off3 32 offl 24 off5 14 ls 16 la 12",
        "int32": "si 8",
    }
    for t, text in kinds.items():
        w = text.split()
        for name, n in zip(w[::2], w[1::2]):
            d[name] = ("sbuf", [128, int(n)], t)
    d["cb"] = d.pop("one")[:1] + ([128, 640], "bfloat16")
    w = "xq 272 rq 128 rr 288 wq 512 uq 128 ur 128 vq 128 xs 512 xl 384 hq 384 hs 144 zq 288 z 224".split()
    for name, n in zip(w[::2], w[1::2]):
        d[name] = ("sbuf", [128, int(n)], "float8_e4m3fn_x4")
        d[name + "s"] = ("sbuf", [128, int(n)], "uint8")
    return d


SCRATCH = _buffers()
SEMAPHORES = ["v", "s", "t", "p", "dx", "dx2", "dr", "dw", "du", "dv", "dgt", "dgo", "out", "sent", "qa", "ha"] \
    + ["xa%d" % i for i in range(3)] + ["ar%d" % i for i in range(3)]
FAR = 4096
WAKE, CYC = 0.12, 0.00083


def _o(name, a=0, z=None, step=1):
    return ("@", name, a, SCRATCH[name][1][1] if z is None else z, step, None, None, None)


def _cast(o, how):
    return o[:5] + (how,) + o[6:]


def _ind(o, off):
    return o[:6] + (off, o[7])


def _part(o, p, n=32):
    return o[:7] + ((p, p + n),)


def _keys(o):
    if o[1] == "ps":
        return [("ps", b) for b in range(o[2] // 512, (o[3] - 1) // 512 + 1)]
    blocks = range(o[7][0] // 32, (o[7][1] - 1) // 32 + 1) if o[7] else range(4)
    return [(o[1], c, b) for c in range(o[2], o[3], o[4]) for b in blocks]


def _isop(x):
    return isinstance(x, tuple) and len(x) == 8 and x[0] == "@"


def _width(o):
    return 16 * (o[6][3] - o[6][2]) if o[6] else len(range(o[2], o[3], o[4]))


def _cost(name, args):
    out, n = args[0], _width(args[0])
    if name == "mx":
        return (n + 16) * CYC
    if name == "q":
        return .012 + .00088 * n
    ops = [a for a in args if _isop(a)]
    if name == "pb":
        return .14 + 4 * n * CYC
    if name == "iota":
        return .13 + 2 * n * CYC
    if name == "act":
        return .065 + n * CYC * (1.5 if args[1][6] else 1)
    if out[6]:
        return .05 + 3 * n * CYC
    if any(a[6] for a in ops):
        return .05 + 1.6 * n * CYC
    two = all(SCRATCH[a[1]][2] in ("bfloat16", "uint16") for a in ops if _width(a) > 1)
    return max(64, n * (2 if name == "tt" else .5 if two else 1)) * CYC


def _order(ops):
    n = len(ops)
    prio = [0.0] * n
    for i in range(n - 1, -1, -1):
        prio[i] += ops[i]["cost"] + ops[i]["lat"]
        for d in ops[i]["deps"]:
            prio[d] = max(prio[d], prio[i] + WAKE)
    need = [len(o["deps"]) for o in ops]
    succ = [[] for o in ops]
    for i, o in enumerate(ops):
        for d in o["deps"]:
            succ[d].append(i)
    ready, fin, free = [0.0] * n, [0.0] * n, {}
    can, lists = {}, {}

    def release(i):
        q = ops[i]["q"]
        if q is None:
            finish(i, ready[i])
        else:
            can.setdefault(q, []).append(i)

    def finish(i, start):
        fin[i] = start + ops[i]["cost"] + ops[i]["lat"]
        for j in succ[i]:
            ready[j] = max(ready[j], fin[i] + (WAKE if ops[j]["q"] else 0))
            need[j] -= 1
            if need[j] == 0:
                release(j)
    for i in range(n):
        if not ops[i]["deps"]:
            release(i)
    while True:
        best = None
        for q, c in can.items():
            if not c:
                continue
            t = free.get(q, 0.0)
            m = min(max(t, ready[i]) for i in c)
            pick = max((i for i in c if max(t, ready[i]) <= m + 1e-9), key=lambda i: prio[i])
            for d in sorted(c, key=lambda i: -prio[i]):
                e = max(t, ready[d])
                if prio[d] > prio[pick] and e - m < m + ops[pick]["cost"] - e:
                    pick, m = d, e
                    break
            if best is None or m < best[0]:
                best = (m, q, pick)
        if best is None:
            break
        m, q, i = best
        can[q].remove(i)
        lists.setdefault(q, []).append(i)
        free[q] = m + ops[i]["cost"]
        finish(i, m)
    return lists


def rank_program(g, core, T, topo):
    me = T.rank_of(core)
    if me is None:
        return
    others = [r for r in range(4) if r != me]
    place = lambda src, dst: [r for r in range(4) if r != dst].index(src)

    def far(r):
        a, b = topo.chip(core), topo.chip(T.cores[r])
        return 2 if topo.mates(a, b) else 1 if topo.same_plane(a, b) else 0
    order = sorted(others, key=far)

    ops, wrote, readers = [], {}, {}
    total = {}
    kinds = {"u8": dt.uint8, "u32": dt.uint32}

    def mat(o):
        p, z = o[7] or (0, SCRATCH[o[1]][1][0])
        x = T[o[1]][p:z, o[2]:o[3]] if o[4] == 1 else T[o[1]][p:z, o[2]:o[3]:o[4]]
        if o[5]:
            x = x.bitcast(kinds[o[5]])
        return x.indirect(mat(o[6])) if o[6] else x

    def add(q, fn, outs, ins, cost, lat=0.0, sem=None, extra=()):
        i, deps = len(ops), set(extra)
        for o in list(ins) + list(outs):
            if o[6]:
                ins = list(ins) + [o[6]]
        for o in ins:
            if o[1] != "ps":
                for k in _keys(o):
                    if k in wrote:
                        deps.add(wrote[k])
                    readers.setdefault(k, []).append(i)
        for o in list(outs) + [o for o in ins if o[1] == "ps"]:
            for k in _keys(o):
                if k in wrote:
                    deps.add(wrote[k])
                deps.update(readers.pop(k, ()))
                wrote[k] = i
        deps.discard(i)
        ops.append({"q": q, "fn": fn, "deps": deps, "cost": cost, "lat": lat, "sem": sem})
        return i

    V = g.vector
    calls = {"copy": V.tensor_copy, "tt": V.tensor_tensor, "ts": V.tensor_scalar, "set": V.memset, "tr": V.transpose,
             "scan": V.tensor_tensor_scan, "q": V.quantize_mx, "act": g.scalar.activation, "mx": g.tensor.matmul_mx,
             "iota": lambda *a: g.iota(*a, allow_small_or_imprecise_dtypes=True), "iota32": g.iota, "pb": g.partition_broadcast}

    def do(q, name, args, extra=()):
        k = 2 if name == "q" else 1
        fn = lambda: calls[name](*[mat(a) if _isop(a) else a for a in args])
        return add(q, fn, args[:k], [a for a in args[k:] if _isop(a)], _cost(name.replace("32", ""), args), 0.0, "own", extra)

    v = lambda name, *args, extra=(): do("v", name, args, extra)
    act = lambda *args: do("s", "act", args)
    mx = lambda *args: do("t", "mx", args)
    iota = lambda *args: do("p", "iota", args)

    def dma(q, sem, out, in_, outs, ins, extra=(), lat=2.1):
        e = {"y": g.sync, "s": g.scalar}[q]
        total[sem] = total.get(sem, 0) + 16
        return add(q, lambda: e.dma_start(out(), in_()), outs, ins, 0.06, lat, sem, extra)

    def send(dst, out, in_, sem, *more):
        c = T.cores[dst]
        rid, pid, _ = topo.addr(c)
        total["sent"] = total.get("sent", 0) + len(topo.engines(core, c))
        return add("p", lambda: g.remote_dma(mat(out), mat(in_), T.sem[sem], T.sem["sent"], pid, rid, topo.mask(core, c)), [], [in_] + list(more), 0.25)

    def arrive(sem, src, writes, outs, lat, extra):
        total[sem] = total.get(sem, 0) + writes * sum(len(topo.engines(T.cores[s], core)) for s in src)
        return add(None, None, outs, [], 0.0, lat, sem, extra)

    def pick(to, a, z, win, c, d, off):
        v("copy", _cast(_o(to, a, z), "u32"), _ind(_cast(_o(win, c, d), "u32"), off))
        act(_o(to + "s", a, z), _ind(_o(win + "s", c, d), off), F.Copy)

    o, H, W = _o, [(0, 128), (128, 256)], [(0, 64), (64, 128)]
    f = lambda k: _o("sf", k, k + 1)
    role = lambda b: _o(b, 3, 256, 4)
    ps = lambda b, n: _o("ps", 512 * b, 512 * b + n)
    ones = lambda a, z: _o("cb", 384 + a, 384 + z)

    dma("s", "dr", lambda: T.rtt[:, 0:16], lambda: T.rt[:, 0:16], [o("rtt", 0, 16)], [])
    dma("y", "dx", lambda: T.xt[:, 64:576], lambda: T.x[:, 0:512], [o("xt", 64, 576)], [], (), 2.6)
    dx = dma("y", "dx2", lambda: T.xt[:, 576:960], lambda: T.x[:, 512:896], [o("xt", 576, 960)], [], (), 3.0)
    dma("y", "dw", lambda: T.wt[:, :], lambda: T.w[:, :], [o("wt")], [], (dx,), 4.5)
    dma("y", "du", lambda: T.ut[:, 0:8], lambda: T.u[:, 0:8], [o("ut", 0, 8)], [], (dx,), 4.8)
    dma("y", "dv", lambda: T.vt[:, :], lambda: T.v[:, :], [o("vt")], [], (dx,), 5.0)

    do("p", "iota32", (o("si", 0, 1), [[0, 1]], 0, 1))
    for k in (0, 240):
        iota(o("tokf", k, k + 240), [[1, 240]], 0, 0)
    iota(o("kp"), [[0, 15], [256, 4]], 64 - FAR, 0)
    fill = lambda out: iota(out, [[0, _width(out)]], 0, 0)
    fill(o("el", 0, 544))
    fill(o("el", 544, 1088))
    iota(o("kv"), [[1, 16], [0, 4]], 0, 0)
    iota(o("ka"), [[0, 16], [-1, 4]], 99, 0)
    iota(o("kb"), [[0, 16], [2, 4]], 1, 0)
    for name in ("tabw", "lab2", "qo", "wnw", "m2"):
        fill(o(name))
    v("set", o("rtt", 16, 496), 0.0)
    v("set", o("zero"), 0.0)
    v("set", o("sl"), 8)
    v("set", o("ul"), 0)
    v("set", o("xt", 0, 64), 0.0)
    v("set", o("xt", 960, 1088), 0.0)
    v("set", o("rst"), 1.0)
    v("set", o("rst", 0, 256, 4), 0.0)
    v("set", ones(0, 256), 1.0)
    v("ts", o("si", 1, 2), o("si", 0, 1), 15, None, A.bitwise_and)
    v("ts", o("si", 2, 3), o("si", 0, 1), 15, 2, A.bitwise_and, A.logical_shift_right)
    v("ts", o("si", 3, 4), o("si", 0, 1), 3, None, A.bitwise_and)
    v("ts", o("si", 4, 5), o("si", 0, 1), 16, 4, A.bitwise_and, A.logical_shift_right)
    v("copy", o("sf", 0, 4), o("si", 1, 5))
    v("ts", f(4), f(2), f(1), None, A.is_lt)
    v("ts", f(5), f(2), 3.0, None, A.is_lt)
    v("ts", f(6), f(1), 116.0, None, A.add)
    v("ts", f(7), f(2), -7.0, None, A.add)
    v("tt", f(8), f(7), f(4), A.subtract)
    v("tt", f(9), f(6), f(5), A.mult)
    v("tt", f(10), f(8), f(5), A.mult)
    v("ts", o("sl", 0, 9, 2), o("zero", 0, 5), f(10), 8.0, A.add, A.add)
    v("ts", o("sl", 10, 19, 2), o("zero", 0, 5), f(9), 8.0, A.add, A.add)
    v("ts", f(13), f(3), -1.0, 1.0, A.mult, A.add)
    v("ts", f(20), f(3), 16.0, None, A.mult)
    v("ts", f(15), f(1), 2.0, -16.0, A.is_lt, A.mult)
    v("tt", f(17), f(15), f(13), A.mult)
    v("ts", f(11), f(2), 0.0, 8.0, A.is_equal, A.mult)
    v("ts", f(12), f(2), 3.0, -8.0, A.is_equal, A.mult)
    v("tt", f(14), f(11), f(12), A.add)
    v("ts", f(16), f(4), -1e-30, None, A.mult)
    v("ts", f(18), f(3), 16.0, 31.0 - 64.0, A.mult, A.add)
    act(o("tok"), o("tokf"), F.Identity, f(20))

    v("ts", o("rtt", 496, 512), o("rtt", 0, 16), -1.0, None, A.mult)
    v("q", o("rq"), o("rqs"), o("rtt", 0, 512))
    pick("rr", 0, 144, "rq", 0, 128, o("sl", 0, 9))
    pick("rr", 144, 288, "rq", 0, 128, o("sl", 10, 19))
    for h, (x0, x1) in enumerate([(0, 144), (144, 272)]):
        v("q", o("xq", x0, x1), o("xqs", x0, x1), o("xt", 4 * x0, 4 * x1))
        for j, (lo, sh) in enumerate([(0, 0), (16, 16), (144, 0), (160, 16)]):
            sh += 128 * h
            mx(ps(h, 128), o("rr", lo, lo + 128), o("rrs", lo, lo + 128), o("xq", sh, sh + 128), o("xqs", sh, sh + 128), j == 0, j == 3)

    for h, s in enumerate(H):
        v("ts", o("a1", *s), ps(h, 128), f(16), f(14), A.is_gt, A.add)
        v("tr", o("a2", *s), o("a1", *s))
        v("scan", o("cc", *s), o("rst", *s), o("a2", *s), 0.0, A.mult, A.add)
        v("ts", o("mm", *s), o("cc", *s), 1.5, None, A.is_lt)
        v("tr", o("nn", *s), o("mm", *s))
        v("scan", o("pp", *s), ones(*s), o("nn", *s), o("pp", 127, 128) if h else f(17), A.mult, A.add)
        v("tr", o("tp", *s), o("pp", *s))
    for k in range(2):
        v("ts", o("pe", *W[k]), role("cc"), float(k), float(FAR), A.is_equal, A.mult)
        v("tt", o("pp2", 60 * k, 60 * k + 60), o("pe", 64 * k, 64 * k + 60), o("kp"), A.add)
    for x0, x1 in ((0, 32), (32, 60)):
        for k in (0, 60):
            v("tt", o("pab", k + x0, k + x1), o("tp", 4 * x0 + 3, 4 * x1, 4), o("pp2", k + x0, k + x1), A.add)
    v("scan", o("t1"), o("rst", 0, 120), o("pab"), 0.0, A.mult, A.max)
    v("ts", o("off1"), o("t1", 3, 120, 4), f(18), None, A.add)
    after = [v("copy", _ind(o("el"), o("off1")), o("tok"))]

    def wrap(x, lo, n):
        xn, xp, wl, off = "xn" + x, "xp" + x, "wl" + x, "off2" + ("a" if x else "")
        v("ts", o(xn), o("lt", lo, lo + 16 * n, 16), f(13), None, A.mult)
        v("ts", o(xp), o("lt", lo, lo + 16 * n, 16), f(3), None, A.mult)
        v("tt", o(wl, 0, n, 2), o(xn, 0, n, 2), o(xp, 1, n, 2), A.add)
        v("tt", o(wl, 1, n - 1, 2), o(xn, 3, n, 2), o(xp, 0, n - 2, 2), A.add)
        return v("copy", o(off, 0, n - 1), o(wl, 0, n - 1))

    sent = []

    def token(e, off):
        pick("xs", 128 * e, 128 * e + 128, "xq", 0, 272, off)
        if e != me:
            i = place(me, e)
            sent.append(send(e, _cast(o("xl", 128 * i, 128 * i + 128), "u8"), _cast(o("xs", 128 * e, 128 * e + 128), "u8"), "xa%d" % i))
            sent.append(send(e, o("xls", 128 * i, 128 * i + 128), o("xss", 128 * e, 128 * e + 128), "xa%d" % i, o("xs", 128 * e, 128 * e + 128)))
    for n, e in enumerate(order + [me]):
        v("tr", o("lt", 160 * e, 160 * e + 160), o("el", 256 * e + 32, 256 * e + 192))
        if n == 0:
            after = [wrap("1", 160 * e, 10)]
            token(e, o("off2a", 0, 8))
    wrap("", 0, 40)
    for e in order[1:] + [me]:
        token(e, o("off2", 10 * e, 10 * e + 8))

    v("set", o("hb", 512, 576), 0.0, extra=after)
    v("set", o("ut", 8, 512), 0.0, extra=after)
    for i in range(4):
        v("q", o("wq", 128 * i, 128 * i + 128), o("wqs", 128 * i, 128 * i + 128), o("wt", 512 * i, 512 * i + 512), extra=after)
    v("q", o("uq"), o("uqs"), o("ut"), extra=after)
    pick("ur", 0, 128, "uq", 0, 128, o("ul"))

    def chunk(xc, lo, hlo, hn, hc, hto, banks):
        for i, b in enumerate(banks):
            mx(ps(b, 128), o("wq", 128 * i, 128 * i + 128), o("wqs", 128 * i, 128 * i + 128), o(xc, lo, lo + 128), o(xc + "s", lo, lo + 128), True, True)
            out = o("hb", hlo + i, hlo + 512, 4)
            if i % 2 == 0:
                act(out, ps(b, 128), F.Relu, 0.0, 0.0625)
            else:
                v("ts", out, ps(b, 128), 0.0, 0.0625, A.max, A.mult)
        v("q", o(hc, hto, hto + hn), o(hc + "s", hto, hto + hn), o("hb", hlo, hlo + 4 * hn))

    chunk("xs", 128 * me, 0, 144, "zq", 0, (0, 1, 2, 3))
    fills = []
    for t in ("gt", "gtt"):
        fills.append(act(o(t, 0, 480), o("tokf"), F.Identity, -9e29, 0.0))
        fills.append(act(o(t, 480, 520), o("tokf", 0, 40), F.Identity, -9e29, 0.0))
        act(o(t, 520, 528), o("tokf", 0, 8), F.Identity, 9e29, 0.0)
    mx(ps(0, 128), o("ur"), o("urs"), o("zq", 0, 128), o("zqs", 0, 128), True, True)
    act(o("gt", 0, 128), ps(0, 128), F.Copy)
    act(o("gtt", 0, 128), ps(0, 128), F.Copy)

    rel = [0 if e == me else 128 + 128 * others.index(e) for e in range(4)]
    for e in range(4):
        act(o("kr", e, 64, 4), o("zero"), F.Identity, float(rel[e] - 1 - 512))
    v("ts", o("mab", 0, 64), role("cc"), 0.0, None, A.is_equal, extra=after)
    v("ts", o("mab", 64, 128), role("cc"), 1.0, None, A.is_equal, extra=after)
    v("ts", o("tk"), role("tp"), 128.5, None, A.is_lt, extra=after)
    v("tt", o("v2"), role("tp"), o("kr"), A.add, extra=after)
    v("tt", o("abe", 0, 64), o("mab", 0, 64), o("tk"), A.mult, extra=after)
    v("tt", o("abe", 64, 128), o("mab", 64, 128), o("tk"), A.mult, extra=after)
    v("tt", o("pab2", 0, 64), o("abe", 0, 64), o("v2"), A.mult)
    v("tt", o("pab2", 64, 128), o("abe", 64, 128), o("v2"), A.mult)
    v("scan", o("t2"), o("rst", 0, 128), o("pab2"), 0.0, A.mult, A.add)
    v("ts", o("off3"), o("t2", 3, 128, 4), 512.0, None, A.add)
    v("ts", o("kv2"), o("kv"), f(13), None, A.subtract, extra=after)
    v("ts", o("kv"), o("kv2"), 0.0, None, A.is_ge, extra=after)
    v("ts", o("kv3"), o("kv2"), 13.5, None, A.is_lt, extra=after)
    v("tt", o("kv2"), o("kv"), o("kv3"), A.mult)
    v("tt", o("ae"), o("abe", 0, 64), o("kv2"), A.mult)
    v("tt", o("be"), o("abe", 64, 128), o("kv2"), A.mult)
    v("tt", o("de"), o("ae"), o("be"), A.subtract)
    v("set", o("wa", 240, 256), 0.0, extra=after)
    for k in range(3):
        v("ts", f(25 + k), f(0), float(16 * k), 2.0, A.add, A.mult, extra=after)
        v("ts", f(28 + k), f(25 + k), 2.0, None, A.add, extra=after)
        v("ts", o("bt", 65 * k, 588, 196), o("zero", 0, 3), f(28 + k), -64.0, A.add, A.mult, extra=after)
    v("set", o("rsl"), 1.0, extra=after)
    v("set", o("rsl", 0, 196, 65), 0.0, extra=after)

    asked = []
    BANKS = [(4, 5, 6, 7), (0, 1, 2, 3), (4, 5, 6, 3)]
    for n, s in enumerate(order):
        i = others.index(s)
        arrive("xa%d" % i, [s], 2, [o("xl", 128 * i, 128 * i + 128), o("xls", 128 * i, 128 * i + 128)], 2.4, sent[2 * n:2 * n + 2])
        chunk("xl", 128 * i, 576 + 512 * i, 128, "hq", 128 * i, BANKS[n])
        b = BANKS[n][0 if n else 3]
        mx(ps(b, 128), o("hq", 128 * i, 128 * i + 128), o("hqs", 128 * i, 128 * i + 128), o("uq"), o("uqs"), True, True)
        act(o("qs", i, i + 1), ps(b, 1), F.Copy)
        k, c = place(me, s), T.cores[s]
        rid, pid, _ = topo.addr(c)
        total["sent"] += len(topo.engines(core, c))
        asked.append(add("p", lambda i=i, k=k, c=c, rid=rid, pid=pid: g.remote_dma(T.dg[128 * k:128 * k + 128, :], T.qs[:, i:i + 1], T.sem.qa, T.sem.sent, pid, rid, topo.mask(core, c)),
                         [], [o("qs", i, i + 1)], 0.25))

    v("set", o("tab", 256, 288), 0.0, extra=after)
    v("set", o("tab", 544, 576), 0.0, extra=after)
    for e in range(4):
        v("set", _part(f(24), 32 * e), float(rel[e] - 520), extra=after)
        v("copy", _part(o("offl", 16, 24), 32 * e), _part(o("off2", 10 * e, 10 * e + 8), 32 * e))
    act(o("own"), o("tokf", 0, 128), F.Identity, f(24))
    for k in range(2):
        v("ts", o("tabw", 256 * k, 256 * k + 256, 16), o("t2", 64 * k + 3, 64 * k + 64, 4), 256.0, None, A.add)
        v("tr", o("tab", 288 * k, 288 * k + 256), o("tabw", 256 * k, 256 * k + 256))
        act(o("gab2", 128 * k, 128 * k + 128), _ind(o("tab", 288 * k, 288 * k + 272), o("offl", 16, 24)), F.Identity, -264.0)
    for k, how in enumerate((A.is_equal, A.not_equal)):
        s = H[k]
        v("tt", o("isa", *s), o("gab2", 0, 128), o("own"), how, extra=asked)
        v("tt", o("lab", *s), o("isa", *s), o("gab2", *H[1 - k]), A.mult)
        act(o("lab2", 160 * k + 16, 160 * k + 144), o("lab", *s), F.Copy)
        v("tr", o("lt1", *s), o("lab", *s))
        v("tr", o("lt0", *s), o("lab2", 160 * k + 32, 160 * k + 160))
        v("ts", o("offl", 8 * k, 8 * k + 8, 2), o("lt1", s[0], s[1], 32), 520.0, None, A.add)
        v("ts", o("offl", 8 * k + 1, 8 * k + 8, 2), o("lt0", s[0], s[1], 32), 520.0, None, A.add)

    arrive("qa", others, 1, [o("dg")], 1.7, asked)
    late = []
    for n, e in enumerate(order):
        i, q = others.index(e), "ys"
        late.append(dma(q[n % 2], "dgt", lambda e=e: T.gt[32 * e:32 * e + 1, 128:512], lambda: T.dg[:, :], [_part(o("gt", 128, 512), 32 * e)], [o("dg")]))
        late.append(dma(q[1 - n % 2], "dgt", lambda e=e: T.qo[32 * e:32 * e + 1, :], lambda i=i: T.dg[128 * i:128 * i + 128, :],
                        [_part(o("qo"), 32 * e)], [o("dg")]))
    for k in range(8):
        dma("ys"[k % 2], "dgo", lambda k=k: T.gtt[16 * k:16 * k + 1, 128:512], lambda: T.dg[:, :],
            [o("gtt", 128 + 48 * k, 176 + 48 * k)], [o("dg")], fills)
    v("tt", o("a1", 0, 128), _ind(o("gt"), o("offl", 0, 8)), o("qo"), A.is_le)
    v("tt", o("a1", 128, 256), _ind(o("gt"), o("offl", 8, 16)), o("qo"), A.is_lt)
    counted = v("scan", o("a2", 0, 128), o("a1", 0, 128), o("a1", 128, 256), 0.0, A.add, A.add)
    told = []
    v("tt", o("vp"), o("a2", 0, 128, 2), o("a2", 1, 128, 2), A.add)
    for n, e in enumerate(order):
        s, t = (64 * n, 64 * n + 64), 196 * n
        do("p", "pb", (o("cb", *s), _part(o("vp"), 32 * e, 1), 128))
        for k in range(3):
            v("ts", o("bt", t + 65 * k + 1, t + 65 * k + 65), o("cb", *s), f(25 + k), f(28 + k), A.max, A.min)
        v("scan", o("sc", t, t + 195), o("rsl", 0, 195), o("bt", t, t + 195), 0.0, A.mult, A.subtract)
        v("ts", o("ls", 4 * e, 4 * e + 3), o("sc", t + 64, t + 195, 65), 127.0, None, A.min)
        i = place(me, e)
        told.append(send(e, o("la", 4 * i, 4 * i + 3), o("ls", 4 * e, 4 * e + 3), "ar%d" % i))

    act(o("gab", 0, 128), _ind(o("gtt"), o("off3", 16, 24)), F.Copy)
    v("copy", o("gab", 128, 240), _ind(o("gtt"), o("off3", 24, 31)), extra=(counted,))
    v("tt", o("wa", 0, 128), _ind(o("gtt"), o("off3", 0, 8)), o("gab", 0, 128), A.is_ge, extra=(counted,))
    v("tt", o("wa", 128, 240), _ind(o("gtt"), o("off3", 8, 15)), o("gab", 128, 240), A.is_ge)
    quarter = lambda t, h: o(t, 3 + 128 * h, 128 + 128 * h, 4)
    for s in H:
        v("tr", o("wat", *s), o("wa", *s))
    for e in range(4):
        v("tt", o("x4", e, 64, 4), o("wat", 0, 256, 16), o("de", e, 64, 4), A.mult)
    for h, s in enumerate(H):
        v("tt", quarter("m2", h), o("x4", 32 * h, 32 * h + 32), o("be", 32 * h, 32 * h + 32), A.add)
        v("tr", o("n2", *s), o("m2", *s))
        v("scan", o("rc", *s), ones(*s), o("n2", *s), o("rc", 127, 128) if h else 0.0, A.mult, A.add)
        v("tr", o("rtr", *s), o("rc", *s))

    for e in range(4):
        act(o("kz", e, 64, 4), o("zero"), F.Identity, float(-1 - 128 if e == me else 144 + 48 * others.index(e) - 1 - 128))
    v("q", o("vq"), o("vqs"), o("vt"))
    v("ts", o("h1"), role("rtr"), 48.5, None, A.is_lt)
    v("copy", o("xz"), role("rtr"))
    v("copy", o("xz", me, 64, 4), o("tp", 4 * me + 3, 256, 16))
    v("tt", o("hm"), role("m2"), o("h1"), A.mult)
    v("tt", o("z1"), o("xz"), o("kz"), A.add)
    v("tt", o("z2"), o("z1"), o("hm"), A.mult)
    v("scan", o("z3"), o("rst", 0, 64), o("z2"), 0.0, A.mult, A.add)
    v("ts", o("zn"), o("z3", 3, 64, 4), f(13), None, A.mult)
    v("ts", o("zp"), o("z3", 3, 64, 4), f(3), None, A.mult)
    v("tt", o("zl"), o("zn", 1, 15), o("zp", 0, 14), A.add)
    v("ts", o("off5"), o("zl"), 128.0, None, A.add)
    v("tt", o("w1"), role("m2"), o("ka"), A.mult)
    v("tt", o("w2"), o("hm"), o("kb"), A.mult)
    v("tt", o("w3"), o("w2"), o("w1"), A.add)
    v("scan", o("w4"), o("rst", 0, 64), o("w3"), 0.0, A.mult, A.add)
    v("ts", o("wnw", 0, 256, 16), o("w4", 3, 64, 4), -100.0, None, A.add)
    v("tr", o("wnf"), o("wnw"))
    dma("y", "out", lambda: T.wn[:, :], lambda: T.wnf[16:17, 0:224], [], [o("wnf")])

    came = []
    for n, s in enumerate(order):
        i = others.index(s)
        arrive("ar%d" % i, [s], 1, [o("la", 4 * i, 4 * i + 3)], 1.7, told[n:n + 1])
        pick("hs", 48 * i, 48 * i + 48, "hq", 128 * i, 128 * i + 128, o("la", 4 * i, 4 * i + 3))
        k = 144 + 48 * place(me, s)
        came.append(send(s, _cast(o("zq", k, k + 48), "u8"), _cast(o("hs", 48 * i, 48 * i + 48), "u8"), "ha"))
        came.append(send(s, o("zqs", k, k + 48), o("hss", 48 * i, 48 * i + 48), "ha", o("hs", 48 * i, 48 * i + 48)))

    arrive("ha", others, 2, [o("zq", 144, 288), o("zqs", 144, 288)], 2.0, came)
    pick("z", 0, 128, "zq", 0, 288, o("off5", 0, 8))
    pick("z", 128, 224, "zq", 0, 288, o("off5", 8, 14))
    mx(ps(0, 128), o("vq"), o("vqs"), o("z", 0, 128), o("zs", 0, 128), True, True)
    mx(ps(1, 128), o("vq"), o("vqs"), o("z", 96, 224), o("zs", 96, 224), True, True)
    v("copy", o("ysb", 0, 128), ps(0, 128))
    v("copy", o("ysb", 128, 224), o("ps", 544, 640))
    dma("y", "out", lambda: T.oc[:, :], lambda: T.z[:, 0:224].bitcast(dt.uint8), [], [o("z")])
    for k in range(4):
        dma("s" if k % 2 == 0 else "y", "out", lambda k=k: T.osc[4 * k:4 * k + 4, :], lambda k=k: T.zs[32 * k:32 * k + 4, :], [], [o("zs")])
    for a, z in ((0, 128), (128, 224)):
        dma("y", "out", lambda a=a, z=z: T.y[:, a:z], lambda a=a, z=z: T.ysb[:, a:z], [], [o("ysb", a, z)])

    queue = {"v": V, "s": g.scalar, "t": g.tensor, "p": g, "y": g.sync}
    lists = _order(ops)
    mark = {}
    for q, items in lists.items():
        n = 0
        for i in items:
            if ops[i]["sem"] == "own":
                n += 1
                mark[i] = (q, n)
        total[q] = n
    for i, x in enumerate(ops):
        if x["sem"] and x["sem"] != "own":
            mark[i] = (x["sem"], total[x["sem"]])
    seen = {}
    for q, items in lists.items():
        for i in items:
            best = {}
            for d in ops[i]["deps"]:
                if d in mark and not (q == "t" and ops[d]["q"] == "t"):
                    s, n = mark[d]
                    best[s] = max(n, best.get(s, 0))
            for s, n in sorted(best.items()):
                if seen.get((q, s), 0) < n:
                    queue[q].wait_ge(T.sem[s], n)
                    seen[(q, s)] = n
            call = ops[i]["fn"]()
            if ops[i]["sem"]:
                call.then_inc(T.sem[mark[i][0]], 1 if ops[i]["sem"] == "own" else 16)
    for s, n in sorted(total.items()):
        if n and seen.get(("p", s), 0) < n:
            g.wait_ge(T.sem[s], n)
